import numpy as np
import ml_dtypes


def mxq(x, axis, fmt="e4m3"):
    dtype, down = {"e4m3": (ml_dtypes.float8_e4m3fn, 7), "e5m2": (ml_dtypes.float8_e5m2, 14)}[fmt]
    v = np.moveaxis(np.asarray(x, np.float32).astype(ml_dtypes.bfloat16).astype(np.float64), axis, -1)
    blocks = v.reshape(v.shape[:-1] + (-1, 32))
    amax = np.abs(blocks).max(-1, keepdims=True)
    byte = np.maximum(np.where(amax > 0, np.frexp(amax)[1] - 1 + 127, 0) - down, 1)
    scale = np.exp2(byte - 127.0)
    codes = (blocks / scale).astype(np.float32).astype(dtype).astype(np.float64)
    return np.moveaxis((codes * scale).reshape(v.shape), -1, axis)


WIDE = False


def mx_kscale(k):
    if not WIDE:
        return np.ones(k)
    levels = np.array([10, -10, 5, -5, 0])
    if k % 512:
        return np.exp2(np.random.permutation(np.resize(levels, k // 32))).repeat(32)
    a = np.empty((k // 512, 16))
    for p in range(k // 512):
        a[p, :8] = np.random.permutation(np.resize(levels, 8))
        for g in range(8):
            far = levels[np.abs(levels - a[p, g]) >= 10]
            a[p, g + 8] = far[np.random.randint(len(far))]
    return np.exp2(a.ravel()).repeat(32)


def f64(x):
    return np.asarray(x).astype(np.float64)


def striped(idx):
    return np.tile(idx.reshape(-1, 16).T, (8, 1)).astype(np.uint16)


def unstriped(offs):
    return offs[:16].T.reshape(-1).astype(np.int64)


E2M1 = np.array([0.0, 0.5, 1.0, 1.5, 2.0, 3.0, 4.0, 6.0, -0.0, -0.5, -1.0, -1.5, -2.0, -3.0, -4.0, -6.0])


def pack_weight(w, fmt):
    k, n = w.shape
    w = f64(np.asarray(w, np.float32).astype(ml_dtypes.bfloat16)).reshape(k // 32, 32, n)
    amax = np.abs(w).max(1)
    if fmt == "e4m3":
        byte = np.frexp(amax)[1] - 1 + 127 - 7
    else:
        mant, ex = np.frexp(amax / 6.0)
        byte = np.where(mant > 0.5, ex, ex - 1) + 127
    byte = np.clip(np.where(amax > 0, byte, 1), 1, 254)
    scaled = (w * np.exp2(127.0 - byte)[:, None, :]).reshape(k, n).astype(np.float32)
    by_word = np.ascontiguousarray(scaled.reshape(k // 512, 128, 4, n).transpose(0, 1, 3, 2))
    if fmt == "e4m3":
        words = by_word.astype(ml_dtypes.float8_e4m3fn).view(np.uint8)
    else:
        c = by_word.astype(ml_dtypes.float4_e2m1fn).view(np.uint8) & 0xF
        words = (c[..., 0::2] | (c[..., 1::2] << 4)).reshape(k // 512, 128, 2 * n)
    return np.ascontiguousarray(words), np.ascontiguousarray(byte.astype(np.uint8).reshape(k // 512, 16, n))


def unpack_weight(words, scales, fmt):
    g, _, n = scales.shape
    words = np.ascontiguousarray(words).reshape(g, 128, n, -1)
    if fmt == "e4m3":
        vals = words.view(ml_dtypes.float8_e4m3fn).astype(np.float64)
    else:
        nib = np.empty((g, 128, n, 4), np.uint8)
        nib[..., 0::2] = words & 0xF
        nib[..., 1::2] = words >> 4
        vals = E2M1[nib]
    vals = vals * np.repeat(np.exp2(scales.astype(np.float64) - 127.0), 8, axis=1)[..., None]
    return vals.transpose(0, 1, 3, 2).reshape(g * 512, n)


def relu2(v):
    return np.maximum(v, 0.0) ** 2


K, T, E, C, N = 1536, 1024, 24, 128, 128
TOP = 3


def by_expert(wq, xq):
    return np.concatenate([wq[e].T @ xq[:, e * C:(e + 1) * C] for e in range(E)], axis=1)


def setup_inputs():
    n = np.random.standard_normal
    s = mx_kscale(K)[:, None]
    deal = np.repeat(np.arange(E), C).reshape(TOP, T)[:, np.random.permutation(T)]
    deal = np.take_along_axis(deal, np.argsort(np.random.rand(TOP, T), axis=0), axis=0)
    for _ in range(8):
        s_, t_ = np.random.permutation(T).reshape(2, -1); r = np.random.randint(TOP, size=T // 2); x, y = deal[r, s_].copy(), deal[r, t_].copy()
        ok = ~((deal[:, s_] == y).any(0) | (deal[:, t_] == x).any(0)); deal[r[ok], s_[ok]] = y[ok]; deal[r[ok], t_[ok]] = x[ok]
    order = np.lexsort((np.random.rand(TOP * T), deal.reshape(-1)))
    slot_token = order % T; pos = np.empty(TOP * T, np.int64); pos[order] = np.arange(TOP * T); pos = pos.reshape(TOP, T)
    g = np.random.uniform(0.5, 1.5, (TOP, T)); g = g / g.sum(0)
    w = [pack_weight(m, "e2m1") for m in n((E, K, N)) / np.sqrt(K) / s[None]]
    w_slot = np.empty(E * C)
    for r in range(TOP): w_slot[pos[r]] = g[r]
    return {
        "xT": (n((K, T)) * s).astype(np.float32),
        "w_words": np.stack([m[0] for m in w]),
        "w_scales": np.stack([m[1] for m in w]),
        "b": (0.3 * n((N, E))).astype(np.float32),
        "gate": np.tile(w_slot, (K, 1)).astype(np.float32),
        "offs": striped(slot_token),
        "pos1": striped(pos[0]),
        "pos2": striped(pos[1]),
        "pos3": striped(pos[2]),
    }


def reference(xT, w_words, w_scales, b, gate, offs, pos1, pos2, pos3):
    idx = unstriped(offs)
    w = np.stack([unpack_weight(w_words[e], w_scales[e], "e2m1") for e in range(E)])
    xq = mxq(f64(gate) * f64(xT)[:, idx], 0, "e4m3")
    y = by_expert(w, xq)
    y = relu2(y + np.repeat(f64(b), C, axis=1))
    return y[:, unstriped(pos1)] + y[:, unstriped(pos2)] + y[:, unstriped(pos3)]

@@ -1,0 +1,182 @@
+from contextlib import ExitStack
+
+import concourse.mybir as mybir
+
+K, T, E, C, N = 1536, 1024, 24, 128, 128
+S = E * C
+P = 128
+PACK = 4
+PASSES = K // (P * PACK)
+LANE = 16
+PAD = 16
+BANKS = 8
+
+FLOPS = 2 * K * N * S
+BYTES = 4 * K * T + E * K * N // 2 + E * K * N // 32 + 4 * N * E + 4 * S + 2 * P * (S + 3 * T) // LANE + 4 * N * T
+
+F32 = mybir.dt.float32
+BF16 = mybir.dt.bfloat16
+I32 = mybir.dt.int32
+U32 = mybir.dt.uint32
+U16 = mybir.dt.uint16
+U8 = mybir.dt.uint8
+FP8X4 = mybir.dt.float8_e4m3fn_x4
+FP4X4 = mybir.dt.float4_e2m1fn_x4
+MULT = mybir.AluOpType.mult
+ADD = mybir.AluOpType.add
+ACT = mybir.ActivationFunctionType
+
+CHUNK = 1024
+FIRST = 256
+LAST_WIDTHS = (512, 256, 128, 128)
+OUT_SPLIT = 640
+
+
+def steps():
+    out = []
+    for s0 in range(0, S, CHUNK):
+        for a in range(PASSES):
+            if s0 + CHUNK == S and a == PASSES - 1:
+                s = s0
+                for w in LAST_WIDTHS:
+                    out.append((a, s, w))
+                    s += w
+            else:
+                out.append((a, s0, CHUNK))
+    return out
+
+
+def tile_moe_pre_lin_relu2_kernel(
+    tc, xT, w_words, w_scales, b, gate, offs, pos1, pos2, pos3, out
+):
+    nc = tc.nc
+    with ExitStack() as ctx:
+        keep = ctx.enter_context(tc.tile_pool(name="keep", bufs=1))
+        stage = ctx.enter_context(tc.tile_pool(name="stage", bufs=2))
+        quant = ctx.enter_context(tc.tile_pool(name="quant", bufs=5))
+        psum = ctx.enter_context(tc.psum_pool(name="psum", bufs=1))
+
+        offs_sb = keep.tile([P, S // LANE], U16, name="offs_sb")
+        pos_sb = [keep.tile([P, T // LANE], U16, name=f"pos_sb{r}") for r in range(3)]
+        gate_sb = keep.tile([P, S], F32, name="gate_sb")
+        bias_sb = keep.tile([P, E], F32, name="bias_sb")
+        x_sb = [[keep.tile([P, T + PAD], F32, name=f"x_sb{a}_{t}") for t in range(PACK)] for a in range(PASSES)]
+        w_sb = keep.tile([P, E * PASSES, 2 * N], U8, name="w_sb", align_bytes=64)
+        ws_sb = keep.tile([P, E * PASSES, N], U8, name="ws_sb", align_bytes=64)
+        y_sb = keep.tile([P, S], F32, name="y_sb")
+
+        x_rows = xT.rearrange("(a p t) c -> a t p c", p=P, t=PACK)
+
+        def load_x(a, t):
+            nc.sync.dma_start(out=x_sb[a][t][:, 0:T], in_=x_rows[a, t])
+
+        def load_gate(c0, c1):
+            nc.sync.dma_start(out=gate_sb[:, c0:c1], in_=gate[0:P, c0:c1])
+
+        def load_w(e0, e1):
+            nc.sync.dma_start(
+                out=w_sb[:, e0 * PASSES : e1 * PASSES, :].bitcast(I32),
+                in_=w_words[e0:e1].rearrange("e a p m -> p (e a) m").bitcast(I32),
+            )
+
+        for a in range(PASSES):
+            for t in range(PACK):
+                nc.vector.memset(x_sb[a][t][:, T : T + PAD], 0.0)
+        nc.vector.memset(ws_sb[:].rearrange("p g n -> p (g n)").bitcast(I32), 0)
+
+        load_x(0, 0)
+        nc.sync.dma_start(offs_sb[:], offs)
+        load_gate(0, FIRST)
+        load_gate(FIRST, CHUNK)
+        for i in range(1, PASSES * PACK):
+            load_x(i // PACK, i % PACK)
+        load_gate(CHUNK, 2 * CHUNK)
+        load_w(0, BANKS)
+        ws_rows = w_scales.rearrange("e a (g r) n -> r g (e a) n", r=4)
+        for r in range(4):
+            nc.sync.dma_start(out=ws_sb[r:P:32, :, :].bitcast(I32), in_=ws_rows[r].bitcast(I32))
+        nc.sync.dma_start(out=bias_sb[:], in_=b)
+        load_gate(2 * CHUNK, S)
+        load_w(BANKS, 2 * BANKS)
+        load_w(2 * BANKS, E)
+        for r, pos in enumerate((pos1, pos2, pos3)):
+            nc.sync.dma_start(pos_sb[r][:], pos)
+
+        acc = {}
+
+        def gather(a, s0, w, first):
+            gated = stage.tile([P, PACK, w], F32, name="gated")
+            for t in range(PACK):
+                cuts = (0, FIRST, w) if first and t == 0 else (0, w)
+                for c0, c1 in zip(cuts, cuts[1:]):
+                    nc.vector.tensor_tensor(
+                        gated[:, t, c0:c1],
+                        x_sb[a][t][:].indirect(offs_sb[:, (s0 + c0) // LANE : (s0 + c1) // LANE]),
+                        gate_sb[:, s0 + c0 : s0 + c1],
+                        MULT,
+                    )
+            grouped = stage.tile([P, w, PACK], BF16, name="grouped", align_bytes=64)
+            nc.scalar.copy(out=grouped[:], in_=gated[:].rearrange("p t c -> p c t"))
+            return grouped
+
+        def multiply(a, s0, w, grouped):
+            codes = quant.tile([P, w], U32, name="codes", align_bytes=64)
+            scales = quant.tile([P, w], U8, name="scales", align_bytes=64)
+            nc.vector.quantize_mx(
+                out=codes[:].bitcast(FP8X4), scales=scales[:], in_=grouped[:].rearrange("p c t -> p (c t)")
+            )
+            for c0 in range(0, w, C):
+                e = (s0 + c0) // C
+                if a == 0:
+                    acc[e] = psum.tile([N, C], F32, name=f"acc{e % BANKS}")
+                g = e * PASSES + a
+                nc.tensor.matmul_mx(
+                    out=acc[e][:],
+                    lhsT=w_sb[:, g, :].bitcast(FP4X4),
+                    lhsT_scale=ws_sb[:, g, :],
+                    rhs=codes[:, c0 : c0 + C].bitcast(FP8X4),
+                    rhs_scale=scales[:, c0 : c0 + C],
+                    start=(a == 0),
+                    stop=(a == PASSES - 1),
+                )
+            if a == PASSES - 1:
+                relu = stage.tile([P, w], F32, name="relu")
+                for c0 in range(0, w, C):
+                    e = (s0 + c0) // C
+                    nc.scalar.activation(relu[:, c0 : c0 + C], acc[e][:], ACT.Relu, bias=bias_sb[:, e : e + 1])
+                nc.scalar.activation(y_sb[:, s0 : s0 + w], relu[:], ACT.Square)
+
+        pending = None
+        for i, step in enumerate(steps()):
+            grouped = gather(*step, i == 0)
+            if pending is not None:
+                multiply(*pending)
+            pending = (*step, grouped)
+        multiply(*pending)
+
+        picked = [keep.tile([P, T], F32, name=f"picked{r}") for r in range(3)]
+        pair = keep.tile([P, T], F32, name="pair")
+        total = keep.tile([P, T], F32, name="total")
+        lo, hi = slice(0, OUT_SPLIT), slice(OUT_SPLIT, T)
+
+        def fetch(r, cols):
+            nc.vector.tensor_copy(
+                picked[r][:, cols], y_sb[:].indirect(pos_sb[r][:, cols.start // LANE : cols.stop // LANE])
+            )
+
+        def add_pair(cols):
+            nc.vector.tensor_tensor(pair[:, cols], picked[0][:, cols], picked[1][:, cols], ADD)
+
+        def finish(cols):
+            nc.vector.tensor_tensor(total[:, cols], pair[:, cols], picked[2][:, cols], ADD)
+            nc.sync.dma_start(out=out[:, cols], in_=total[:, cols])
+
+        for r in range(3):
+            fetch(r, lo)
+        add_pair(lo)
+        fetch(0, hi)
+        fetch(1, hi)
+        finish(lo)
+        add_pair(hi)
+        fetch(2, hi)
+        finish(hi)

@@ -27,7 +27,7 @@ ADD = mybir.AluOpType.add
 ACT = mybir.ActivationFunctionType
 
 CHUNK = 1024
-FIRST = 256
+FIRST = 352
 LAST_WIDTHS = (512, 256, 128, 128)
 OUT_SPLIT = 640
 
@@ -90,13 +90,12 @@ def tile_moe_pre_lin_relu2_kernel(
         load_gate(FIRST, CHUNK)
         for i in range(1, PASSES * PACK):
             load_x(i // PACK, i % PACK)
-        load_gate(CHUNK, 2 * CHUNK)
+        load_gate(CHUNK, S)
+        nc.sync.dma_start(out=bias_sb[:], in_=b)
         load_w(0, BANKS)
         ws_rows = w_scales.rearrange("e a (g r) n -> r g (e a) n", r=4)
         for r in range(4):
             nc.sync.dma_start(out=ws_sb[r:P:32, :, :].bitcast(I32), in_=ws_rows[r].bitcast(I32))
-        nc.sync.dma_start(out=bias_sb[:], in_=b)
-        load_gate(2 * CHUNK, S)
         load_w(BANKS, 2 * BANKS)
         load_w(2 * BANKS, E)
         for r, pos in enumerate((pos1, pos2, pos3)):
@@ -115,8 +114,14 @@ def tile_moe_pre_lin_relu2_kernel(
                         gate_sb[:, s0 + c0 : s0 + c1],
                         MULT,
                     )
+            return gated
+
+        def interleave(copy, w, gated):
             grouped = stage.tile([P, w, PACK], BF16, name="grouped", align_bytes=64)
-            nc.scalar.copy(out=grouped[:], in_=gated[:].rearrange("p t c -> p c t"))
+            copy(
+                out=grouped[:].rearrange("p (c i) t -> p c t i", i=4),
+                in_=gated[:].rearrange("p t (c i) -> p c t i", i=4),
+            )
             return grouped
 
         def multiply(a, s0, w, grouped):
@@ -147,12 +152,15 @@ def tile_moe_pre_lin_relu2_kernel(
                 nc.scalar.activation(y_sb[:, s0 : s0 + w], relu[:], ACT.Square)
 
         pending = None
-        for i, step in enumerate(steps()):
-            grouped = gather(*step, i == 0)
+        plan = steps()
+        for i, step in enumerate(plan[:-1]):
+            grouped = interleave(nc.scalar.copy, step[2], gather(*step, i == 0))
             if pending is not None:
                 multiply(*pending)
             pending = (*step, grouped)
+        gated = gather(*plan[-1], False)
         multiply(*pending)
+        multiply(*plan[-1], interleave(nc.vector.tensor_copy, plan[-1][2], gated))
 
         picked = [keep.tile([P, T], F32, name=f"picked{r}") for r in range(3)]
         pair = keep.tile([P, T], F32, name="pair")

@@ -30,6 +30,7 @@ CHUNK = 1024
 FIRST = 352
 LAST_WIDTHS = (512, 256, 128, 128)
 OUT_SPLIT = 640
+EARLY = 2
 
 
 def steps():
@@ -73,7 +74,12 @@ def tile_moe_pre_lin_relu2_kernel(
         def load_gate(c0, c1):
             nc.sync.dma_start(out=gate_sb[:, c0:c1], in_=gate[0:P, c0:c1])
 
+        ws_rows = w_scales.rearrange("e a (g r) n -> r g (e a) n", r=4)
+
         def load_w(e0, e1):
+            groups = slice(e0 * PASSES, e1 * PASSES)
+            for r in range(4):
+                nc.sync.dma_start(out=ws_sb[r:P:32, groups, :].bitcast(I32), in_=ws_rows[r, :, groups].bitcast(I32))
             nc.sync.dma_start(
                 out=w_sb[:, e0 * PASSES : e1 * PASSES, :].bitcast(I32),
                 in_=w_words[e0:e1].rearrange("e a p m -> p (e a) m").bitcast(I32),
@@ -89,15 +95,13 @@ def tile_moe_pre_lin_relu2_kernel(
         load_gate(0, FIRST)
         load_gate(FIRST, CHUNK)
         for i in range(1, PASSES * PACK):
+            if i == (PASSES - 1) * PACK:
+                load_gate(CHUNK, 2 * CHUNK)
             load_x(i // PACK, i % PACK)
-        load_gate(CHUNK, S)
+        load_gate(2 * CHUNK, S)
         nc.sync.dma_start(out=bias_sb[:], in_=b)
-        load_w(0, BANKS)
-        ws_rows = w_scales.rearrange("e a (g r) n -> r g (e a) n", r=4)
-        for r in range(4):
-            nc.sync.dma_start(out=ws_sb[r:P:32, :, :].bitcast(I32), in_=ws_rows[r].bitcast(I32))
-        load_w(BANKS, 2 * BANKS)
-        load_w(2 * BANKS, E)
+        for e0 in range(0, E, BANKS):
+            load_w(e0, e0 + BANKS)
         for r, pos in enumerate((pos1, pos2, pos3)):
             nc.sync.dma_start(pos_sb[r][:], pos)
 
@@ -124,32 +128,49 @@ def tile_moe_pre_lin_relu2_kernel(
             )
             return grouped
 
+        held = {}
+        early = {e: psum.tile([N, C], F32, name=f"early{e}") for e in range(E - EARLY, E)}
+
+        def matmul(acc, e, a):
+            codes, scales, s0 = held[a]
+            cols = slice(e * C - s0, (e + 1) * C - s0)
+            g = e * PASSES + a
+            nc.tensor.matmul_mx(
+                out=acc,
+                lhsT=w_sb[:, g, :].bitcast(FP4X4),
+                lhsT_scale=ws_sb[:, g, :],
+                rhs=codes[:, cols].bitcast(FP8X4),
+                rhs_scale=scales[:, cols],
+                start=(a == 0),
+                stop=(a == PASSES - 1),
+            )
+
         def multiply(a, s0, w, grouped):
             codes = quant.tile([P, w], U32, name="codes", align_bytes=64)
             scales = quant.tile([P, w], U8, name="scales", align_bytes=64)
             nc.vector.quantize_mx(
                 out=codes[:].bitcast(FP8X4), scales=scales[:], in_=grouped[:].rearrange("p c t -> p (c t)")
             )
-            for c0 in range(0, w, C):
-                e = (s0 + c0) // C
-                if a == 0:
-                    acc[e] = psum.tile([N, C], F32, name=f"acc{e % BANKS}")
-                g = e * PASSES + a
-                nc.tensor.matmul_mx(
-                    out=acc[e][:],
-                    lhsT=w_sb[:, g, :].bitcast(FP4X4),
-                    lhsT_scale=ws_sb[:, g, :],
-                    rhs=codes[:, c0 : c0 + C].bitcast(FP8X4),
-                    rhs_scale=scales[:, c0 : c0 + C],
-                    start=(a == 0),
-                    stop=(a == PASSES - 1),
-                )
-            if a == PASSES - 1:
-                relu = stage.tile([P, w], F32, name="relu")
-                for c0 in range(0, w, C):
-                    e = (s0 + c0) // C
-                    nc.scalar.activation(relu[:, c0 : c0 + C], acc[e][:], ACT.Relu, bias=bias_sb[:, e : e + 1])
-                nc.scalar.activation(y_sb[:, s0 : s0 + w], relu[:], ACT.Square)
+            held[a] = (codes, scales, s0)
+            experts = range(s0 // C, (s0 + w) // C)
+            if a < PASSES - 1:
+                for e in experts:
+                    if e in early:
+                        matmul(early[e][:], e, a)
+                return
+            relu = stage.tile([P, w], F32, name="relu")
+            for e in experts:
+                if e in early:
+                    acc = early[e][:]
+                    matmul(acc, e, a)
+                else:
+                    bank = psum.tile([N, C], F32, name="bank", bufs=BANKS - EARLY)
+                    acc = bank[:]
+                    for g in range(PASSES):
+                        matmul(acc, e, g)
+                c0 = e * C - s0
+                nc.scalar.activation(relu[:, c0 : c0 + C], acc, ACT.Relu, bias=bias_sb[:, e : e + 1])
+            nc.scalar.activation(y_sb[:, s0 : s0 + w], relu[:], ACT.Square)
 
         pending = None
         plan = steps()

@@ -108,7 +108,7 @@ def tile_moe_pre_lin_relu2_kernel(
         acc = {}
 
         def gather(a, s0, w, first):
-            gated = stage.tile([P, PACK, w], F32, name="gated")
+            gated = stage.tile([P, PACK, w], F32, name="gated", bufs=3)
             for t in range(PACK):
                 cuts = (0, FIRST, w) if first and t == 0 else (0, w)
                 for c0, c1 in zip(cuts, cuts[1:]):
@@ -194,18 +194,16 @@ def tile_moe_pre_lin_relu2_kernel(
             )
 
         def add_pair(cols):
-            nc.vector.tensor_tensor(pair[:, cols], picked[0][:, cols], picked[1][:, cols], ADD)
+            nc.gpsimd.tensor_tensor(pair[:, cols], picked[0][:, cols], picked[1][:, cols], ADD)
 
-        def finish(cols):
-            nc.vector.tensor_tensor(total[:, cols], pair[:, cols], picked[2][:, cols], ADD)
+        def finish(engine, cols):
+            engine.tensor_tensor(total[:, cols], pair[:, cols], picked[2][:, cols], ADD)
             nc.sync.dma_start(out=out[:, cols], in_=total[:, cols])
 
-        for r in range(3):
-            fetch(r, lo)
-        add_pair(lo)
-        fetch(0, hi)
-        fetch(1, hi)
-        finish(lo)
-        add_pair(hi)
-        fetch(2, hi)
-        finish(hi)
+        for cols in (lo, hi):
+            fetch(0, cols)
+            fetch(1, cols)
+            add_pair(cols)
+        for cols in (lo, hi):
+            fetch(2, cols)
+            finish(nc.vector, cols)

@@ -29,7 +29,7 @@ ACT = mybir.ActivationFunctionType
 CHUNK = 1024
 FIRST = 352
 LAST_WIDTHS = (512, 256, 128, 128)
-OUT_SPLIT = 640
+OUT_SPLIT = 512
 EARLY = 2
 
 
@@ -204,6 +204,6 @@ def tile_moe_pre_lin_relu2_kernel(
             fetch(0, cols)
             fetch(1, cols)
             add_pair(cols)
-        for cols in (lo, hi):
+        for engine, cols in ((nc.gpsimd, lo), (nc.vector, hi)):
             fetch(2, cols)
-            finish(nc.vector, cols)
+            finish(engine, cols)

@@ -27,9 +27,9 @@ ADD = mybir.AluOpType.add
 ACT = mybir.ActivationFunctionType
 
 CHUNK = 1024
-FIRST = 352
+FIRST_CUTS = (0, 128, 384, CHUNK)
 LAST_WIDTHS = (512, 256, 128, 128)
-OUT_SPLIT = 512
+OUT_CUTS = (0, 512, 896, T)
 EARLY = 2
 
 
@@ -88,12 +88,12 @@ def tile_moe_pre_lin_relu2_kernel(
         for a in range(PASSES):
             for t in range(PACK):
                 nc.vector.memset(x_sb[a][t][:, T : T + PAD], 0.0)
-        nc.vector.memset(ws_sb[:].rearrange("p g n -> p (g n)").bitcast(I32), 0)
+        nc.gpsimd.memset(ws_sb[:].rearrange("p g n -> p (g n)").bitcast(I32), 0)
 
-        load_x(0, 0)
         nc.sync.dma_start(offs_sb[:], offs)
-        load_gate(0, FIRST)
-        load_gate(FIRST, CHUNK)
+        load_x(0, 0)
+        for c0, c1 in zip(FIRST_CUTS, FIRST_CUTS[1:]):
+            load_gate(c0, c1)
         for i in range(1, PASSES * PACK):
             if i == (PASSES - 1) * PACK:
                 load_gate(CHUNK, 2 * CHUNK)
@@ -110,7 +110,7 @@ def tile_moe_pre_lin_relu2_kernel(
         def gather(a, s0, w, first):
             gated = stage.tile([P, PACK, w], F32, name="gated", bufs=3)
             for t in range(PACK):
-                cuts = (0, FIRST, w) if first and t == 0 else (0, w)
+                cuts = FIRST_CUTS if first and t == 0 else (0, w)
                 for c0, c1 in zip(cuts, cuts[1:]):
                     nc.vector.tensor_tensor(
                         gated[:, t, c0:c1],
@@ -183,27 +183,19 @@ def tile_moe_pre_lin_relu2_kernel(
         multiply(*pending)
         multiply(*plan[-1], interleave(nc.vector.tensor_copy, plan[-1][2], gated))
 
-        picked = [keep.tile([P, T], F32, name=f"picked{r}") for r in range(3)]
+        picked = keep.tile([P, T], F32, name="picked")
         pair = keep.tile([P, T], F32, name="pair")
         total = keep.tile([P, T], F32, name="total")
-        lo, hi = slice(0, OUT_SPLIT), slice(OUT_SPLIT, T)
+        halves = (slice(0, T // 2), slice(T // 2, T))
 
-        def fetch(r, cols):
-            nc.vector.tensor_copy(
-                picked[r][:, cols], y_sb[:].indirect(pos_sb[r][:, cols.start // LANE : cols.stop // LANE])
-            )
+        def window(r, cols):
+            return y_sb[:].indirect(pos_sb[r][:, cols.start // LANE : cols.stop // LANE])
 
-        def add_pair(cols):
-            nc.gpsimd.tensor_tensor(pair[:, cols], picked[0][:, cols], picked[1][:, cols], ADD)
-
-        def finish(engine, cols):
-            engine.tensor_tensor(total[:, cols], pair[:, cols], picked[2][:, cols], ADD)
+        for cols in halves:
+            nc.vector.tensor_copy(picked[:, cols], window(0, cols))
+        for cols in halves:
+            nc.vector.tensor_tensor(pair[:, cols], window(1, cols), picked[:, cols], ADD)
+        for c0, c1 in zip(OUT_CUTS, OUT_CUTS[1:]):
+            cols = slice(c0, c1)
+            nc.vector.tensor_tensor(total[:, cols], window(2, cols), pair[:, cols], ADD)
             nc.sync.dma_start(out=out[:, cols], in_=total[:, cols])
-
-        for cols in (lo, hi):
-            fetch(0, cols)
-            fetch(1, cols)
-            add_pair(cols)
-        for engine, cols in ((nc.gpsimd, lo), (nc.vector, hi)):
-            fetch(2, cols)
-            finish(engine, cols)

@@ -28,22 +28,23 @@ ACT = mybir.ActivationFunctionType
 
 CHUNK = 1024
 FIRST_CUTS = (0, 128, 384, CHUNK)
-LAST_WIDTHS = (512, 256, 128, 128)
+LAST_GROUPS = (512, 256, 256)
+LAG = 2
 OUT_CUTS = (0, 512, 896, T)
 EARLY = 2
 
 
 def steps():
-    out = []
-    for s0 in range(0, S, CHUNK):
-        for a in range(PASSES):
-            if s0 + CHUNK == S and a == PASSES - 1:
-                s = s0
-                for w in LAST_WIDTHS:
-                    out.append((a, s, w))
-                    s += w
-            else:
-                out.append((a, s0, CHUNK))
+    out = [(a, s0, CHUNK) for s0 in range(0, S - CHUNK, CHUNK) for a in range(PASSES)]
+    s0 = S - CHUNK
+    out.append((0, s0, CHUNK))
+    for w in LAST_GROUPS:
+        out.append((1, s0, w))
+        if s0 + w < S:
+            out.append((2, s0, w))
+        else:
+            out.extend((2, s, C) for s in range(s0, S, C))
+        s0 += w
     return out
 
 
@@ -54,7 +55,7 @@ def tile_moe_pre_lin_relu2_kernel(
     with ExitStack() as ctx:
         keep = ctx.enter_context(tc.tile_pool(name="keep", bufs=1))
         stage = ctx.enter_context(tc.tile_pool(name="stage", bufs=2))
-        quant = ctx.enter_context(tc.tile_pool(name="quant", bufs=5))
+        quant = ctx.enter_context(tc.tile_pool(name="quant", bufs=7))
         psum = ctx.enter_context(tc.psum_pool(name="psum", bufs=1))
 
         offs_sb = keep.tile([P, S // LANE], U16, name="offs_sb")
@@ -105,8 +106,6 @@ def tile_moe_pre_lin_relu2_kernel(
         for r, pos in enumerate((pos1, pos2, pos3)):
             nc.sync.dma_start(pos_sb[r][:], pos)
 
-        acc = {}
-
         def gather(a, s0, w, first):
             gated = stage.tile([P, PACK, w], F32, name="gated", bufs=3)
             for t in range(PACK):
@@ -121,7 +120,7 @@ def tile_moe_pre_lin_relu2_kernel(
             return gated
 
         def interleave(copy, w, gated):
-            grouped = stage.tile([P, w, PACK], BF16, name="grouped", align_bytes=64)
+            grouped = stage.tile([P, w, PACK], BF16, name="grouped", align_bytes=64, bufs=LAG + 1)
             copy(
                 out=grouped[:].rearrange("p (c i) t -> p c t i", i=4),
                 in_=gated[:].rearrange("p t (c i) -> p c t i", i=4),
@@ -132,7 +131,7 @@ def tile_moe_pre_lin_relu2_kernel(
         early = {e: psum.tile([N, C], F32, name=f"early{e}") for e in range(E - EARLY, E)}
 
         def matmul(acc, e, a):
-            codes, scales, s0 = held[a]
+            codes, scales, s0 = held[e, a]
             cols = slice(e * C - s0, (e + 1) * C - s0)
             g = e * PASSES + a
             nc.tensor.matmul_mx(
@@ -151,8 +150,9 @@ def tile_moe_pre_lin_relu2_kernel(
             nc.vector.quantize_mx(
                 out=codes[:].bitcast(FP8X4), scales=scales[:], in_=grouped[:].rearrange("p c t -> p (c t)")
             )
-            held[a] = (codes, scales, s0)
             experts = range(s0 // C, (s0 + w) // C)
+            for e in experts:
+                held[e, a] = (codes, scales, s0)
             if a < PASSES - 1:
                 for e in experts:
                     if e in early:
@@ -172,16 +172,17 @@ def tile_moe_pre_lin_relu2_kernel(
                 nc.scalar.activation(relu[:, c0 : c0 + C], acc, ACT.Relu, bias=bias_sb[:, e : e + 1])
             nc.scalar.activation(y_sb[:, s0 : s0 + w], relu[:], ACT.Square)
 
-        pending = None
         plan = steps()
-        for i, step in enumerate(plan[:-1]):
-            grouped = interleave(nc.scalar.copy, step[2], gather(*step, i == 0))
-            if pending is not None:
-                multiply(*pending)
-            pending = (*step, grouped)
-        gated = gather(*plan[-1], False)
-        multiply(*pending)
-        multiply(*plan[-1], interleave(nc.vector.tensor_copy, plan[-1][2], gated))
+        last = len(plan) - 1
+        woven = []
+        for i, step in enumerate(plan[:last]):
+            woven.append(interleave(nc.scalar.copy, step[2], gather(*step, i == 0)))
+            if i >= LAG:
+                multiply(*plan[i - LAG], woven[i - LAG])
+        gated = gather(*plan[last], False)
+        for i in range(last - LAG, last):
+            multiply(*plan[i], woven[i])
+        multiply(*plan[last], interleave(nc.vector.tensor_copy, plan[last][2], gated))
 
         picked = keep.tile([P, T], F32, name="picked")
         pair = keep.tile([P, T], F32, name="pair")

@@ -27,15 +27,19 @@ ADD = mybir.AluOpType.add
 ACT = mybir.ActivationFunctionType
 
 CHUNK = 1024
-FIRST_CUTS = (0, 128, 384, CHUNK)
+WIDE = 2 * CHUNK
+FIRST_CUTS = (0, 128, 384, CHUNK, WIDE)
 LAST_GROUPS = (512, 256, 256)
 LAG = 2
-OUT_CUTS = (0, 512, 896, T)
+OUT_CUTS = (0, 640, 896, T)
 EARLY = 2
+VECTOR_PADS = 3
+HELD = WIDE // C
 
 
 def steps():
-    out = [(a, s0, CHUNK) for s0 in range(0, S - CHUNK, CHUNK) for a in range(PASSES)]
+    out = [(a, 0, WIDE) for a in range(PASSES - 1)]
+    out.extend((PASSES - 1, s0, CHUNK) for s0 in range(0, WIDE, CHUNK))
     s0 = S - CHUNK
     out.append((0, s0, CHUNK))
     for w in LAST_GROUPS:
@@ -55,16 +59,18 @@ def tile_moe_pre_lin_relu2_kernel(
     with ExitStack() as ctx:
         keep = ctx.enter_context(tc.tile_pool(name="keep", bufs=1))
         stage = ctx.enter_context(tc.tile_pool(name="stage", bufs=2))
-        quant = ctx.enter_context(tc.tile_pool(name="quant", bufs=7))
+        quant = ctx.enter_context(tc.tile_pool(name="quant", bufs=6))
         psum = ctx.enter_context(tc.psum_pool(name="psum", bufs=1))
 
         offs_sb = keep.tile([P, S // LANE], U16, name="offs_sb")
         pos_sb = [keep.tile([P, T // LANE], U16, name=f"pos_sb{r}") for r in range(3)]
         gate_sb = keep.tile([P, S], F32, name="gate_sb")
         bias_sb = keep.tile([P, E], F32, name="bias_sb")
-        x_sb = [[keep.tile([P, T + PAD], F32, name=f"x_sb{a}_{t}") for t in range(PACK)] for a in range(PASSES)]
-        w_sb = keep.tile([P, E * PASSES, 2 * N], U8, name="w_sb", align_bytes=64)
-        ws_sb = keep.tile([P, E * PASSES, N], U8, name="ws_sb", align_bytes=64)
+        columns = [WIDE + PAD] * (PASSES - 1) + [T + PAD]
+        x_sb = [[keep.tile([P, columns[a]], F32, name=f"x_sb{a}_{t}") for t in range(PACK)] for a in range(PASSES)]
+        gated_sb = keep.tile([P, 7 * WIDE], F32, name="gated_sb")
+        w_sb = keep.tile([P, HELD * PASSES, 2 * N], U8, name="w_sb", align_bytes=64)
+        ws_sb = keep.tile([P, HELD * PASSES, N], U8, name="ws_sb", align_bytes=64)
         y_sb = keep.tile([P, S], F32, name="y_sb")
 
         x_rows = xT.rearrange("(a p t) c -> a t p c", p=P, t=PACK)
@@ -79,37 +85,40 @@ def tile_moe_pre_lin_relu2_kernel(
 
         def load_w(e0, e1):
             groups = slice(e0 * PASSES, e1 * PASSES)
+            places = slice(e0 % HELD * PASSES, (e0 % HELD + e1 - e0) * PASSES)
             for r in range(4):
-                nc.sync.dma_start(out=ws_sb[r:P:32, groups, :].bitcast(I32), in_=ws_rows[r, :, groups].bitcast(I32))
+                nc.sync.dma_start(out=ws_sb[r:P:32, places, :].bitcast(I32), in_=ws_rows[r, :, groups].bitcast(I32))
             nc.sync.dma_start(
-                out=w_sb[:, e0 * PASSES : e1 * PASSES, :].bitcast(I32),
+                out=w_sb[:, places, :].bitcast(I32),
                 in_=w_words[e0:e1].rearrange("e a p m -> p (e a) m").bitcast(I32),
             )
 
-        for a in range(PASSES):
-            for t in range(PACK):
-                nc.vector.memset(x_sb[a][t][:, T : T + PAD], 0.0)
         nc.gpsimd.memset(ws_sb[:].rearrange("p g n -> p (g n)").bitcast(I32), 0)
+        for i in range(PASSES * PACK):
+            engine = nc.vector if i < VECTOR_PADS else nc.gpsimd
+            engine.memset(x_sb[i // PACK][i % PACK][:, T : columns[i // PACK]].bitcast(I32), 0)
 
         nc.sync.dma_start(offs_sb[:], offs)
         load_x(0, 0)
         for c0, c1 in zip(FIRST_CUTS, FIRST_CUTS[1:]):
             load_gate(c0, c1)
         for i in range(1, PASSES * PACK):
-            if i == (PASSES - 1) * PACK:
-                load_gate(CHUNK, 2 * CHUNK)
             load_x(i // PACK, i % PACK)
-        load_gate(2 * CHUNK, S)
+        load_gate(WIDE, S)
         nc.sync.dma_start(out=bias_sb[:], in_=b)
-        for e0 in range(0, E, BANKS):
+        for e0 in range(0, HELD, BANKS):
             load_w(e0, e0 + BANKS)
         for r, pos in enumerate((pos1, pos2, pos3)):
             nc.sync.dma_start(pos_sb[r][:], pos)
 
-        def gather(a, s0, w, first):
-            gated = stage.tile([P, PACK, w], F32, name="gated", bufs=3)
+        def gather(i, a, s0, w):
+            if w == WIDE:
+                base = (1 - i) * (PACK - 1) * WIDE
+            else:
+                base = (2 if i == 2 else 2 - (i - 4) % 3) * PACK * CHUNK
+            gated = gated_sb[:, base : base + PACK * w].rearrange("p (t c) -> p t c", t=PACK)
             for t in range(PACK):
-                cuts = FIRST_CUTS if first and t == 0 else (0, w)
+                cuts = FIRST_CUTS if i == 0 and t == 0 else (0, w)
                 for c0, c1 in zip(cuts, cuts[1:]):
                     nc.vector.tensor_tensor(
                         gated[:, t, c0:c1],
@@ -123,7 +132,7 @@ def tile_moe_pre_lin_relu2_kernel(
             grouped = stage.tile([P, w, PACK], BF16, name="grouped", align_bytes=64, bufs=LAG + 1)
             copy(
                 out=grouped[:].rearrange("p (c i) t -> p c t i", i=4),
-                in_=gated[:].rearrange("p t (c i) -> p c t i", i=4),
+                in_=gated.rearrange("p t (c i) -> p c t i", i=4),
             )
             return grouped
 
@@ -133,7 +142,7 @@ def tile_moe_pre_lin_relu2_kernel(
         def matmul(acc, e, a):
             codes, scales, s0 = held[e, a]
             cols = slice(e * C - s0, (e + 1) * C - s0)
-            g = e * PASSES + a
+            g = e % HELD * PASSES + a
             nc.tensor.matmul_mx(
                 out=acc,
                 lhsT=w_sb[:, g, :].bitcast(FP4X4),
@@ -158,7 +167,6 @@ def tile_moe_pre_lin_relu2_kernel(
                     if e in early:
                         matmul(early[e][:], e, a)
                 return
-            relu = stage.tile([P, w], F32, name="relu")
             for e in experts:
                 if e in early:
                     acc = early[e][:]
@@ -168,26 +176,36 @@ def tile_moe_pre_lin_relu2_kernel(
                     acc = bank[:]
                     for g in range(PASSES):
                         matmul(acc, e, g)
-                c0 = e * C - s0
-                nc.scalar.activation(relu[:, c0 : c0 + C], acc, ACT.Relu, bias=bias_sb[:, e : e + 1])
-            nc.scalar.activation(y_sb[:, s0 : s0 + w], relu[:], ACT.Square)
+                nc.scalar.activation(y_sb[:, e * C : (e + 1) * C], acc, ACT.Relu, bias=bias_sb[:, e : e + 1])
+            nc.scalar.activation(y_sb[:, s0 : s0 + w], y_sb[:, s0 : s0 + w], ACT.Square)
 
         plan = steps()
         last = len(plan) - 1
-        woven = []
-        for i, step in enumerate(plan[:last]):
-            woven.append(interleave(nc.scalar.copy, step[2], gather(*step, i == 0)))
-            if i >= LAG:
+        halves = {}
+        for i in range(PASSES - 1):
+            gated = gather(i, *plan[i])
+            for s0 in range(0, WIDE, CHUNK):
+                halves[i, s0] = interleave(nc.scalar.copy, CHUNK, gated[:, :, s0 : s0 + CHUNK])
+                if i > 0:
+                    multiply(i - 1, s0, CHUNK, halves[i - 1, s0])
+        woven = {}
+        for i in range(PASSES - 1, last):
+            woven[i] = interleave(nc.scalar.copy, plan[i][2], gather(i, *plan[i]))
+            if i == 2:
+                for s0 in range(0, WIDE, CHUNK):
+                    multiply(1, s0, CHUNK, halves[1, s0])
+            elif i == 3:
+                multiply(*plan[2], woven[2])
+                load_w(HELD, E)
+            elif i > 4:
                 multiply(*plan[i - LAG], woven[i - LAG])
-        gated = gather(*plan[last], False)
+        gated = gather(last, *plan[last])
         for i in range(last - LAG, last):
             multiply(*plan[i], woven[i])
         multiply(*plan[last], interleave(nc.vector.tensor_copy, plan[last][2], gated))
 
-        picked = keep.tile([P, T], F32, name="picked")
-        pair = keep.tile([P, T], F32, name="pair")
-        total = keep.tile([P, T], F32, name="total")
-        halves = (slice(0, T // 2), slice(T // 2, T))
+        picked, pair, total = (gated_sb[:, r * T : (r + 1) * T] for r in range(3))
+        halves = (slice(0, OUT_CUTS[1]), slice(OUT_CUTS[1], T))
 
         def window(r, cols):
             return y_sb[:].indirect(pos_sb[r][:, cols.start // LANE : cols.stop // LANE])

@@ -29,27 +29,36 @@ ACT = mybir.ActivationFunctionType
 CHUNK = 1024
 WIDE = 2 * CHUNK
 FIRST_CUTS = (0, 128, 384, CHUNK, WIDE)
-LAST_GROUPS = (512, 256, 256)
+LAST_GROUPS = (CHUNK // 2, CHUNK // 4, CHUNK // 4)
 LAG = 2
 OUT_CUTS = (0, 640, 896, T)
 EARLY = 2
-VECTOR_PADS = 3
 HELD = WIDE // C
+STAGED_PLANES = 2 * PACK - 1
+RING = 3
+CODE_BUFS = 6
 
 
 def steps():
-    out = [(a, 0, WIDE) for a in range(PASSES - 1)]
-    out.extend((PASSES - 1, s0, CHUNK) for s0 in range(0, WIDE, CHUNK))
+    plan = [(a, 0, WIDE) for a in range(PASSES - 1)]
+    plan.extend((PASSES - 1, s0, CHUNK) for s0 in range(0, WIDE, CHUNK))
     s0 = S - CHUNK
-    out.append((0, s0, CHUNK))
+    plan.append((0, s0, CHUNK))
     for w in LAST_GROUPS:
-        out.append((1, s0, w))
+        plan.append((1, s0, w))
         if s0 + w < S:
-            out.append((2, s0, w))
+            plan.append((2, s0, w))
         else:
-            out.extend((2, s, C) for s in range(s0, S, C))
+            plan.extend((2, s, C) for s in range(s0, S, C))
         s0 += w
-    return out
+    return plan
+
+
+def staging_start(i):
+    if i < 2:
+        return (1 - i) * (PACK - 1) * WIDE
+    place = RING - 1 if i == 2 else RING - 1 - (i - 4) % RING
+    return place * PACK * CHUNK
 
 
 def tile_moe_pre_lin_relu2_kernel(
@@ -58,8 +67,8 @@ def tile_moe_pre_lin_relu2_kernel(
     nc = tc.nc
     with ExitStack() as ctx:
         keep = ctx.enter_context(tc.tile_pool(name="keep", bufs=1))
-        stage = ctx.enter_context(tc.tile_pool(name="stage", bufs=2))
-        quant = ctx.enter_context(tc.tile_pool(name="quant", bufs=6))
+        stage = ctx.enter_context(tc.tile_pool(name="stage", bufs=LAG + 1))
+        quant = ctx.enter_context(tc.tile_pool(name="quant", bufs=CODE_BUFS))
         psum = ctx.enter_context(tc.psum_pool(name="psum", bufs=1))
 
         offs_sb = keep.tile([P, S // LANE], U16, name="offs_sb")
@@ -68,7 +77,7 @@ def tile_moe_pre_lin_relu2_kernel(
         bias_sb = keep.tile([P, E], F32, name="bias_sb")
         columns = [WIDE + PAD] * (PASSES - 1) + [T + PAD]
         x_sb = [[keep.tile([P, columns[a]], F32, name=f"x_sb{a}_{t}") for t in range(PACK)] for a in range(PASSES)]
-        gated_sb = keep.tile([P, 7 * WIDE], F32, name="gated_sb")
+        gated_sb = keep.tile([P, STAGED_PLANES * WIDE], F32, name="gated_sb")
         w_sb = keep.tile([P, HELD * PASSES, 2 * N], U8, name="w_sb", align_bytes=64)
         ws_sb = keep.tile([P, HELD * PASSES, N], U8, name="ws_sb", align_bytes=64)
         y_sb = keep.tile([P, S], F32, name="y_sb")
@@ -93,10 +102,13 @@ def tile_moe_pre_lin_relu2_kernel(
                 in_=w_words[e0:e1].rearrange("e a p m -> p (e a) m").bitcast(I32),
             )
 
-        nc.gpsimd.memset(ws_sb[:].rearrange("p g n -> p (g n)").bitcast(I32), 0)
-        for i in range(PASSES * PACK):
-            engine = nc.vector if i < VECTOR_PADS else nc.gpsimd
-            engine.memset(x_sb[i // PACK][i % PACK][:, T : columns[i // PACK]].bitcast(I32), 0)
+        pads = [x_sb[a][t][:, T : columns[a]] for a in range(PASSES) for t in range(PACK)]
+        wide_pads = (PASSES - 1) * PACK
+        for pad in pads[0:1] + pads[wide_pads:]:
+            nc.vector.memset(pad.bitcast(I32), 0)
+        for pad in pads[1:wide_pads]:
+            nc.scalar.copy(out=pad, in_=pads[0])
+        nc.vector.memset(ws_sb[:].rearrange("p g n -> p (g n)").bitcast(I32), 0)
 
         nc.sync.dma_start(offs_sb[:], offs)
         load_x(0, 0)
@@ -112,10 +124,7 @@ def tile_moe_pre_lin_relu2_kernel(
             nc.sync.dma_start(pos_sb[r][:], pos)
 
         def gather(i, a, s0, w):
-            if w == WIDE:
-                base = (1 - i) * (PACK - 1) * WIDE
-            else:
-                base = (2 if i == 2 else 2 - (i - 4) % 3) * PACK * CHUNK
+            base = staging_start(i)
             gated = gated_sb[:, base : base + PACK * w].rearrange("p (t c) -> p t c", t=PACK)
             for t in range(PACK):
                 cuts = FIRST_CUTS if i == 0 and t == 0 else (0, w)
@@ -128,8 +137,8 @@ def tile_moe_pre_lin_relu2_kernel(
                     )
             return gated
 
-        def interleave(copy, w, gated):
-            grouped = stage.tile([P, w, PACK], BF16, name="grouped", align_bytes=64, bufs=LAG + 1)
+        def weave(copy, w, gated):
+            grouped = stage.tile([P, w, PACK], BF16, name="grouped", align_bytes=64)
             copy(
                 out=grouped[:].rearrange("p (c i) t -> p c t i", i=4),
                 in_=gated.rearrange("p t (c i) -> p c t i", i=4),
@@ -181,40 +190,40 @@ def tile_moe_pre_lin_relu2_kernel(
 
         plan = steps()
         last = len(plan) - 1
-        halves = {}
+        wide_woven = {}
         for i in range(PASSES - 1):
             gated = gather(i, *plan[i])
             for s0 in range(0, WIDE, CHUNK):
-                halves[i, s0] = interleave(nc.scalar.copy, CHUNK, gated[:, :, s0 : s0 + CHUNK])
+                wide_woven[i, s0] = weave(nc.scalar.copy, CHUNK, gated[:, :, s0 : s0 + CHUNK])
                 if i > 0:
-                    multiply(i - 1, s0, CHUNK, halves[i - 1, s0])
+                    multiply(i - 1, s0, CHUNK, wide_woven[i - 1, s0])
         woven = {}
         for i in range(PASSES - 1, last):
-            woven[i] = interleave(nc.scalar.copy, plan[i][2], gather(i, *plan[i]))
+            woven[i] = weave(nc.scalar.copy, plan[i][2], gather(i, *plan[i]))
             if i == 2:
                 for s0 in range(0, WIDE, CHUNK):
-                    multiply(1, s0, CHUNK, halves[1, s0])
+                    multiply(1, s0, CHUNK, wide_woven[1, s0])
             elif i == 3:
                 multiply(*plan[2], woven[2])
                 load_w(HELD, E)
-            elif i > 4:
+            elif i - LAG > 2:
                 multiply(*plan[i - LAG], woven[i - LAG])
         gated = gather(last, *plan[last])
         for i in range(last - LAG, last):
             multiply(*plan[i], woven[i])
-        multiply(*plan[last], interleave(nc.vector.tensor_copy, plan[last][2], gated))
+        multiply(*plan[last], weave(nc.vector.tensor_copy, plan[last][2], gated))
 
         picked, pair, total = (gated_sb[:, r * T : (r + 1) * T] for r in range(3))
-        halves = (slice(0, OUT_CUTS[1]), slice(OUT_CUTS[1], T))
+        parts = (slice(0, OUT_CUTS[1]), slice(OUT_CUTS[1], T))
 
-        def window(r, cols):
+        def results(r, cols):
             return y_sb[:].indirect(pos_sb[r][:, cols.start // LANE : cols.stop // LANE])
 
-        for cols in halves:
-            nc.vector.tensor_copy(picked[:, cols], window(0, cols))
-        for cols in halves:
-            nc.vector.tensor_tensor(pair[:, cols], window(1, cols), picked[:, cols], ADD)
+        for cols in parts:
+            nc.vector.tensor_copy(picked[:, cols], results(0, cols))
+        for cols in parts:
+            nc.vector.tensor_tensor(pair[:, cols], results(1, cols), picked[:, cols], ADD)
         for c0, c1 in zip(OUT_CUTS, OUT_CUTS[1:]):
             cols = slice(c0, c1)
-            nc.vector.tensor_tensor(total[:, cols], window(2, cols), pair[:, cols], ADD)
+            nc.vector.tensor_tensor(total[:, cols], results(2, cols), pair[:, cols], ADD)
             nc.sync.dma_start(out=out[:, cols], in_=total[:, cols])

@@ -24,41 +24,20 @@ FP8X4 = mybir.dt.float8_e4m3fn_x4
 FP4X4 = mybir.dt.float4_e2m1fn_x4
 MULT = mybir.AluOpType.mult
 ADD = mybir.AluOpType.add
+MAX = mybir.AluOpType.max
 ACT = mybir.ActivationFunctionType
 
 CHUNK = 1024
 WIDE = 2 * CHUNK
 FIRST_CUTS = (0, 128, 384, CHUNK, WIDE)
-LAST_GROUPS = (CHUNK // 2, CHUNK // 4, CHUNK // 4)
-LAG = 2
-OUT_CUTS = (0, 640, 896, T)
 EARLY = 2
-HELD = WIDE // C
-STAGED_PLANES = 2 * PACK - 1
-RING = 3
+TAIL = EARLY * C
+BODY = CHUNK - TAIL
+HALF = CHUNK // 2
+OUT_CUTS = (0, 640, 896, T)
+ON_VECTOR = E - EARLY
+WOVEN_BUFS = 3
 CODE_BUFS = 6
-
-
-def steps():
-    plan = [(a, 0, WIDE) for a in range(PASSES - 1)]
-    plan.extend((PASSES - 1, s0, CHUNK) for s0 in range(0, WIDE, CHUNK))
-    s0 = S - CHUNK
-    plan.append((0, s0, CHUNK))
-    for w in LAST_GROUPS:
-        plan.append((1, s0, w))
-        if s0 + w < S:
-            plan.append((2, s0, w))
-        else:
-            plan.extend((2, s, C) for s in range(s0, S, C))
-        s0 += w
-    return plan
-
-
-def staging_start(i):
-    if i < 2:
-        return (1 - i) * (PACK - 1) * WIDE
-    place = RING - 1 if i == 2 else RING - 1 - (i - 4) % RING
-    return place * PACK * CHUNK
 
 
 def tile_moe_pre_lin_relu2_kernel(
@@ -67,7 +46,7 @@ def tile_moe_pre_lin_relu2_kernel(
     nc = tc.nc
     with ExitStack() as ctx:
         keep = ctx.enter_context(tc.tile_pool(name="keep", bufs=1))
-        stage = ctx.enter_context(tc.tile_pool(name="stage", bufs=LAG + 1))
+        stage = ctx.enter_context(tc.tile_pool(name="stage", bufs=WOVEN_BUFS))
         quant = ctx.enter_context(tc.tile_pool(name="quant", bufs=CODE_BUFS))
         psum = ctx.enter_context(tc.psum_pool(name="psum", bufs=1))
 
@@ -77,9 +56,9 @@ def tile_moe_pre_lin_relu2_kernel(
         bias_sb = keep.tile([P, E], F32, name="bias_sb")
         columns = [WIDE + PAD] * (PASSES - 1) + [T + PAD]
         x_sb = [[keep.tile([P, columns[a]], F32, name=f"x_sb{a}_{t}") for t in range(PACK)] for a in range(PASSES)]
-        gated_sb = keep.tile([P, STAGED_PLANES * WIDE], F32, name="gated_sb")
-        w_sb = keep.tile([P, HELD * PASSES, 2 * N], U8, name="w_sb", align_bytes=64)
-        ws_sb = keep.tile([P, HELD * PASSES, N], U8, name="ws_sb", align_bytes=64)
+        gated_sb = keep.tile([P, PACK * (CHUNK + WIDE)], F32, name="gated_sb")
+        w_sb = keep.tile([P, E * PASSES, 2 * N], U8, name="w_sb", align_bytes=64)
+        ws_sb = keep.tile([P, E * PASSES, N], U8, name="ws_sb", align_bytes=64)
         y_sb = keep.tile([P, S], F32, name="y_sb")
 
         x_rows = xT.rearrange("(a p t) c -> a t p c", p=P, t=PACK)
@@ -90,44 +69,35 @@ def tile_moe_pre_lin_relu2_kernel(
         def load_gate(c0, c1):
             nc.sync.dma_start(out=gate_sb[:, c0:c1], in_=gate[0:P, c0:c1])
 
-        ws_rows = w_scales.rearrange("e a (g r) n -> r g (e a) n", r=4)
-
-        def load_w(e0, e1):
-            groups = slice(e0 * PASSES, e1 * PASSES)
-            places = slice(e0 % HELD * PASSES, (e0 % HELD + e1 - e0) * PASSES)
-            for r in range(4):
-                nc.sync.dma_start(out=ws_sb[r:P:32, places, :].bitcast(I32), in_=ws_rows[r, :, groups].bitcast(I32))
-            nc.sync.dma_start(
-                out=w_sb[:, places, :].bitcast(I32),
-                in_=w_words[e0:e1].rearrange("e a p m -> p (e a) m").bitcast(I32),
-            )
-
-        pads = [x_sb[a][t][:, T : columns[a]] for a in range(PASSES) for t in range(PACK)]
-        wide_pads = (PASSES - 1) * PACK
-        for pad in pads[0:1] + pads[wide_pads:]:
-            nc.vector.memset(pad.bitcast(I32), 0)
-        for pad in pads[1:wide_pads]:
-            nc.scalar.copy(out=pad, in_=pads[0])
         nc.vector.memset(ws_sb[:].rearrange("p g n -> p (g n)").bitcast(I32), 0)
 
         nc.sync.dma_start(offs_sb[:], offs)
         load_x(0, 0)
         for c0, c1 in zip(FIRST_CUTS, FIRST_CUTS[1:]):
             load_gate(c0, c1)
-        for i in range(1, PASSES * PACK):
-            load_x(i // PACK, i % PACK)
+        for t in range(1, PACK):
+            load_x(0, t)
         load_gate(WIDE, S)
+        for i in range(PACK, PASSES * PACK):
+            load_x(i // PACK, i % PACK)
         nc.sync.dma_start(out=bias_sb[:], in_=b)
-        for e0 in range(0, HELD, BANKS):
-            load_w(e0, e0 + BANKS)
+        ws_rows = w_scales.rearrange("e a (g r) n -> r g (e a) n", r=4)
+        w_rows = w_words.rearrange("e a p m -> p (e a) m")
+        for g0 in range(0, E * PASSES, BANKS * PASSES):
+            groups = slice(g0, g0 + BANKS * PASSES)
+            for r in range(4):
+                nc.sync.dma_start(out=ws_sb[r:P:32, groups, :].bitcast(I32), in_=ws_rows[r, :, groups].bitcast(I32))
+            nc.sync.dma_start(out=w_sb[:, groups, :].bitcast(I32), in_=w_rows[:, groups, :].bitcast(I32))
         for r, pos in enumerate((pos1, pos2, pos3)):
             nc.sync.dma_start(pos_sb[r][:], pos)
 
-        def gather(i, a, s0, w):
-            base = staging_start(i)
-            gated = gated_sb[:, base : base + PACK * w].rearrange("p (t c) -> p t c", t=PACK)
+        def room(c0, pitch):
+            return gated_sb[:, c0 : c0 + PACK * pitch].rearrange("p (t c) -> p t c", t=PACK)
+
+        def gather(gated, a, s0, first_cuts=None, last_cuts=None):
+            w = gated.shape[2]
             for t in range(PACK):
-                cuts = FIRST_CUTS if i == 0 and t == 0 else (0, w)
+                cuts = {0: first_cuts, PACK - 1: last_cuts}.get(t) or (0, w)
                 for c0, c1 in zip(cuts, cuts[1:]):
                     nc.vector.tensor_tensor(
                         gated[:, t, c0:c1],
@@ -135,83 +105,119 @@ def tile_moe_pre_lin_relu2_kernel(
                         gate_sb[:, s0 + c0 : s0 + c1],
                         MULT,
                     )
-            return gated
 
-        def weave(copy, w, gated):
-            grouped = stage.tile([P, w, PACK], BF16, name="grouped", align_bytes=64)
-            copy(
-                out=grouped[:].rearrange("p (c i) t -> p c t i", i=4),
+        def weave(gated, grouped):
+            nc.scalar.copy(
+                out=grouped.rearrange("p (c i) t -> p c t i", i=4),
                 in_=gated.rearrange("p t (c i) -> p c t i", i=4),
             )
+
+        def woven(gated, cuts=(0, CHUNK)):
+            grouped = stage.tile([P, CHUNK, PACK], BF16, name="grouped", align_bytes=64)
+            for c0, c1 in zip(cuts, cuts[1:]):
+                weave(gated[:, :, c0:c1], grouped[:, c0:c1, :])
             return grouped
 
         held = {}
-        early = {e: psum.tile([N, C], F32, name=f"early{e}") for e in range(E - EARLY, E)}
+        sums = {}
+        banks = {}
 
-        def matmul(acc, e, a):
+        def matmul(acc, e, a, start, stop):
             codes, scales, s0 = held[e, a]
             cols = slice(e * C - s0, (e + 1) * C - s0)
-            g = e % HELD * PASSES + a
+            g = e * PASSES + a
             nc.tensor.matmul_mx(
                 out=acc,
                 lhsT=w_sb[:, g, :].bitcast(FP4X4),
                 lhsT_scale=ws_sb[:, g, :],
                 rhs=codes[:, cols].bitcast(FP8X4),
                 rhs_scale=scales[:, cols],
-                start=(a == 0),
-                stop=(a == PASSES - 1),
+                start=start,
+                stop=stop,
             )
 
-        def multiply(a, s0, w, grouped):
-            codes = quant.tile([P, w], U32, name="codes", align_bytes=64)
-            scales = quant.tile([P, w], U8, name="scales", align_bytes=64)
+        def begin(e, passes):
+            banks[e] = psum.tile([N, C], F32, name="bank", bufs=BANKS)
+            for g in range(passes):
+                matmul(banks[e][:], e, g, g == 0, False)
+
+        def multiply(a, s0, grouped):
+            w = grouped.shape[1]
+            if w > TAIL:
+                codes = quant.tile([P, w], U32, name="codes", align_bytes=64)
+                scales = quant.tile([P, w], U8, name="scales", align_bytes=64)
+            else:
+                codes = keep.tile([P, w], U32, name=f"codes{s0}", align_bytes=64)
+                scales = keep.tile([P, w], U8, name=f"scales{s0}", align_bytes=64)
             nc.vector.quantize_mx(
-                out=codes[:].bitcast(FP8X4), scales=scales[:], in_=grouped[:].rearrange("p c t -> p (c t)")
+                out=codes[:].bitcast(FP8X4), scales=scales[:], in_=grouped.rearrange("p c t -> p (c t)")
             )
             experts = range(s0 // C, (s0 + w) // C)
+            last = a == PASSES - 1
             for e in experts:
                 held[e, a] = (codes, scales, s0)
-            if a < PASSES - 1:
-                for e in experts:
-                    if e in early:
-                        matmul(early[e][:], e, a)
-                return
-            for e in experts:
-                if e in early:
-                    acc = early[e][:]
-                    matmul(acc, e, a)
-                else:
-                    bank = psum.tile([N, C], F32, name="bank", bufs=BANKS - EARLY)
-                    acc = bank[:]
-                    for g in range(PASSES):
-                        matmul(acc, e, g)
-                nc.scalar.activation(y_sb[:, e * C : (e + 1) * C], acc, ACT.Relu, bias=bias_sb[:, e : e + 1])
-            nc.scalar.activation(y_sb[:, s0 : s0 + w], y_sb[:, s0 : s0 + w], ACT.Square)
+                if a == 0:
+                    continue
+                if e not in banks and last:
+                    begin(e, a)
+                if e in banks:
+                    matmul(banks[e][:], e, a, False, last)
+                if last:
+                    acc = banks[e][:]
+                if last and e < ON_VECTOR:
+                    nc.scalar.activation(y_sb[:, e * C : (e + 1) * C], acc, ACT.Relu, bias=bias_sb[:, e : e + 1])
+                elif last:
+                    sums[e] = acc
+            if last and s0 < WIDE:
+                for c0 in range(s0, s0 + w, HALF):
+                    nc.scalar.activation(y_sb[:, c0 : c0 + HALF], y_sb[:, c0 : c0 + HALF], ACT.Square)
 
-        plan = steps()
-        last = len(plan) - 1
-        wide_woven = {}
-        for i in range(PASSES - 1):
-            gated = gather(i, *plan[i])
-            for s0 in range(0, WIDE, CHUNK):
-                wide_woven[i, s0] = weave(nc.scalar.copy, CHUNK, gated[:, :, s0 : s0 + CHUNK])
-                if i > 0:
-                    multiply(i - 1, s0, CHUNK, wide_woven[i - 1, s0])
-        woven = {}
-        for i in range(PASSES - 1, last):
-            woven[i] = weave(nc.scalar.copy, plan[i][2], gather(i, *plan[i]))
-            if i == 2:
-                for s0 in range(0, WIDE, CHUNK):
-                    multiply(1, s0, CHUNK, wide_woven[1, s0])
-            elif i == 3:
-                multiply(*plan[2], woven[2])
-                load_w(HELD, E)
-            elif i - LAG > 2:
-                multiply(*plan[i - LAG], woven[i - LAG])
-        gated = gather(last, *plan[last])
-        for i in range(last - LAG, last):
-            multiply(*plan[i], woven[i])
-        multiply(*plan[last], weave(nc.vector.tensor_copy, plan[last][2], gated))
+        lower = room(0, CHUNK)
+        upper = room(PACK * CHUNK, WIDE)
+        halves = [upper[:, :, 0:CHUNK], upper[:, :, CHUNK:WIDE]]
+
+        gather(upper, 0, 0, FIRST_CUTS)
+        first = [woven(half) for half in halves]
+
+        gather(lower, 0, WIDE)
+        first.append(woven(lower))
+        multiply(0, 0, first[0][:])
+        multiply(0, CHUNK, first[1][:])
+
+        gather(upper, 1, 0)
+        second = [woven(half) for half in halves]
+        multiply(0, WIDE, first[2][:])
+
+        gather(lower, 2, 0)
+        third = [woven(lower)]
+        multiply(1, 0, second[0][:])
+        multiply(1, CHUNK, second[1][:])
+
+        gather(halves[1], 2, CHUNK)
+        third.append(woven(halves[1]))
+        multiply(2, 0, third[0][:])
+
+        gather(lower, 1, WIDE)
+        second.append(woven(lower))
+        multiply(2, CHUNK, third[1][:])
+        for e in range(WIDE // C, E):
+            begin(e, 1)
+
+        gather(halves[1][:, :, 0:BODY], 2, WIDE, last_cuts=(0, HALF, BODY))
+        body = woven(halves[1], (0, HALF, BODY))
+        multiply(1, WIDE, second[2][:, 0:HALF, :])
+
+        gather(lower[:, :, 0:TAIL], 2, S - TAIL)
+        tail = woven(lower, (0, TAIL))
+        multiply(1, WIDE + HALF, second[2][:, HALF:CHUNK, :])
+        multiply(2, WIDE, body[:, 0:HALF, :])
+        multiply(2, WIDE + HALF, body[:, HALF:BODY, :])
+        nc.scalar.activation(y_sb[:, WIDE : S - HALF], y_sb[:, WIDE : S - HALF], ACT.Square)
+        multiply(2, S - TAIL, tail[:, 0:TAIL, :])
+        for e in range(ON_VECTOR, E):
+            nc.vector.tensor_scalar(y_sb[:, e * C : (e + 1) * C], sums[e], bias_sb[:, e : e + 1], 0.0, ADD, MAX)
+        for cols in (slice(S - HALF, S - C), slice(S - C, S)):
+            nc.vector.tensor_tensor(y_sb[:, cols], y_sb[:, cols], y_sb[:, cols], MULT)
 
         picked, pair, total = (gated_sb[:, r * T : (r + 1) * T] for r in range(3))
         parts = (slice(0, OUT_CUTS[1]), slice(OUT_CUTS[1], T))

@@ -35,7 +35,7 @@ TAIL = EARLY * C
 BODY = CHUNK - TAIL
 HALF = CHUNK // 2
 OUT_CUTS = (0, 640, 896, T)
-ON_VECTOR = E - EARLY
+ON_VECTOR = E - 1
 WOVEN_BUFS = 3
 CODE_BUFS = 6
 
@@ -106,8 +106,8 @@ def tile_moe_pre_lin_relu2_kernel(
                         MULT,
                     )
 
-        def weave(gated, grouped):
-            nc.scalar.copy(
+        def weave(gated, grouped, copy=nc.scalar.copy):
+            copy(
                 out=grouped.rearrange("p (c i) t -> p c t i", i=4),
                 in_=gated.rearrange("p t (c i) -> p c t i", i=4),
             )
@@ -141,6 +141,9 @@ def tile_moe_pre_lin_relu2_kernel(
             for g in range(passes):
                 matmul(banks[e][:], e, g, g == 0, False)
 
+        def square(c0, c1):
+            nc.scalar.activation(y_sb[:, c0:c1], y_sb[:, c0:c1], ACT.Square)
+
         def multiply(a, s0, grouped):
             w = grouped.shape[1]
             if w > TAIL:
@@ -168,9 +171,6 @@ def tile_moe_pre_lin_relu2_kernel(
                     nc.scalar.activation(y_sb[:, e * C : (e + 1) * C], acc, ACT.Relu, bias=bias_sb[:, e : e + 1])
                 elif last:
                     sums[e] = acc
-            if last and s0 < WIDE:
-                for c0 in range(s0, s0 + w, HALF):
-                    nc.scalar.activation(y_sb[:, c0 : c0 + HALF], y_sb[:, c0 : c0 + HALF], ACT.Square)
 
         lower = room(0, CHUNK)
         upper = room(PACK * CHUNK, WIDE)
@@ -196,28 +196,37 @@ def tile_moe_pre_lin_relu2_kernel(
         gather(halves[1], 2, CHUNK)
         third.append(woven(halves[1]))
         multiply(2, 0, third[0][:])
+        square(0, HALF)
+        square(HALF, CHUNK)
 
         gather(lower, 1, WIDE)
         second.append(woven(lower))
         multiply(2, CHUNK, third[1][:])
+        square(CHUNK, CHUNK + HALF)
+        square(CHUNK + HALF, WIDE)
         for e in range(WIDE // C, E):
             begin(e, 1)
 
-        gather(halves[1][:, :, 0:BODY], 2, WIDE, last_cuts=(0, HALF, BODY))
-        body = woven(halves[1], (0, HALF, BODY))
-        multiply(1, WIDE, second[2][:, 0:HALF, :])
+        gather(halves[1][:, :, 0:HALF], 2, WIDE)
+        half = woven(halves[1], (0, HALF))
+        multiply(1, WIDE, second[2][:])
 
-        gather(lower[:, :, 0:TAIL], 2, S - TAIL)
-        tail = woven(lower, (0, TAIL))
-        multiply(1, WIDE + HALF, second[2][:, HALF:CHUNK, :])
-        multiply(2, WIDE, body[:, 0:HALF, :])
-        multiply(2, WIDE + HALF, body[:, HALF:BODY, :])
-        nc.scalar.activation(y_sb[:, WIDE : S - HALF], y_sb[:, WIDE : S - HALF], ACT.Square)
-        multiply(2, S - TAIL, tail[:, 0:TAIL, :])
-        for e in range(ON_VECTOR, E):
-            nc.vector.tensor_scalar(y_sb[:, e * C : (e + 1) * C], sums[e], bias_sb[:, e : e + 1], 0.0, ADD, MAX)
-        for cols in (slice(S - HALF, S - C), slice(S - C, S)):
-            nc.vector.tensor_tensor(y_sb[:, cols], y_sb[:, cols], y_sb[:, cols], MULT)
+        gather(lower[:, :, 0:TAIL], 2, WIDE + HALF)
+        quarter = woven(lower, (0, TAIL))
+        multiply(2, WIDE, half[:, 0:HALF, :])
+
+        gather(halves[1][:, :, 0:TAIL], 2, S - TAIL)
+        weave(halves[1][:, :, C:TAIL], quarter[:, TAIL + C : HALF, :])
+        square(WIDE, WIDE + HALF)
+        multiply(2, WIDE + HALF, quarter[:, 0:TAIL, :])
+        square(WIDE + HALF, S - TAIL)
+        weave(halves[1][:, :, 0:C], quarter[:, TAIL : TAIL + C, :], nc.vector.tensor_copy)
+        multiply(2, S - TAIL, quarter[:, TAIL : TAIL + C, :])
+        square(S - TAIL, S - C)
+        multiply(2, S - C, quarter[:, TAIL + C : HALF, :])
+        cols = slice(S - C, S)
+        nc.vector.tensor_scalar(y_sb[:, cols], sums[E - 1], bias_sb[:, E - 1 : E], 0.0, ADD, MAX)
+        nc.vector.tensor_tensor(y_sb[:, cols], y_sb[:, cols], y_sb[:, cols], MULT)
 
         picked, pair, total = (gated_sb[:, r * T : (r + 1) * T] for r in range(3))
         parts = (slice(0, OUT_CUTS[1]), slice(OUT_CUTS[1], T))

@@ -209,24 +209,25 @@ def tile_moe_pre_lin_relu2_kernel(
 
         gather(halves[1][:, :, 0:HALF], 2, WIDE)
         half = woven(halves[1], (0, HALF))
-        multiply(1, WIDE, second[2][:])
+        multiply(1, WIDE, second[2][:, 0:HALF, :])
 
         gather(lower[:, :, 0:TAIL], 2, WIDE + HALF)
         quarter = woven(lower, (0, TAIL))
+        multiply(1, WIDE + HALF, second[2][:, HALF:CHUNK, :])
         multiply(2, WIDE, half[:, 0:HALF, :])
+        square(WIDE, WIDE + TAIL)
+        square(WIDE + TAIL, WIDE + HALF)
 
         gather(halves[1][:, :, 0:TAIL], 2, S - TAIL)
         weave(halves[1][:, :, C:TAIL], quarter[:, TAIL + C : HALF, :])
-        square(WIDE, WIDE + HALF)
         multiply(2, WIDE + HALF, quarter[:, 0:TAIL, :])
-        square(WIDE + HALF, S - TAIL)
         weave(halves[1][:, :, 0:C], quarter[:, TAIL : TAIL + C, :], nc.vector.tensor_copy)
         multiply(2, S - TAIL, quarter[:, TAIL : TAIL + C, :])
         square(S - TAIL, S - C)
         multiply(2, S - C, quarter[:, TAIL + C : HALF, :])
-        cols = slice(S - C, S)
-        nc.vector.tensor_scalar(y_sb[:, cols], sums[E - 1], bias_sb[:, E - 1 : E], 0.0, ADD, MAX)
-        nc.vector.tensor_tensor(y_sb[:, cols], y_sb[:, cols], y_sb[:, cols], MULT)
+        nc.vector.tensor_scalar(y_sb[:, S - C : S], sums[E - 1], bias_sb[:, E - 1 : E], 0.0, ADD, MAX)
+        for cols in (slice(WIDE + HALF, S - TAIL), slice(S - C, S)):
+            nc.vector.tensor_tensor(y_sb[:, cols], y_sb[:, cols], y_sb[:, cols], MULT)
 
         picked, pair, total = (gated_sb[:, r * T : (r + 1) * T] for r in range(3))
         parts = (slice(0, OUT_CUTS[1]), slice(OUT_CUTS[1], T))

@@ -29,13 +29,10 @@ ACT = mybir.ActivationFunctionType
 
 CHUNK = 1024
 WIDE = 2 * CHUNK
-FIRST_CUTS = (0, 128, 384, CHUNK, WIDE)
-EARLY = 2
-TAIL = EARLY * C
-BODY = CHUNK - TAIL
 HALF = CHUNK // 2
+QUARTER = CHUNK // 4
+FIRST_CUTS = (0, 160, 448, CHUNK, WIDE)
 OUT_CUTS = (0, 640, 896, T)
-ON_VECTOR = E - 1
 WOVEN_BUFS = 3
 CODE_BUFS = 6
 
@@ -91,14 +88,10 @@ def tile_moe_pre_lin_relu2_kernel(
         for r, pos in enumerate((pos1, pos2, pos3)):
             nc.sync.dma_start(pos_sb[r][:], pos)
 
-        def room(c0, pitch):
-            return gated_sb[:, c0 : c0 + PACK * pitch].rearrange("p (t c) -> p t c", t=PACK)
-
-        def gather(gated, a, s0, first_cuts=None, last_cuts=None):
-            w = gated.shape[2]
+        def gather(gated, a, s0, cuts=None):
             for t in range(PACK):
-                cuts = {0: first_cuts, PACK - 1: last_cuts}.get(t) or (0, w)
-                for c0, c1 in zip(cuts, cuts[1:]):
+                edges = (cuts or {}).get(t, (0, gated.shape[2]))
+                for c0, c1 in zip(edges, edges[1:]):
                     nc.vector.tensor_tensor(
                         gated[:, t, c0:c1],
                         x_sb[a][t][:].indirect(offs_sb[:, (s0 + c0) // LANE : (s0 + c1) // LANE]),
@@ -106,47 +99,42 @@ def tile_moe_pre_lin_relu2_kernel(
                         MULT,
                     )
 
-        def weave(gated, grouped, copy=nc.scalar.copy):
+        def weave(copy, gated, grouped):
             copy(
                 out=grouped.rearrange("p (c i) t -> p c t i", i=4),
                 in_=gated.rearrange("p t (c i) -> p c t i", i=4),
             )
 
-        def woven(gated, cuts=(0, CHUNK)):
+        def woven(gated):
             grouped = stage.tile([P, CHUNK, PACK], BF16, name="grouped", align_bytes=64)
-            for c0, c1 in zip(cuts, cuts[1:]):
-                weave(gated[:, :, c0:c1], grouped[:, c0:c1, :])
+            weave(nc.scalar.copy, gated, grouped[:, 0 : gated.shape[2], :])
             return grouped
 
         held = {}
-        sums = {}
         banks = {}
 
-        def matmul(acc, e, a, start, stop):
+        def matmul(e, a):
             codes, scales, s0 = held[e, a]
             cols = slice(e * C - s0, (e + 1) * C - s0)
             g = e * PASSES + a
             nc.tensor.matmul_mx(
-                out=acc,
+                out=banks[e][:],
                 lhsT=w_sb[:, g, :].bitcast(FP4X4),
                 lhsT_scale=ws_sb[:, g, :],
                 rhs=codes[:, cols].bitcast(FP8X4),
                 rhs_scale=scales[:, cols],
-                start=start,
-                stop=stop,
+                start=(a == 0),
+                stop=(a == PASSES - 1),
             )
 
         def begin(e, passes):
             banks[e] = psum.tile([N, C], F32, name="bank", bufs=BANKS)
-            for g in range(passes):
-                matmul(banks[e][:], e, g, g == 0, False)
-
-        def square(c0, c1):
-            nc.scalar.activation(y_sb[:, c0:c1], y_sb[:, c0:c1], ACT.Square)
+            for a in range(passes):
+                matmul(e, a)
 
         def multiply(a, s0, grouped):
             w = grouped.shape[1]
-            if w > TAIL:
+            if w > QUARTER:
                 codes = quant.tile([P, w], U32, name="codes", align_bytes=64)
                 scales = quant.tile([P, w], U8, name="scales", align_bytes=64)
             else:
@@ -155,78 +143,76 @@ def tile_moe_pre_lin_relu2_kernel(
             nc.vector.quantize_mx(
                 out=codes[:].bitcast(FP8X4), scales=scales[:], in_=grouped.rearrange("p c t -> p (c t)")
             )
-            experts = range(s0 // C, (s0 + w) // C)
-            last = a == PASSES - 1
-            for e in experts:
+            for e in range(s0 // C, (s0 + w) // C):
                 held[e, a] = (codes, scales, s0)
-                if a == 0:
-                    continue
-                if e not in banks and last:
+                if a == PASSES - 1 and e not in banks:
                     begin(e, a)
                 if e in banks:
-                    matmul(banks[e][:], e, a, False, last)
-                if last:
-                    acc = banks[e][:]
-                if last and e < ON_VECTOR:
-                    nc.scalar.activation(y_sb[:, e * C : (e + 1) * C], acc, ACT.Relu, bias=bias_sb[:, e : e + 1])
-                elif last:
-                    sums[e] = acc
+                    matmul(e, a)
+                if a == PASSES - 1 and e < E - 1:
+                    nc.scalar.activation(
+                        y_sb[:, e * C : (e + 1) * C], banks[e][:], ACT.Relu, bias=bias_sb[:, e : e + 1]
+                    )
 
-        lower = room(0, CHUNK)
-        upper = room(PACK * CHUNK, WIDE)
-        halves = [upper[:, :, 0:CHUNK], upper[:, :, CHUNK:WIDE]]
+        def square(s0, w, pieces):
+            for c0 in range(s0, s0 + w, w // pieces):
+                cols = slice(c0, c0 + w // pieces)
+                nc.scalar.activation(y_sb[:, cols], y_sb[:, cols], ACT.Square)
 
-        gather(upper, 0, 0, FIRST_CUTS)
-        first = [woven(half) for half in halves]
+        narrow = gated_sb[:, 0 : PACK * CHUNK].rearrange("p (t c) -> p t c", t=PACK)
+        wide = gated_sb[:, PACK * CHUNK :].rearrange("p (t c) -> p t c", t=PACK)
+        halves = [wide[:, :, 0:CHUNK], wide[:, :, CHUNK:WIDE]]
 
-        gather(lower, 0, WIDE)
-        first.append(woven(lower))
-        multiply(0, 0, first[0][:])
-        multiply(0, CHUNK, first[1][:])
+        gather(wide, 0, 0, {0: FIRST_CUTS})
+        pass0 = [woven(half) for half in halves]
 
-        gather(upper, 1, 0)
-        second = [woven(half) for half in halves]
-        multiply(0, WIDE, first[2][:])
+        gather(narrow, 0, WIDE)
+        pass0.append(woven(narrow))
+        multiply(0, 0, pass0[0][:])
+        multiply(0, CHUNK, pass0[1][:])
 
-        gather(lower, 2, 0)
-        third = [woven(lower)]
-        multiply(1, 0, second[0][:])
-        multiply(1, CHUNK, second[1][:])
+        gather(wide, 1, 0)
+        pass1 = [woven(half) for half in halves]
+        multiply(0, WIDE, pass0[2][:])
+
+        gather(narrow, 2, 0)
+        pass2 = [woven(narrow)]
+        multiply(1, 0, pass1[0][:])
+        multiply(1, CHUNK, pass1[1][:])
 
         gather(halves[1], 2, CHUNK)
-        third.append(woven(halves[1]))
-        multiply(2, 0, third[0][:])
-        square(0, HALF)
-        square(HALF, CHUNK)
+        pass2.append(woven(halves[1]))
+        multiply(2, 0, pass2[0][:])
+        square(0, CHUNK, 2)
 
-        gather(lower, 1, WIDE)
-        second.append(woven(lower))
-        multiply(2, CHUNK, third[1][:])
-        square(CHUNK, CHUNK + HALF)
-        square(CHUNK + HALF, WIDE)
+        gather(narrow, 1, WIDE)
+        pass1.append(woven(narrow))
+        multiply(2, CHUNK, pass2[1][:])
+        square(CHUNK, CHUNK, 2)
         for e in range(WIDE // C, E):
             begin(e, 1)
 
         gather(halves[1][:, :, 0:HALF], 2, WIDE)
-        half = woven(halves[1], (0, HALF))
-        multiply(1, WIDE, second[2][:, 0:HALF, :])
+        half_woven = woven(halves[1][:, :, 0:HALF])
+        multiply(1, WIDE, pass1[2][:, 0:HALF, :])
 
-        gather(lower[:, :, 0:TAIL], 2, WIDE + HALF)
-        quarter = woven(lower, (0, TAIL))
-        multiply(1, WIDE + HALF, second[2][:, HALF:CHUNK, :])
-        multiply(2, WIDE, half[:, 0:HALF, :])
-        square(WIDE, WIDE + TAIL)
-        square(WIDE + TAIL, WIDE + HALF)
+        gather(narrow[:, :, 0:QUARTER], 2, WIDE + HALF)
+        quarters_woven = woven(narrow[:, :, 0:QUARTER])
+        multiply(1, WIDE + HALF, pass1[2][:, HALF:CHUNK, :])
+        multiply(2, WIDE, half_woven[:, 0:HALF, :])
+        square(WIDE, HALF, 2)
 
-        gather(halves[1][:, :, 0:TAIL], 2, S - TAIL)
-        weave(halves[1][:, :, C:TAIL], quarter[:, TAIL + C : HALF, :])
-        multiply(2, WIDE + HALF, quarter[:, 0:TAIL, :])
-        weave(halves[1][:, :, 0:C], quarter[:, TAIL : TAIL + C, :], nc.vector.tensor_copy)
-        multiply(2, S - TAIL, quarter[:, TAIL : TAIL + C, :])
-        square(S - TAIL, S - C)
-        multiply(2, S - C, quarter[:, TAIL + C : HALF, :])
-        nc.vector.tensor_scalar(y_sb[:, S - C : S], sums[E - 1], bias_sb[:, E - 1 : E], 0.0, ADD, MAX)
-        for cols in (slice(WIDE + HALF, S - TAIL), slice(S - C, S)):
+        last_gated = halves[1][:, :, 0:QUARTER]
+        last_woven = quarters_woven[:, QUARTER:HALF, :]
+        gather(last_gated, 2, S - QUARTER, {PACK - 1: (0, C, QUARTER)})
+        weave(nc.scalar.copy, last_gated[:, :, 0:C], last_woven[:, 0:C, :])
+        multiply(2, WIDE + HALF, quarters_woven[:, 0:QUARTER, :])
+        weave(nc.vector.tensor_copy, last_gated[:, :, C:QUARTER], last_woven[:, C:QUARTER, :])
+        multiply(2, S - QUARTER, last_woven[:, 0:C, :])
+        square(S - QUARTER, C, 1)
+        multiply(2, S - C, last_woven[:, C:QUARTER, :])
+        nc.vector.tensor_scalar(y_sb[:, S - C : S], banks[E - 1][:], bias_sb[:, E - 1 : E], 0.0, ADD, MAX)
+        for cols in (slice(WIDE + HALF, S - QUARTER), slice(S - C, S)):
             nc.vector.tensor_tensor(y_sb[:, cols], y_sb[:, cols], y_sb[:, cols], MULT)
 
         picked, pair, total = (gated_sb[:, r * T : (r + 1) * T] for r in range(3))

@@ -28,13 +28,10 @@ MAX = mybir.AluOpType.max
 ACT = mybir.ActivationFunctionType
 
 CHUNK = 1024
-WIDE = 2 * CHUNK
-HALF = CHUNK // 2
-QUARTER = CHUNK // 4
-FIRST_CUTS = (0, 160, 448, CHUNK, WIDE)
-OUT_CUTS = (0, 640, 896, T)
-WOVEN_BUFS = 3
-CODE_BUFS = 6
+OWN = 768
+G1, G2, G3 = OWN, OWN + 1024, OWN + 1024 + 768
+OWN_CUT = 256
+OUT_CUTS = (0, 128, 512, 896, T)
 
 
 def tile_moe_pre_lin_relu2_kernel(
@@ -43,19 +40,20 @@ def tile_moe_pre_lin_relu2_kernel(
     nc = tc.nc
     with ExitStack() as ctx:
         keep = ctx.enter_context(tc.tile_pool(name="keep", bufs=1))
-        stage = ctx.enter_context(tc.tile_pool(name="stage", bufs=WOVEN_BUFS))
-        quant = ctx.enter_context(tc.tile_pool(name="quant", bufs=CODE_BUFS))
+        stage = ctx.enter_context(tc.tile_pool(name="stage", bufs=2))
+        weaving = ctx.enter_context(tc.tile_pool(name="weaving", bufs=3))
         psum = ctx.enter_context(tc.psum_pool(name="psum", bufs=1))
 
         offs_sb = keep.tile([P, S // LANE], U16, name="offs_sb")
         pos_sb = [keep.tile([P, T // LANE], U16, name=f"pos_sb{r}") for r in range(3)]
         gate_sb = keep.tile([P, S], F32, name="gate_sb")
         bias_sb = keep.tile([P, E], F32, name="bias_sb")
-        columns = [WIDE + PAD] * (PASSES - 1) + [T + PAD]
-        x_sb = [[keep.tile([P, columns[a]], F32, name=f"x_sb{a}_{t}") for t in range(PACK)] for a in range(PASSES)]
-        gated_sb = keep.tile([P, PACK * (CHUNK + WIDE)], F32, name="gated_sb")
+        x_sb = [[keep.tile([P, T + PAD], F32, name=f"x_sb{a}_{t}") for t in range(PACK)] for a in range(PASSES)]
+        own_sb = keep.tile([P, PACK, OWN], F32, name="own_sb")
         w_sb = keep.tile([P, E * PASSES, 2 * N], U8, name="w_sb", align_bytes=64)
         ws_sb = keep.tile([P, E * PASSES, N], U8, name="ws_sb", align_bytes=64)
+        codes = [keep.tile([P, S], U32, name=f"codes{a}", align_bytes=64) for a in range(PASSES)]
+        scales = [keep.tile([P, S], U8, name=f"scales{a}", align_bytes=64) for a in range(PASSES)]
         y_sb = keep.tile([P, S], F32, name="y_sb")
 
         x_rows = xT.rearrange("(a p t) c -> a t p c", p=P, t=PACK)
@@ -70,13 +68,14 @@ def tile_moe_pre_lin_relu2_kernel(
 
         nc.sync.dma_start(offs_sb[:], offs)
         load_x(0, 0)
-        for c0, c1 in zip(FIRST_CUTS, FIRST_CUTS[1:]):
-            load_gate(c0, c1)
+        load_gate(0, OWN_CUT)
+        load_gate(OWN_CUT, OWN)
         for t in range(1, PACK):
             load_x(0, t)
-        load_gate(WIDE, S)
+        load_gate(G1, G2)
         for i in range(PACK, PASSES * PACK):
             load_x(i // PACK, i % PACK)
+        load_gate(G2, S)
         nc.sync.dma_start(out=bias_sb[:], in_=b)
         ws_rows = w_scales.rearrange("e a (g r) n -> r g (e a) n", r=4)
         w_rows = w_words.rearrange("e a p m -> p (e a) m")
@@ -88,144 +87,155 @@ def tile_moe_pre_lin_relu2_kernel(
         for r, pos in enumerate((pos1, pos2, pos3)):
             nc.sync.dma_start(pos_sb[r][:], pos)
 
-        def gather(gated, a, s0, cuts=None):
+        def window(a, t, s0, s1):
+            return x_sb[a][t][:].indirect(offs_sb[:, s0 // LANE : s1 // LANE])
+
+        def fetch(a, s0, s1):
+            fetched = stage.tile([P, PACK, CHUNK], F32, name="fetched")
             for t in range(PACK):
-                edges = (cuts or {}).get(t, (0, gated.shape[2]))
-                for c0, c1 in zip(edges, edges[1:]):
-                    nc.vector.tensor_tensor(
-                        gated[:, t, c0:c1],
-                        x_sb[a][t][:].indirect(offs_sb[:, (s0 + c0) // LANE : (s0 + c1) // LANE]),
-                        gate_sb[:, s0 + c0 : s0 + c1],
-                        MULT,
-                    )
+                nc.scalar.activation(fetched[:, t, 0 : s1 - s0], window(a, t, s0, s1), ACT.Copy)
+            return fetched
 
-        def weave(copy, gated, grouped):
-            copy(
-                out=grouped.rearrange("p (c i) t -> p c t i", i=4),
-                in_=gated.rearrange("p t (c i) -> p c t i", i=4),
-            )
+        def fetch_own(a, t, c0=0, c1=OWN):
+            nc.vector.tensor_tensor(own_sb[:, t, c0:c1], window(a, t, c0, c1), gate_sb[:, c0:c1], MULT)
 
-        def woven(gated):
-            grouped = stage.tile([P, CHUNK, PACK], BF16, name="grouped", align_bytes=64)
-            weave(nc.scalar.copy, gated, grouped[:, 0 : gated.shape[2], :])
-            return grouped
+        def by_lines(planes):
+            return planes.rearrange("p t (c i) -> p c t i", i=4)
 
-        held = {}
+        def new_woven(w):
+            woven = weaving.tile([P, CHUNK, PACK], BF16, name="woven", align_bytes=64)
+            return woven[:, 0:w, :]
+
+        def weave_own():
+            woven = new_woven(OWN)
+            nc.vector.tensor_copy(woven.rearrange("p (c i) t -> p c t i", i=4), by_lines(own_sb[:]))
+            return woven
+
+        def scale_weave(fetched, s0, s1):
+            w = s1 - s0
+            woven = new_woven(w)
+            gates = gate_sb[:, s0:s1].rearrange("p (c o i) -> p c o i", o=1, i=4).to_broadcast([P, w // 4, PACK, 4])
+            nc.vector.tensor_tensor(woven.rearrange("p (c i) t -> p c t i", i=4), by_lines(fetched), gates, MULT)
+            return woven
+
+        def quantise(a, s0, woven):
+            w = woven.shape[1]
+            c0 = 0
+            while c0 < w:
+                n = max(m for m in (128, 256, 512, 1024) if m <= w - c0)
+                cols = slice(s0 + c0, s0 + c0 + n)
+                nc.vector.quantize_mx(
+                    out=codes[a][:, cols].bitcast(FP8X4),
+                    scales=scales[a][:, cols],
+                    in_=woven[:, c0 : c0 + n, :].rearrange("p c t -> p (c t)"),
+                )
+                c0 += n
+
         banks = {}
 
-        def matmul(e, a):
-            codes, scales, s0 = held[e, a]
-            cols = slice(e * C - s0, (e + 1) * C - s0)
-            g = e * PASSES + a
-            nc.tensor.matmul_mx(
-                out=banks[e][:],
-                lhsT=w_sb[:, g, :].bitcast(FP4X4),
-                lhsT_scale=ws_sb[:, g, :],
-                rhs=codes[:, cols].bitcast(FP8X4),
-                rhs_scale=scales[:, cols],
-                start=(a == 0),
-                stop=(a == PASSES - 1),
-            )
-
-        def begin(e, passes):
-            banks[e] = psum.tile([N, C], F32, name="bank", bufs=BANKS)
-            for a in range(passes):
-                matmul(e, a)
-
-        def multiply(a, s0, grouped):
-            w = grouped.shape[1]
-            if w > QUARTER:
-                codes = quant.tile([P, w], U32, name="codes", align_bytes=64)
-                scales = quant.tile([P, w], U8, name="scales", align_bytes=64)
-            else:
-                codes = keep.tile([P, w], U32, name=f"codes{s0}", align_bytes=64)
-                scales = keep.tile([P, w], U8, name=f"scales{s0}", align_bytes=64)
-            nc.vector.quantize_mx(
-                out=codes[:].bitcast(FP8X4), scales=scales[:], in_=grouped.rearrange("p c t -> p (c t)")
-            )
-            for e in range(s0 // C, (s0 + w) // C):
-                held[e, a] = (codes, scales, s0)
-                if a == PASSES - 1 and e not in banks:
-                    begin(e, a)
-                if e in banks:
-                    matmul(e, a)
-                if a == PASSES - 1 and e < E - 1:
-                    nc.scalar.activation(
-                        y_sb[:, e * C : (e + 1) * C], banks[e][:], ACT.Relu, bias=bias_sb[:, e : e + 1]
+        def multiply(s0, s1, passes):
+            for e in range(s0 // C, s1 // C):
+                if e not in banks:
+                    banks[e] = psum.tile([N, C], F32, name="bank", bufs=BANKS)
+                for a in passes:
+                    g = e * PASSES + a
+                    cols = slice(e * C, (e + 1) * C)
+                    nc.tensor.matmul_mx(
+                        out=banks[e][:],
+                        lhsT=w_sb[:, g, :].bitcast(FP4X4),
+                        lhsT_scale=ws_sb[:, g, :],
+                        rhs=codes[a][:, cols].bitcast(FP8X4),
+                        rhs_scale=scales[a][:, cols],
+                        start=(a == 0),
+                        stop=(a == PASSES - 1),
                     )
 
-        def square(s0, w, pieces):
-            for c0 in range(s0, s0 + w, w // pieces):
-                cols = slice(c0, c0 + w // pieces)
+        def finish(s0, s1):
+            for e in range(s0 // C, s1 // C):
+                nc.scalar.activation(y_sb[:, e * C : (e + 1) * C], banks[e][:], ACT.Relu, bias=bias_sb[:, e : e + 1])
+            h = (s0 + s1) // 2
+            for cols in (slice(s0, h), slice(h, s1)):
                 nc.scalar.activation(y_sb[:, cols], y_sb[:, cols], ACT.Square)
 
-        narrow = gated_sb[:, 0 : PACK * CHUNK].rearrange("p (t c) -> p t c", t=PACK)
-        wide = gated_sb[:, PACK * CHUNK :].rearrange("p (t c) -> p t c", t=PACK)
-        halves = [wide[:, :, 0:CHUNK], wide[:, :, CHUNK:WIDE]]
+        every = range(PASSES)
 
-        gather(wide, 0, 0, {0: FIRST_CUTS})
-        pass0 = [woven(half) for half in halves]
+        f = fetch(0, G1, G2)
+        fetch_own(0, 0, 0, OWN_CUT)
+        fetch_own(0, 0, OWN_CUT, OWN)
+        for t in range(1, PACK):
+            fetch_own(0, t)
+        own = weave_own()
+        f_next = fetch(1, G1, G2)
+        woven = scale_weave(f[:], G1, G2)
+        quantise(0, 0, own)
+        fetch_own(1, 0)
+        quantise(0, G1, woven)
+        fetch_own(1, 1)
 
-        gather(narrow, 0, WIDE)
-        pass0.append(woven(narrow))
-        multiply(0, 0, pass0[0][:])
-        multiply(0, CHUNK, pass0[1][:])
+        f, f_next = f_next, fetch(2, G1, G2)
+        woven = scale_weave(f[:], G1, G2)
+        fetch_own(1, 2)
+        quantise(1, G1, woven)
+        fetch_own(1, 3)
 
-        gather(wide, 1, 0)
-        pass1 = [woven(half) for half in halves]
-        multiply(0, WIDE, pass0[2][:])
+        f, f_next = f_next, fetch(0, G2, G3)
+        woven = scale_weave(f[:], G1, G2)
+        own = weave_own()
+        quantise(2, G1, woven)
+        multiply(G1, G2, every)
+        quantise(1, 0, own)
 
-        gather(narrow, 2, 0)
-        pass2 = [woven(narrow)]
-        multiply(1, 0, pass1[0][:])
-        multiply(1, CHUNK, pass1[1][:])
+        f, f_next = f_next, fetch(1, G2, G3)
+        finish(G1, G2)
+        woven = scale_weave(f[:, :, 0 : G3 - G2], G2, G3)
+        fetch_own(2, 0)
+        quantise(0, G2, woven)
+        fetch_own(2, 1)
 
-        gather(halves[1], 2, CHUNK)
-        pass2.append(woven(halves[1]))
-        multiply(2, 0, pass2[0][:])
-        square(0, CHUNK, 2)
+        f, f_next = f_next, fetch(2, G2, G3)
+        woven = scale_weave(f[:, :, 0 : G3 - G2], G2, G3)
+        fetch_own(2, 2)
+        quantise(1, G2, woven)
+        fetch_own(2, 3)
 
-        gather(narrow, 1, WIDE)
-        pass1.append(woven(narrow))
-        multiply(2, CHUNK, pass2[1][:])
-        square(CHUNK, CHUNK, 2)
-        for e in range(WIDE // C, E):
-            begin(e, 1)
+        f, f_next = f_next, fetch(0, G3, S)
+        woven = scale_weave(f[:, :, 0 : G3 - G2], G2, G3)
+        own = weave_own()
+        quantise(2, G2, woven)
+        multiply(G2, G3, every)
+        quantise(2, 0, own)
 
-        gather(halves[1][:, :, 0:HALF], 2, WIDE)
-        half_woven = woven(halves[1][:, :, 0:HALF])
-        multiply(1, WIDE, pass1[2][:, 0:HALF, :])
+        f, f_next = f_next, fetch(1, G3, S)
+        finish(G2, G3)
+        multiply(0, OWN, every)
+        woven = scale_weave(f[:, :, 0 : S - G3], G3, S)
+        quantise(0, G3, woven)
 
-        gather(narrow[:, :, 0:QUARTER], 2, WIDE + HALF)
-        quarters_woven = woven(narrow[:, :, 0:QUARTER])
-        multiply(1, WIDE + HALF, pass1[2][:, HALF:CHUNK, :])
-        multiply(2, WIDE, half_woven[:, 0:HALF, :])
-        square(WIDE, HALF, 2)
+        f, f_next = f_next, fetch(2, G3, S)
+        woven = scale_weave(f[:, :, 0 : S - G3], G3, S)
+        quantise(1, G3, woven)
+        finish(0, OWN)
+        multiply(G3, S, range(PASSES - 1))
 
-        last_gated = halves[1][:, :, 0:QUARTER]
-        last_woven = quarters_woven[:, QUARTER:HALF, :]
-        gather(last_gated, 2, S - QUARTER, {PACK - 1: (0, C, QUARTER)})
-        weave(nc.scalar.copy, last_gated[:, :, 0:C], last_woven[:, 0:C, :])
-        multiply(2, WIDE + HALF, quarters_woven[:, 0:QUARTER, :])
-        weave(nc.vector.tensor_copy, last_gated[:, :, C:QUARTER], last_woven[:, C:QUARTER, :])
-        multiply(2, S - QUARTER, last_woven[:, 0:C, :])
-        square(S - QUARTER, C, 1)
-        multiply(2, S - C, last_woven[:, C:QUARTER, :])
-        nc.vector.tensor_scalar(y_sb[:, S - C : S], banks[E - 1][:], bias_sb[:, E - 1 : E], 0.0, ADD, MAX)
-        for cols in (slice(WIDE + HALF, S - QUARTER), slice(S - C, S)):
-            nc.vector.tensor_tensor(y_sb[:, cols], y_sb[:, cols], y_sb[:, cols], MULT)
+        f = f_next
+        half = (S - G3) // 2
+        halves = [scale_weave(f[:, :, c0 : c0 + half], G3 + c0, G3 + c0 + half) for c0 in (0, half)]
+        for i, woven in enumerate(halves):
+            s0 = G3 + i * half
+            quantise(2, s0, woven)
+            multiply(s0, s0 + half, (PASSES - 1,))
+        finish(G3, S)
 
-        picked, pair, total = (gated_sb[:, r * T : (r + 1) * T] for r in range(3))
-        parts = (slice(0, OUT_CUTS[1]), slice(OUT_CUTS[1], T))
+        picked = stage.tile([P, PACK, CHUNK], F32, name="fetched")
 
         def results(r, cols):
             return y_sb[:].indirect(pos_sb[r][:, cols.start // LANE : cols.stop // LANE])
 
+        parts = [slice(c0, c1) for c0, c1 in zip(OUT_CUTS, OUT_CUTS[1:])]
         for cols in parts:
-            nc.vector.tensor_copy(picked[:, cols], results(0, cols))
+            nc.scalar.activation(picked[:, 0, cols], results(0, cols), ACT.Copy)
         for cols in parts:
-            nc.vector.tensor_tensor(pair[:, cols], results(1, cols), picked[:, cols], ADD)
-        for c0, c1 in zip(OUT_CUTS, OUT_CUTS[1:]):
-            cols = slice(c0, c1)
-            nc.vector.tensor_tensor(total[:, cols], results(2, cols), pair[:, cols], ADD)
-            nc.sync.dma_start(out=out[:, cols], in_=total[:, cols])
+            nc.vector.tensor_tensor(picked[:, 1, cols], results(1, cols), picked[:, 0, cols], ADD)
+        for cols in parts:
+            nc.vector.tensor_tensor(picked[:, 2, cols], results(2, cols), picked[:, 1, cols], ADD)
+            nc.sync.dma_start(out=out[:, cols], in_=picked[:, 2, cols])

@@ -64,6 +64,10 @@ def tile_moe_pre_lin_relu2_kernel(
         def load_gate(c0, c1):
             nc.sync.dma_start(out=gate_sb[:, c0:c1], in_=gate[0:P, c0:c1])
 
+        warm = keep.tile([P, 2], F32, name="warm")
+        nc.vector.memset(warm[:, 0:1], 0.0)
+        nc.scalar.activation(warm[:, 1:2], warm[:, 0:1], ACT.Copy)
+
         nc.vector.memset(ws_sb[:].rearrange("p g n -> p (g n)").bitcast(I32), 0)
 
         nc.sync.dma_start(offs_sb[:], offs)

@@ -1,6 +1,7 @@
 from contextlib import ExitStack
 
 import concourse.mybir as mybir
+from concourse.masks import make_identity
 
 K, T, E, C, N = 1536, 1024, 24, 128, 128
 S = E * C
@@ -28,10 +29,24 @@ MAX = mybir.AluOpType.max
 ACT = mybir.ActivationFunctionType
 
 CHUNK = 1024
-OWN = 768
-G1, G2, G3 = OWN, OWN + 1024, OWN + 1024 + 768
-OWN_CUT = 256
-OUT_CUTS = (0, 128, 512, 896, T)
+HALF = CHUNK // 2
+STEPS = (
+    (0, 0, CHUNK, 512, HALF),
+    (0, CHUNK, CHUNK, 384, HALF),
+    (1, 0, CHUNK, 384, HALF),
+    (2, 0, CHUNK, 352, HALF),
+    (1, CHUNK, CHUNK, 352, HALF),
+    (2, CHUNK, CHUNK, 352, HALF),
+    (0, 2 * CHUNK, CHUNK, 352, HALF),
+    (1, 2 * CHUNK, CHUNK, 352, 256),
+    (2, 2 * CHUNK, 512, 160, 0),
+    (2, 2 * CHUNK + 512, 256, 0, 0),
+    (2, 2 * CHUNK + 768, 256, 0, 0),
+)
+MAIN = 768
+FETCH_BUFS = 3
+ALONE = 192
+MID, END = 608, 896
 
 
 def tile_moe_pre_lin_relu2_kernel(
@@ -40,16 +55,18 @@ def tile_moe_pre_lin_relu2_kernel(
     nc = tc.nc
     with ExitStack() as ctx:
         keep = ctx.enter_context(tc.tile_pool(name="keep", bufs=1))
-        stage = ctx.enter_context(tc.tile_pool(name="stage", bufs=2))
-        weaving = ctx.enter_context(tc.tile_pool(name="weaving", bufs=3))
+        stage = ctx.enter_context(tc.tile_pool(name="stage", bufs=FETCH_BUFS))
         psum = ctx.enter_context(tc.psum_pool(name="psum", bufs=1))
 
         offs_sb = keep.tile([P, S // LANE], U16, name="offs_sb")
         pos_sb = [keep.tile([P, T // LANE], U16, name=f"pos_sb{r}") for r in range(3)]
-        gate_sb = keep.tile([P, S], F32, name="gate_sb")
+        gate_sb = keep.tile([P, S // CHUNK, HALF], F32, name="gate_sb")
+        gate_rows = keep.tile([P, P], F32, name="gate_rows")
+        gate_cols = keep.tile([P, S // P], F32, name="gate_cols")
+        identity = keep.tile([P, P], F32, name="identity")
         bias_sb = keep.tile([P, E], F32, name="bias_sb")
         x_sb = [[keep.tile([P, T + PAD], F32, name=f"x_sb{a}_{t}") for t in range(PACK)] for a in range(PASSES)]
-        own_sb = keep.tile([P, PACK, OWN], F32, name="own_sb")
+        woven_sb = keep.tile([P, 2 * MAIN + HALF, PACK], BF16, name="woven_sb", align_bytes=64)
         w_sb = keep.tile([P, E * PASSES, 2 * N], U8, name="w_sb", align_bytes=64)
         ws_sb = keep.tile([P, E * PASSES, N], U8, name="ws_sb", align_bytes=64)
         codes = [keep.tile([P, S], U32, name=f"codes{a}", align_bytes=64) for a in range(PASSES)]
@@ -61,8 +78,10 @@ def tile_moe_pre_lin_relu2_kernel(
         def load_x(a, t):
             nc.sync.dma_start(out=x_sb[a][t][:, 0:T], in_=x_rows[a, t])
 
-        def load_gate(c0, c1):
-            nc.sync.dma_start(out=gate_sb[:, c0:c1], in_=gate[0:P, c0:c1])
+        def load_gate(c):
+            nc.sync.dma_start(out=gate_sb[:, c, :], in_=gate[0:P, c * CHUNK + HALF : (c + 1) * CHUNK])
+
+        make_identity(nc, identity[:])
 
         warm = keep.tile([P, 2], F32, name="warm")
         nc.vector.memset(warm[:, 0:1], 0.0)
@@ -72,14 +91,14 @@ def tile_moe_pre_lin_relu2_kernel(
 
         nc.sync.dma_start(offs_sb[:], offs)
         load_x(0, 0)
-        load_gate(0, OWN_CUT)
-        load_gate(OWN_CUT, OWN)
+        nc.sync.dma_start(out=gate_rows[:], in_=gate.rearrange("k (g j) -> (k g) j", j=P)[0:P, :])
         for t in range(1, PACK):
             load_x(0, t)
-        load_gate(G1, G2)
+        load_gate(0)
+        load_gate(1)
         for i in range(PACK, PASSES * PACK):
             load_x(i // PACK, i % PACK)
-        load_gate(G2, S)
+        load_gate(2)
         nc.sync.dma_start(out=bias_sb[:], in_=b)
         ws_rows = w_scales.rearrange("e a (g r) n -> r g (e a) n", r=4)
         w_rows = w_words.rearrange("e a p m -> p (e a) m")
@@ -94,152 +113,165 @@ def tile_moe_pre_lin_relu2_kernel(
         def window(a, t, s0, s1):
             return x_sb[a][t][:].indirect(offs_sb[:, s0 // LANE : s1 // LANE])
 
-        def fetch(a, s0, s1):
-            fetched = stage.tile([P, PACK, CHUNK], F32, name="fetched")
-            for t in range(PACK):
-                nc.scalar.activation(fetched[:, t, 0 : s1 - s0], window(a, t, s0, s1), ACT.Copy)
-            return fetched
+        def scale_weave(engine, woven, planes, gates):
+            w = planes.shape[2]
+            engine.tensor_tensor(
+                woven.rearrange("p (c i) t -> p c t i", i=4),
+                planes.rearrange("p t (c i) -> p c t i", i=4),
+                gates.rearrange("p (c o i) -> p c o i", o=1, i=4).to_broadcast([P, w // 4, PACK, 4]),
+                MULT,
+            )
 
-        def fetch_own(a, t, c0=0, c1=OWN):
-            nc.vector.tensor_tensor(own_sb[:, t, c0:c1], window(a, t, c0, c1), gate_sb[:, c0:c1], MULT)
+        turned = psum.tile([P, HALF], F32, name="gates", bufs=2)
+        nc.tensor.transpose(turned[:, 0:P], gate_rows[:], identity[:])
+        gate_ps = {}
 
-        def by_lines(planes):
-            return planes.rearrange("p t (c i) -> p c t i", i=4)
-
-        def new_woven(w):
-            woven = weaving.tile([P, CHUNK, PACK], BF16, name="woven", align_bytes=64)
-            return woven[:, 0:w, :]
-
-        def weave_own():
-            woven = new_woven(OWN)
-            nc.vector.tensor_copy(woven.rearrange("p (c i) t -> p c t i", i=4), by_lines(own_sb[:]))
-            return woven
-
-        def scale_weave(fetched, s0, s1):
-            w = s1 - s0
-            woven = new_woven(w)
-            gates = gate_sb[:, s0:s1].rearrange("p (c o i) -> p c o i", o=1, i=4).to_broadcast([P, w // 4, PACK, 4])
-            nc.vector.tensor_tensor(woven.rearrange("p (c i) t -> p c t i", i=4), by_lines(fetched), gates, MULT)
-            return woven
-
-        def quantise(a, s0, woven):
-            w = woven.shape[1]
-            c0 = 0
-            while c0 < w:
-                n = max(m for m in (128, 256, 512, 1024) if m <= w - c0)
-                cols = slice(s0 + c0, s0 + c0 + n)
-                nc.vector.quantize_mx(
-                    out=codes[a][:, cols].bitcast(FP8X4),
-                    scales=scales[a][:, cols],
-                    in_=woven[:, c0 : c0 + n, :].rearrange("p c t -> p (c t)"),
+        def spread_gate(h):
+            gate_ps[h] = psum.tile([P, HALF], F32, name="gates", bufs=2)
+            for j in range(HALF // P):
+                g = h * (HALF // P) + j
+                nc.tensor.transpose(
+                    gate_ps[h][:, j * P : (j + 1) * P], gate_cols[:, g : g + 1].to_broadcast([P, P]), identity[:]
                 )
-                c0 += n
 
         banks = {}
+        opens, closes = set(), set()
 
-        def multiply(s0, s1, passes):
-            for e in range(s0 // C, s1 // C):
-                if e not in banks:
-                    banks[e] = psum.tile([N, C], F32, name="bank", bufs=BANKS)
-                for a in passes:
-                    g = e * PASSES + a
-                    cols = slice(e * C, (e + 1) * C)
-                    nc.tensor.matmul_mx(
-                        out=banks[e][:],
-                        lhsT=w_sb[:, g, :].bitcast(FP4X4),
-                        lhsT_scale=ws_sb[:, g, :],
-                        rhs=codes[a][:, cols].bitcast(FP8X4),
-                        rhs_scale=scales[a][:, cols],
-                        start=(a == 0),
-                        stop=(a == PASSES - 1),
-                    )
+        def open_banks(s0, s1, share):
+            for e0 in range(s0 // C, s1 // C, share):
+                bank = psum.tile([N, HALF], F32, name="bank", bufs=BANKS - 2)
+                for e in range(e0, min(e0 + share, s1 // C)):
+                    banks[e] = bank[:, (e - e0) * C : (e - e0 + 1) * C]
+                opens.add(e0)
+                closes.add(min(e0 + share, s1 // C) - 1)
 
-        def finish(s0, s1):
-            for e in range(s0 // C, s1 // C):
-                nc.scalar.activation(y_sb[:, e * C : (e + 1) * C], banks[e][:], ACT.Relu, bias=bias_sb[:, e : e + 1])
-            h = (s0 + s1) // 2
-            for cols in (slice(s0, h), slice(h, s1)):
-                nc.scalar.activation(y_sb[:, cols], y_sb[:, cols], ACT.Square)
+        def multiply(a, e, c0):
+            g = e * PASSES + a
+            nc.tensor.matmul_mx(
+                out=banks[e],
+                lhsT=w_sb[:, g, :].bitcast(FP4X4),
+                lhsT_scale=ws_sb[:, g, :],
+                rhs=codes[a][:, c0 : c0 + C].bitcast(FP8X4),
+                rhs_scale=scales[a][:, c0 : c0 + C],
+                start=(a == 0 and e in opens),
+                stop=(a == PASSES - 1 and e in closes),
+            )
 
-        every = range(PASSES)
+        fetched = {}
 
-        f = fetch(0, G1, G2)
-        fetch_own(0, 0, 0, OWN_CUT)
-        fetch_own(0, 0, OWN_CUT, OWN)
-        for t in range(1, PACK):
-            fetch_own(0, t)
-        own = weave_own()
-        f_next = fetch(1, G1, G2)
-        woven = scale_weave(f[:], G1, G2)
-        quantise(0, 0, own)
-        fetch_own(1, 0)
-        quantise(0, G1, woven)
-        fetch_own(1, 1)
+        def fetch(k):
+            a, s0, n, g, p = STEPS[k]
+            room = stage.tile([P, PACK * CHUNK], F32, name="fetched")
+            fetched[k] = room[:, 0 : PACK * n].rearrange("p (t c) -> p t c", t=PACK)
+            for t in range(PACK):
+                nc.scalar.activation(fetched[k][:, t, 0 : n - g], window(a, t, s0, s0 + n - g), ACT.Copy)
 
-        f, f_next = f_next, fetch(2, G1, G2)
-        woven = scale_weave(f[:], G1, G2)
-        fetch_own(1, 2)
-        quantise(1, G1, woven)
-        fetch_own(1, 3)
+        def fetch_vector(k):
+            a, s0, n, g, p = STEPS[k]
+            for t in range(PACK if g else 0):
+                nc.vector.tensor_copy(fetched[k][:, t, n - g : n], window(a, t, s0 + n - g, s0 + n))
 
-        f, f_next = f_next, fetch(0, G2, G3)
-        woven = scale_weave(f[:], G1, G2)
-        own = weave_own()
-        quantise(2, G1, woven)
-        multiply(G1, G2, every)
-        quantise(1, 0, own)
+        def places(k):
+            a, s0, n, g, p = STEPS[k]
+            return (MAIN - (n - p), MAIN) if k % 2 == 0 else (MAIN + HALF, MAIN + HALF - p)
 
-        f, f_next = f_next, fetch(1, G2, G3)
-        finish(G1, G2)
-        woven = scale_weave(f[:, :, 0 : G3 - G2], G2, G3)
-        fetch_own(2, 0)
-        quantise(0, G2, woven)
-        fetch_own(2, 1)
+        def weave_main(k):
+            a, s0, n, g, p = STEPS[k]
+            w0 = places(k)[0]
+            for c0 in range(0, n - p, HALF):
+                c1 = min(c0 + HALF, n - p)
+                h, at = divmod(s0 + c0, HALF)
+                scale_weave(nc.vector, woven_sb[:, w0 + c0 : w0 + c1, :], fetched[k][:, :, c0:c1], gate_ps[h][:, at : at + c1 - c0])
 
-        f, f_next = f_next, fetch(2, G2, G3)
-        woven = scale_weave(f[:, :, 0 : G3 - G2], G2, G3)
-        fetch_own(2, 2)
-        quantise(1, G2, woven)
-        fetch_own(2, 3)
+        def weave_side(k):
+            a, s0, n, g, p = STEPS[k]
+            if p:
+                w0 = places(k)[1]
+                scale_weave(nc.gpsimd, woven_sb[:, w0 : w0 + p, :], fetched[k][:, :, n - p : n], gate_sb[:, s0 // CHUNK, HALF - p : HALF])
 
-        f, f_next = f_next, fetch(0, G3, S)
-        woven = scale_weave(f[:, :, 0 : G3 - G2], G2, G3)
-        own = weave_own()
-        quantise(2, G2, woven)
-        multiply(G2, G3, every)
-        quantise(2, 0, own)
+        def quantise(k):
+            a, s0, n, g, p = STEPS[k]
+            w0 = min(places(k))
+            if p == 0:
+                w0 = places(k)[0]
+            nc.vector.quantize_mx(
+                out=codes[a][:, s0 : s0 + n].bitcast(FP8X4),
+                scales=scales[a][:, s0 : s0 + n],
+                in_=woven_sb[:, w0 : w0 + n, :].rearrange("p c t -> p (c t)"),
+            )
+            turn = p if k % 2 else 0
+            for e in range(s0 // C, (s0 + n) // C):
+                multiply(a, e, s0 + (e * C - s0 + turn) % n)
 
-        f, f_next = f_next, fetch(1, G3, S)
-        finish(G2, G3)
-        multiply(0, OWN, every)
-        woven = scale_weave(f[:, :, 0 : S - G3], G3, S)
-        quantise(0, G3, woven)
+        def epilogue(k):
+            a, s0, n, g, p = STEPS[k]
+            if a == PASSES - 1:
+                for e in range(s0 // C, (s0 + n) // C):
+                    nc.scalar.activation(y_sb[:, e * C : (e + 1) * C], banks[e], ACT.Relu, bias=bias_sb[:, e : e + 1])
+                for c0 in (s0, s0 + n // 2):
+                    cols = slice(c0, c0 + n // 2)
+                    nc.scalar.activation(y_sb[:, cols], y_sb[:, cols], ACT.Square)
 
-        f, f_next = f_next, fetch(2, G3, S)
-        woven = scale_weave(f[:, :, 0 : S - G3], G3, S)
-        quantise(1, G3, woven)
-        finish(0, OWN)
-        multiply(G3, S, range(PASSES - 1))
-
-        f = f_next
-        half = (S - G3) // 2
-        halves = [scale_weave(f[:, :, c0 : c0 + half], G3 + c0, G3 + c0 + half) for c0 in (0, half)]
-        for i, woven in enumerate(halves):
-            s0 = G3 + i * half
-            quantise(2, s0, woven)
-            multiply(s0, s0 + half, (PASSES - 1,))
-        finish(G3, S)
+        last = len(STEPS) - 1
+        open_banks(0, 2 * CHUNK, 4)
+        fetch(0)
+        fetch_vector(0)
+        nc.vector.tensor_copy(gate_cols[:], turned[:, 0 : S // P])
+        spread_gate(0)
+        spread_gate(2)
+        fetch(1)
+        weave_main(0)
+        weave_side(0)
+        fetch_vector(1)
+        for k in range(1, last + 1):
+            if k < last:
+                fetch(k + 1)
+            if k > 2:
+                epilogue(k - 3)
+            if k == 6:
+                spread_gate(4)
+                open_banks(2 * CHUNK, S - 4 * C, 4)
+                open_banks(S - 4 * C, S - 2 * C, 2)
+                open_banks(S - 2 * C, S, 1)
+            if k == 7:
+                spread_gate(5)
+            weave_main(k)
+            if k < last:
+                fetch_vector(k + 1)
+            quantise(k - 1)
+            weave_side(k)
+        epilogue(last - 2)
+        quantise(last)
+        epilogue(last - 1)
+        epilogue(last)
 
         picked = stage.tile([P, PACK, CHUNK], F32, name="fetched")
+        first, second, pair, total = (picked[:, r, :] for r in range(PACK))
 
-        def results(r, cols):
-            return y_sb[:].indirect(pos_sb[r][:, cols.start // LANE : cols.stop // LANE])
+        def results(r, c0, c1):
+            return y_sb[:].indirect(pos_sb[r][:, c0 // LANE : c1 // LANE])
 
-        parts = [slice(c0, c1) for c0, c1 in zip(OUT_CUTS, OUT_CUTS[1:])]
-        for cols in parts:
-            nc.scalar.activation(picked[:, 0, cols], results(0, cols), ACT.Copy)
-        for cols in parts:
-            nc.vector.tensor_tensor(picked[:, 1, cols], results(1, cols), picked[:, 0, cols], ADD)
-        for cols in parts:
-            nc.vector.tensor_tensor(picked[:, 2, cols], results(2, cols), picked[:, 1, cols], ADD)
-            nc.sync.dma_start(out=out[:, cols], in_=picked[:, 2, cols])
+        def pick(into, r, c0, c1):
+            nc.scalar.activation(into[:, c0:c1], results(r, c0, c1), ACT.Copy)
+
+        def pick_add(into, r, other, c0, c1):
+            nc.vector.tensor_tensor(into[:, c0:c1], results(r, c0, c1), other[:, c0:c1], ADD)
+
+        def add_store(c0, c1, stored):
+            nc.vector.tensor_tensor(total[:, c0:c1], pair[:, c0:c1], second[:, c0:c1], ADD)
+            nc.sync.dma_start(out=out[:, stored:c1], in_=total[:, stored:c1])
+
+        pick(first, 0, ALONE, MID)
+        pick(second, 1, ALONE, MID)
+        pick(first, 0, MID, T)
+        pick(second, 1, MID, END)
+        pick(second, 1, END, T)
+        nc.vector.tensor_copy(first[:, 0:ALONE], results(0, 0, ALONE))
+        pick_add(pair, 1, first, 0, ALONE)
+        pick_add(pair, 2, first, ALONE, MID)
+        pick_add(total, 2, pair, 0, ALONE)
+        add_store(ALONE, MID, 0)
+        pick_add(pair, 2, first, MID, END)
+        pick_add(pair, 2, first, END, T)
+        add_store(MID, END, MID)
+        add_store(END, T, END)

@@ -1,7 +1,6 @@
 from contextlib import ExitStack
 
 import concourse.mybir as mybir
-from concourse.masks import make_identity
 
 K, T, E, C, N = 1536, 1024, 24, 128, 128
 S = E * C
@@ -31,21 +30,24 @@ ACT = mybir.ActivationFunctionType
 CHUNK = 1024
 HALF = CHUNK // 2
 STEPS = (
-    (0, 0, CHUNK, 512, HALF),
-    (0, CHUNK, CHUNK, 384, HALF),
-    (1, 0, CHUNK, 384, HALF),
-    (2, 0, CHUNK, 352, HALF),
-    (1, CHUNK, CHUNK, 352, HALF),
-    (2, CHUNK, CHUNK, 352, HALF),
-    (0, 2 * CHUNK, CHUNK, 352, HALF),
-    (1, 2 * CHUNK, CHUNK, 352, 256),
-    (2, 2 * CHUNK, 512, 160, 0),
+    (0, 0, CHUNK, 416, 512),
+    (0, CHUNK, CHUNK, 512, 512),
+    (1, 0, CHUNK, 384, 512),
+    (1, CHUNK, CHUNK, 384, 512),
+    (2, 0, CHUNK, 384, 512),
+    (2, CHUNK, CHUNK, 384, 512),
+    (0, 2 * CHUNK, CHUNK, 384, 512),
+    (1, 2 * CHUNK, CHUNK, 192, 192),
+    (2, 2 * CHUNK, 512, 0, 0),
     (2, 2 * CHUNK + 512, 256, 0, 0),
-    (2, 2 * CHUNK + 768, 256, 0, 0),
+    (2, 2 * CHUNK + 768, 128, 0, 0),
+    (2, 2 * CHUNK + 896, 128, 0, 0),
 )
-MAIN = 768
+MAIN = 1024
 FETCH_BUFS = 3
+SIDE_BUFS = 2
 ALONE = 192
+EARLY = 256
 MID, END = 608, 896
 
 
@@ -60,13 +62,13 @@ def tile_moe_pre_lin_relu2_kernel(
 
         offs_sb = keep.tile([P, S // LANE], U16, name="offs_sb")
         pos_sb = [keep.tile([P, T // LANE], U16, name=f"pos_sb{r}") for r in range(3)]
-        gate_sb = keep.tile([P, S // CHUNK, HALF], F32, name="gate_sb")
+        gate_sb = [keep.tile([P, HALF], F32, name=f"gate_sb{c}") for c in range(S // CHUNK)]
         gate_rows = keep.tile([P, P], F32, name="gate_rows")
         gate_cols = keep.tile([P, S // P], F32, name="gate_cols")
         identity = keep.tile([P, P], F32, name="identity")
         bias_sb = keep.tile([P, E], F32, name="bias_sb")
         x_sb = [[keep.tile([P, T + PAD], F32, name=f"x_sb{a}_{t}") for t in range(PACK)] for a in range(PASSES)]
-        woven_sb = keep.tile([P, 2 * MAIN + HALF, PACK], BF16, name="woven_sb", align_bytes=64)
+        woven_sb = keep.tile([P, 2 * CHUNK + 384, PACK], BF16, name="woven_sb", align_bytes=64)
         w_sb = keep.tile([P, E * PASSES, 2 * N], U8, name="w_sb", align_bytes=64)
         ws_sb = keep.tile([P, E * PASSES, N], U8, name="ws_sb", align_bytes=64)
         codes = [keep.tile([P, S], U32, name=f"codes{a}", align_bytes=64) for a in range(PASSES)]
@@ -78,14 +80,30 @@ def tile_moe_pre_lin_relu2_kernel(
         def load_x(a, t):
             nc.sync.dma_start(out=x_sb[a][t][:, 0:T], in_=x_rows[a, t])
 
-        def load_gate(c):
-            nc.sync.dma_start(out=gate_sb[:, c, :], in_=gate[0:P, c * CHUNK + HALF : (c + 1) * CHUNK])
+        gate_last = keep.tile([P, STEPS[7][4]], F32, name="gate_last")
 
-        make_identity(nc, identity[:])
+        def side_gate(c, c0, c1):
+            if c == 2 and c0 < HALF:
+                return gate_last[:, c0:c1]
+            at = 0 if c == 1 else HALF
+            return gate_sb[c][:, c0 - at : c1 - at]
+
+        def load_gate(c, c0, c1):
+            nc.sync.dma_start(out=side_gate(c, c0, c1), in_=gate[0:P, c * CHUNK + c0 : c * CHUNK + c1])
 
         warm = keep.tile([P, 2], F32, name="warm")
         nc.vector.memset(warm[:, 0:1], 0.0)
         nc.scalar.activation(warm[:, 1:2], warm[:, 0:1], ACT.Copy)
+
+        ones = keep.tile([P, P], F32, name="ones", align_bytes=64)
+        column = keep.tile([P, P], F32, name="column", align_bytes=64)
+        across = keep.tile([P, P], F32, name="across", align_bytes=64)
+        nc.vector.memset(ones[:], 1.0)
+        nc.vector.memset(identity[:], 0.0)
+        nc.vector.tensor_tensor_scan(column[:], ones[:], ones[:], 0.0, MULT, ADD)
+        nc.vector.transpose(across[:], column[:])
+        for q in range(0, P, 32):
+            nc.vector.tensor_tensor(identity[q : q + 32, q : q + 32], across[q : q + 32, q : q + 32], column[q : q + 32, q : q + 32], mybir.AluOpType.is_equal)
 
         nc.vector.memset(ws_sb[:].rearrange("p g n -> p (g n)").bitcast(I32), 0)
 
@@ -94,11 +112,15 @@ def tile_moe_pre_lin_relu2_kernel(
         nc.sync.dma_start(out=gate_rows[:], in_=gate.rearrange("k (g j) -> (k g) j", j=P)[0:P, :])
         for t in range(1, PACK):
             load_x(0, t)
-        load_gate(0)
-        load_gate(1)
-        for i in range(PACK, PASSES * PACK):
-            load_x(i // PACK, i % PACK)
-        load_gate(2)
+        load_gate(0, CHUNK - EARLY, CHUNK)
+        for t in range(PACK):
+            load_x(1, t)
+        load_gate(0, HALF, CHUNK - EARLY)
+        load_gate(1, 0, HALF)
+        for t in range(PACK):
+            load_x(2, t)
+        load_gate(2, HALF, CHUNK)
+        load_gate(2, 0, STEPS[7][4])
         nc.sync.dma_start(out=bias_sb[:], in_=b)
         ws_rows = w_scales.rearrange("e a (g r) n -> r g (e a) n", r=4)
         w_rows = w_words.rearrange("e a p m -> p (e a) m")
@@ -157,60 +179,75 @@ def tile_moe_pre_lin_relu2_kernel(
                 stop=(a == PASSES - 1 and e in closes),
             )
 
-        fetched = {}
+        main, side, rooms = {}, {}, []
 
         def fetch(k):
             a, s0, n, g, p = STEPS[k]
-            room = stage.tile([P, PACK * CHUNK], F32, name="fetched")
-            fetched[k] = room[:, 0 : PACK * n].rearrange("p (t c) -> p t c", t=PACK)
+            if s0 % CHUNK == 0:
+                rooms.append(stage.tile([P, PACK * MAIN], F32, name="main"))
+            at = max(0, s0 % CHUNK - STEPS[8][3])
+            main[k] = rooms[-1][:, PACK * at : PACK * (at + n - g)].rearrange("p (t c) -> p t c", t=PACK)
+            m0 = s0 + (g if k % 2 else 0)
             for t in range(PACK):
-                nc.scalar.activation(fetched[k][:, t, 0 : n - g], window(a, t, s0, s0 + n - g), ACT.Copy)
+                nc.scalar.activation(main[k][:, t, :], window(a, t, m0, m0 + n - g), ACT.Copy)
 
         def fetch_vector(k):
             a, s0, n, g, p = STEPS[k]
+            if g:
+                side[k] = stage.tile([P, PACK, HALF], F32, name="side", bufs=SIDE_BUFS)
+            g0 = s0 + (0 if k % 2 else n - g)
             for t in range(PACK if g else 0):
-                nc.vector.tensor_copy(fetched[k][:, t, n - g : n], window(a, t, s0 + n - g, s0 + n))
+                nc.vector.tensor_copy(side[k][:, t, 0:g], window(a, t, g0, g0 + g))
 
-        def places(k):
+        def start(k):
             a, s0, n, g, p = STEPS[k]
-            return (MAIN - (n - p), MAIN) if k % 2 == 0 else (MAIN + HALF, MAIN + HALF - p)
+            if k % 2 == 0:
+                return CHUNK - (n - p)
+            return CHUNK + max(0, STEPS[k - 1][4] - p)
 
         def weave_main(k):
             a, s0, n, g, p = STEPS[k]
-            w0 = places(k)[0]
-            for c0 in range(0, n - p, HALF):
-                c1 = min(c0 + HALF, n - p)
-                h, at = divmod(s0 + c0, HALF)
-                scale_weave(nc.vector, woven_sb[:, w0 + c0 : w0 + c1, :], fetched[k][:, :, c0:c1], gate_ps[h][:, at : at + c1 - c0])
+            woven = woven_sb[:, start(k) : start(k) + n, :]
+            m0 = g if k % 2 else 0
+            c0, c1 = (p, n) if k % 2 else (0, n - p)
+            for b0, b1 in ((c0, min(c1, HALF)), (max(c0, HALF), c1)):
+                if b0 < b1:
+                    h, at = divmod(s0 + b0, HALF)
+                    gates = gate_ps[h][:, at : at + b1 - b0]
+                    scale_weave(nc.vector, woven[:, b0:b1, :], main[k][:, :, b0 - m0 : b1 - m0], gates)
 
         def weave_side(k):
             a, s0, n, g, p = STEPS[k]
+            chunk = s0 // CHUNK
+            woven = woven_sb[:, start(k) : start(k) + n, :]
+            g0 = 0 if k % 2 else n - g
+            early = EARLY if k == 0 else 0
+            if early:
+                scale_weave(nc.gpsimd, woven[:, n - early : n, :], side[k][:, :, g - early : g], side_gate(chunk, n - early, n))
+            if p > g:
+                c0, m0 = (g, 0) if k % 2 else (n - p, n - p)
+                scale_weave(nc.gpsimd, woven[:, c0 : c0 + p - g, :], main[k][:, :, m0 : m0 + p - g], side_gate(chunk, c0, c0 + p - g))
             if p:
-                w0 = places(k)[1]
-                scale_weave(nc.gpsimd, woven_sb[:, w0 : w0 + p, :], fetched[k][:, :, n - p : n], gate_sb[:, s0 // CHUNK, HALF - p : HALF])
+                w = g - early
+                scale_weave(nc.gpsimd, woven[:, g0 : g0 + w, :], side[k][:, :, 0:w], side_gate(chunk, g0, g0 + w))
 
         def quantise(k):
             a, s0, n, g, p = STEPS[k]
-            w0 = min(places(k))
-            if p == 0:
-                w0 = places(k)[0]
             nc.vector.quantize_mx(
                 out=codes[a][:, s0 : s0 + n].bitcast(FP8X4),
                 scales=scales[a][:, s0 : s0 + n],
-                in_=woven_sb[:, w0 : w0 + n, :].rearrange("p c t -> p (c t)"),
+                in_=woven_sb[:, start(k) : start(k) + n, :].rearrange("p c t -> p (c t)"),
             )
-            turn = p if k % 2 else 0
             for e in range(s0 // C, (s0 + n) // C):
-                multiply(a, e, s0 + (e * C - s0 + turn) % n)
+                multiply(a, e, e * C)
 
-        def epilogue(k):
-            a, s0, n, g, p = STEPS[k]
-            if a == PASSES - 1:
-                for e in range(s0 // C, (s0 + n) // C):
-                    nc.scalar.activation(y_sb[:, e * C : (e + 1) * C], banks[e], ACT.Relu, bias=bias_sb[:, e : e + 1])
-                for c0 in (s0, s0 + n // 2):
-                    cols = slice(c0, c0 + n // 2)
-                    nc.scalar.activation(y_sb[:, cols], y_sb[:, cols], ACT.Square)
+        def relu(s0, s1):
+            for e in range(s0 // C, s1 // C):
+                nc.scalar.activation(y_sb[:, e * C : (e + 1) * C], banks[e], ACT.Relu, bias=bias_sb[:, e : e + 1])
+
+        def square(s0, s1):
+            for c0 in range(s0, s1, HALF):
+                nc.scalar.activation(y_sb[:, c0 : c0 + HALF], y_sb[:, c0 : c0 + HALF], ACT.Square)
 
         last = len(STEPS) - 1
         open_banks(0, 2 * CHUNK, 4)
@@ -218,34 +255,39 @@ def tile_moe_pre_lin_relu2_kernel(
         fetch_vector(0)
         nc.vector.tensor_copy(gate_cols[:], turned[:, 0 : S // P])
         spread_gate(0)
-        spread_gate(2)
-        fetch(1)
-        weave_main(0)
-        weave_side(0)
-        fetch_vector(1)
-        for k in range(1, last + 1):
+        spread_gate(3)
+        for k in range(last + 1):
             if k < last:
                 fetch(k + 1)
-            if k > 2:
-                epilogue(k - 3)
-            if k == 6:
-                spread_gate(4)
+            if k in (5, 6):
+                spread_gate(k - 1)
+            if k in (6, 7):
+                relu((k - 6) * CHUNK, (k - 5) * CHUNK)
+                square((k - 6) * CHUNK, (k - 5) * CHUNK)
+            if k == 7:
                 open_banks(2 * CHUNK, S - 4 * C, 4)
                 open_banks(S - 4 * C, S - 2 * C, 2)
                 open_banks(S - 2 * C, S, 1)
-            if k == 7:
-                spread_gate(5)
             weave_main(k)
+            if k > 0:
+                quantise(k - 1)
+            weave_side(k)
             if k < last:
                 fetch_vector(k + 1)
-            quantise(k - 1)
-            weave_side(k)
-        epilogue(last - 2)
         quantise(last)
-        epilogue(last - 1)
-        epilogue(last)
+        relu(2 * CHUNK, S - 2 * C)
+        square(2 * CHUNK, 2 * CHUNK + HALF)
+        relu(S - 2 * C, S - C)
+        nc.scalar.activation(y_sb[:, S - 2 * C : S - C], y_sb[:, S - 2 * C : S - C], ACT.Square)
 
-        picked = stage.tile([P, PACK, CHUNK], F32, name="fetched")
+        def square_vector(s0, s1):
+            nc.vector.tensor_tensor(y_sb[:, s0:s1], y_sb[:, s0:s1], y_sb[:, s0:s1], MULT)
+
+        square_vector(S - 4 * C, S - 2 * C)
+        nc.vector.tensor_scalar(y_sb[:, S - C : S], banks[E - 1], bias_sb[:, E - 1 : E], 0.0, ADD, MAX)
+        square_vector(S - C, S)
+
+        picked = stage.tile([P, PACK, CHUNK], F32, name="main")
         first, second, pair, total = (picked[:, r, :] for r in range(PACK))
 
         def results(r, c0, c1):

@@ -29,14 +29,15 @@ ACT = mybir.ActivationFunctionType
 
 CHUNK = 1024
 HALF = CHUNK // 2
+SHARE = 576
 STEPS = (
-    (0, 0, CHUNK, 416, 512),
-    (0, CHUNK, CHUNK, 512, 512),
-    (1, 0, CHUNK, 384, 512),
-    (1, CHUNK, CHUNK, 384, 512),
-    (2, 0, CHUNK, 384, 512),
-    (2, CHUNK, CHUNK, 384, 512),
-    (0, 2 * CHUNK, CHUNK, 384, 512),
+    (0, 0, CHUNK, 416, SHARE),
+    (0, CHUNK, CHUNK, 512, SHARE),
+    (1, 0, CHUNK, 384, SHARE),
+    (1, CHUNK, CHUNK, 384, SHARE),
+    (2, 0, CHUNK, 384, SHARE),
+    (2, CHUNK, CHUNK, 384, SHARE),
+    (0, 2 * CHUNK, CHUNK, 384, SHARE),
     (1, 2 * CHUNK, CHUNK, 192, 192),
     (2, 2 * CHUNK, 512, 0, 0),
     (2, 2 * CHUNK + 512, 256, 0, 0),
@@ -62,7 +63,7 @@ def tile_moe_pre_lin_relu2_kernel(
 
         offs_sb = keep.tile([P, S // LANE], U16, name="offs_sb")
         pos_sb = [keep.tile([P, T // LANE], U16, name=f"pos_sb{r}") for r in range(3)]
-        gate_sb = [keep.tile([P, HALF], F32, name=f"gate_sb{c}") for c in range(S // CHUNK)]
+        gate_sb = [keep.tile([P, SHARE], F32, name=f"gate_sb{c}") for c in range(S // CHUNK)]
         gate_rows = keep.tile([P, P], F32, name="gate_rows")
         gate_cols = keep.tile([P, S // P], F32, name="gate_cols")
         identity = keep.tile([P, P], F32, name="identity")
@@ -83,9 +84,9 @@ def tile_moe_pre_lin_relu2_kernel(
         gate_last = keep.tile([P, STEPS[7][4]], F32, name="gate_last")
 
         def side_gate(c, c0, c1):
-            if c == 2 and c0 < HALF:
+            if c == 2 and c0 < STEPS[7][4]:
                 return gate_last[:, c0:c1]
-            at = 0 if c == 1 else HALF
+            at = 0 if c == 1 else CHUNK - SHARE
             return gate_sb[c][:, c0 - at : c1 - at]
 
         def load_gate(c, c0, c1):
@@ -115,11 +116,11 @@ def tile_moe_pre_lin_relu2_kernel(
         load_gate(0, CHUNK - EARLY, CHUNK)
         for t in range(PACK):
             load_x(1, t)
-        load_gate(0, HALF, CHUNK - EARLY)
-        load_gate(1, 0, HALF)
+        load_gate(0, CHUNK - SHARE, CHUNK - EARLY)
+        load_gate(1, 0, SHARE)
         for t in range(PACK):
             load_x(2, t)
-        load_gate(2, HALF, CHUNK)
+        load_gate(2, CHUNK - SHARE, CHUNK)
         load_gate(2, 0, STEPS[7][4])
         nc.sync.dma_start(out=bias_sb[:], in_=b)
         ws_rows = w_scales.rearrange("e a (g r) n -> r g (e a) n", r=4)

@@ -29,27 +29,42 @@ ACT = mybir.ActivationFunctionType
 
 CHUNK = 1024
 HALF = CHUNK // 2
-SHARE = 576
+SHARE = 544
+PICK = 352
 STEPS = (
-    (0, 0, CHUNK, 416, SHARE),
-    (0, CHUNK, CHUNK, 512, SHARE),
-    (1, 0, CHUNK, 384, SHARE),
-    (1, CHUNK, CHUNK, 384, SHARE),
-    (2, 0, CHUNK, 384, SHARE),
-    (2, CHUNK, CHUNK, 384, SHARE),
-    (0, 2 * CHUNK, CHUNK, 384, SHARE),
-    (1, 2 * CHUNK, CHUNK, 192, 192),
-    (2, 2 * CHUNK, 512, 0, 0),
+    (0, 0, CHUNK, 512, 768),
+    (1, 0, CHUNK, 480, SHARE),
+    (0, CHUNK, CHUNK, PICK, SHARE),
+    (1, CHUNK, CHUNK, PICK, SHARE),
+    (2, CHUNK, CHUNK, PICK, SHARE),
+    (2, 0, CHUNK, PICK, SHARE),
+    (0, 2 * CHUNK, CHUNK, PICK, 576),
+    (1, 2 * CHUNK, CHUNK, 288, 288),
+    (2, 2 * CHUNK, 512, 160, 160),
     (2, 2 * CHUNK + 512, 256, 0, 0),
     (2, 2 * CHUNK + 768, 128, 0, 0),
     (2, 2 * CHUNK + 896, 128, 0, 0),
 )
-MAIN = 1024
 FETCH_BUFS = 3
 SIDE_BUFS = 2
+EARLY = (272, 720)
+SPREADS = {1: 2, 2: 3, 4: 1, 5: 4, 6: 5}
+FINISH = {6: CHUNK, 10: 0}
 ALONE = 192
-EARLY = 256
 MID, END = 608, 896
+
+
+def woven_starts():
+    starts = [0]
+    for k in range(1, len(STEPS)):
+        n, p = STEPS[k][2], STEPS[k][4]
+        end = starts[-1] + STEPS[k - 1][2]
+        starts.append(end - p if k % 2 or not p else starts[-1] - (n - p))
+    return starts
+
+
+STARTS = woven_starts()
+WOVEN = max(at + step[2] for at, step in zip(STARTS, STEPS))
 
 
 def tile_moe_pre_lin_relu2_kernel(
@@ -58,18 +73,18 @@ def tile_moe_pre_lin_relu2_kernel(
     nc = tc.nc
     with ExitStack() as ctx:
         keep = ctx.enter_context(tc.tile_pool(name="keep", bufs=1))
-        stage = ctx.enter_context(tc.tile_pool(name="stage", bufs=FETCH_BUFS))
+        stage = ctx.enter_context(tc.tile_pool(name="stage", bufs=SIDE_BUFS))
         psum = ctx.enter_context(tc.psum_pool(name="psum", bufs=1))
 
         offs_sb = keep.tile([P, S // LANE], U16, name="offs_sb")
         pos_sb = [keep.tile([P, T // LANE], U16, name=f"pos_sb{r}") for r in range(3)]
-        gate_sb = [keep.tile([P, SHARE], F32, name=f"gate_sb{c}") for c in range(S // CHUNK)]
+        gate_sb = keep.tile([P, S], F32, name="gate_sb")
         gate_rows = keep.tile([P, P], F32, name="gate_rows")
         gate_cols = keep.tile([P, S // P], F32, name="gate_cols")
         identity = keep.tile([P, P], F32, name="identity")
         bias_sb = keep.tile([P, E], F32, name="bias_sb")
         x_sb = [[keep.tile([P, T + PAD], F32, name=f"x_sb{a}_{t}") for t in range(PACK)] for a in range(PASSES)]
-        woven_sb = keep.tile([P, 2 * CHUNK + 384, PACK], BF16, name="woven_sb", align_bytes=64)
+        woven_sb = keep.tile([P, WOVEN, PACK], BF16, name="woven_sb", align_bytes=64)
         w_sb = keep.tile([P, E * PASSES, 2 * N], U8, name="w_sb", align_bytes=64)
         ws_sb = keep.tile([P, E * PASSES, N], U8, name="ws_sb", align_bytes=64)
         codes = [keep.tile([P, S], U32, name=f"codes{a}", align_bytes=64) for a in range(PASSES)]
@@ -81,16 +96,8 @@ def tile_moe_pre_lin_relu2_kernel(
         def load_x(a, t):
             nc.sync.dma_start(out=x_sb[a][t][:, 0:T], in_=x_rows[a, t])
 
-        gate_last = keep.tile([P, STEPS[7][4]], F32, name="gate_last")
-
-        def side_gate(c, c0, c1):
-            if c == 2 and c0 < STEPS[7][4]:
-                return gate_last[:, c0:c1]
-            at = 0 if c == 1 else CHUNK - SHARE
-            return gate_sb[c][:, c0 - at : c1 - at]
-
-        def load_gate(c, c0, c1):
-            nc.sync.dma_start(out=side_gate(c, c0, c1), in_=gate[0:P, c * CHUNK + c0 : c * CHUNK + c1])
+        def load_gate(s0, s1):
+            nc.sync.dma_start(out=gate_sb[:, s0:s1], in_=gate[0:P, s0:s1])
 
         warm = keep.tile([P, 2], F32, name="warm")
         nc.vector.memset(warm[:, 0:1], 0.0)
@@ -113,15 +120,15 @@ def tile_moe_pre_lin_relu2_kernel(
         nc.sync.dma_start(out=gate_rows[:], in_=gate.rearrange("k (g j) -> (k g) j", j=P)[0:P, :])
         for t in range(1, PACK):
             load_x(0, t)
-        load_gate(0, CHUNK - EARLY, CHUNK)
+        load_gate(*EARLY)
         for t in range(PACK):
             load_x(1, t)
-        load_gate(0, CHUNK - SHARE, CHUNK - EARLY)
-        load_gate(1, 0, SHARE)
+        load_gate(0, EARLY[0])
+        gate_late = stage.tile([P, CHUNK - EARLY[1]], F32, name="side")
+        nc.sync.dma_start(out=gate_late[:], in_=gate[0:P, EARLY[1] : CHUNK])
         for t in range(PACK):
             load_x(2, t)
-        load_gate(2, CHUNK - SHARE, CHUNK)
-        load_gate(2, 0, STEPS[7][4])
+        load_gate(CHUNK, 2 * CHUNK)
         nc.sync.dma_start(out=bias_sb[:], in_=b)
         ws_rows = w_scales.rearrange("e a (g r) n -> r g (e a) n", r=4)
         w_rows = w_words.rearrange("e a p m -> p (e a) m")
@@ -130,6 +137,8 @@ def tile_moe_pre_lin_relu2_kernel(
             for r in range(4):
                 nc.sync.dma_start(out=ws_sb[r:P:32, groups, :].bitcast(I32), in_=ws_rows[r, :, groups].bitcast(I32))
             nc.sync.dma_start(out=w_sb[:, groups, :].bitcast(I32), in_=w_rows[:, groups, :].bitcast(I32))
+        load_gate(2 * CHUNK, 2 * CHUNK + STEPS[7][4])
+        load_gate(2 * CHUNK + HALF - STEPS[8][4], S)
         for r, pos in enumerate((pos1, pos2, pos3)):
             nc.sync.dma_start(pos_sb[r][:], pos)
 
@@ -149,9 +158,9 @@ def tile_moe_pre_lin_relu2_kernel(
         nc.tensor.transpose(turned[:, 0:P], gate_rows[:], identity[:])
         gate_ps = {}
 
-        def spread_gate(h):
+        def spread_gate(h, groups=HALF // P):
             gate_ps[h] = psum.tile([P, HALF], F32, name="gates", bufs=2)
-            for j in range(HALF // P):
+            for j in range(groups):
                 g = h * (HALF // P) + j
                 nc.tensor.transpose(
                     gate_ps[h][:, j * P : (j + 1) * P], gate_cols[:, g : g + 1].to_broadcast([P, P]), identity[:]
@@ -185,7 +194,7 @@ def tile_moe_pre_lin_relu2_kernel(
         def fetch(k):
             a, s0, n, g, p = STEPS[k]
             if s0 % CHUNK == 0:
-                rooms.append(stage.tile([P, PACK * MAIN], F32, name="main"))
+                rooms.append(stage.tile([P, PACK * CHUNK], F32, name="room", bufs=FETCH_BUFS))
             at = max(0, s0 % CHUNK - STEPS[8][3])
             main[k] = rooms[-1][:, PACK * at : PACK * (at + n - g)].rearrange("p (t c) -> p t c", t=PACK)
             m0 = s0 + (g if k % 2 else 0)
@@ -194,21 +203,17 @@ def tile_moe_pre_lin_relu2_kernel(
 
         def fetch_vector(k):
             a, s0, n, g, p = STEPS[k]
-            if g:
-                side[k] = stage.tile([P, PACK, HALF], F32, name="side", bufs=SIDE_BUFS)
+            if k == 0:
+                side[k] = stage.tile([P, PACK, HALF], F32, name="room", bufs=FETCH_BUFS)
+            elif g:
+                side[k] = stage.tile([P, PACK, HALF], F32, name="side")
             g0 = s0 + (0 if k % 2 else n - g)
             for t in range(PACK if g else 0):
                 nc.vector.tensor_copy(side[k][:, t, 0:g], window(a, t, g0, g0 + g))
 
-        def start(k):
-            a, s0, n, g, p = STEPS[k]
-            if k % 2 == 0:
-                return CHUNK - (n - p)
-            return CHUNK + max(0, STEPS[k - 1][4] - p)
-
         def weave_main(k):
             a, s0, n, g, p = STEPS[k]
-            woven = woven_sb[:, start(k) : start(k) + n, :]
+            woven = woven_sb[:, STARTS[k] : STARTS[k] + n, :]
             m0 = g if k % 2 else 0
             c0, c1 = (p, n) if k % 2 else (0, n - p)
             for b0, b1 in ((c0, min(c1, HALF)), (max(c0, HALF), c1)):
@@ -219,25 +224,24 @@ def tile_moe_pre_lin_relu2_kernel(
 
         def weave_side(k):
             a, s0, n, g, p = STEPS[k]
-            chunk = s0 // CHUNK
-            woven = woven_sb[:, start(k) : start(k) + n, :]
-            g0 = 0 if k % 2 else n - g
-            early = EARLY if k == 0 else 0
-            if early:
-                scale_weave(nc.gpsimd, woven[:, n - early : n, :], side[k][:, :, g - early : g], side_gate(chunk, n - early, n))
-            if p > g:
-                c0, m0 = (g, 0) if k % 2 else (n - p, n - p)
-                scale_weave(nc.gpsimd, woven[:, c0 : c0 + p - g, :], main[k][:, :, m0 : m0 + p - g], side_gate(chunk, c0, c0 + p - g))
-            if p:
-                w = g - early
-                scale_weave(nc.gpsimd, woven[:, g0 : g0 + w, :], side[k][:, :, 0:w], side_gate(chunk, g0, g0 + w))
+            woven = woven_sb[:, STARTS[k] : STARTS[k] + n, :]
+            g0, m0 = (0, g) if k % 2 else (n - g, 0)
+            by_scalar, by_vector = ((g, p), (0, g)) if k % 2 else ((n - p, n - g), (n - g, n))
+            runs = [by_scalar, by_vector]
+            if k == 0:
+                runs = [(EARLY[0], g0), (g0, EARLY[1]), (n - p, EARLY[0]), (EARLY[1], n)]
+            for c0, c1 in runs:
+                if c0 < c1:
+                    planes = side[k][:, :, c0 - g0 : c1 - g0] if g0 <= c0 < g0 + g else main[k][:, :, c0 - m0 : c1 - m0]
+                    gates = gate_late[:, 0 : c1 - c0] if (k, c0) == (0, EARLY[1]) else gate_sb[:, s0 + c0 : s0 + c1]
+                    scale_weave(nc.gpsimd, woven[:, c0:c1, :], planes, gates)
 
         def quantise(k):
             a, s0, n, g, p = STEPS[k]
             nc.vector.quantize_mx(
                 out=codes[a][:, s0 : s0 + n].bitcast(FP8X4),
                 scales=scales[a][:, s0 : s0 + n],
-                in_=woven_sb[:, start(k) : start(k) + n, :].rearrange("p c t -> p (c t)"),
+                in_=woven_sb[:, STARTS[k] : STARTS[k] + n, :].rearrange("p c t -> p (c t)"),
             )
             for e in range(s0 // C, (s0 + n) // C):
                 multiply(a, e, e * C)
@@ -251,30 +255,33 @@ def tile_moe_pre_lin_relu2_kernel(
                 nc.scalar.activation(y_sb[:, c0 : c0 + HALF], y_sb[:, c0 : c0 + HALF], ACT.Square)
 
         last = len(STEPS) - 1
-        open_banks(0, 2 * CHUNK, 4)
+        open_banks(CHUNK, 2 * CHUNK, 4)
+        open_banks(0, CHUNK, 4)
         fetch(0)
         fetch_vector(0)
         nc.vector.tensor_copy(gate_cols[:], turned[:, 0 : S // P])
-        spread_gate(0)
-        spread_gate(3)
-        for k in range(last + 1):
-            if k < last:
-                fetch(k + 1)
-            if k in (5, 6):
-                spread_gate(k - 1)
-            if k in (6, 7):
-                relu((k - 6) * CHUNK, (k - 5) * CHUNK)
-                square((k - 6) * CHUNK, (k - 5) * CHUNK)
+        spread_gate(0, 2)
+        spread_gate(1)
+        for k in range(last):
+            fetch(k + 1)
+            if k in SPREADS:
+                spread_gate(SPREADS[k])
+            if k in FINISH:
+                relu(FINISH[k], FINISH[k] + CHUNK)
+                square(FINISH[k], FINISH[k] + CHUNK)
             if k == 7:
                 open_banks(2 * CHUNK, S - 4 * C, 4)
                 open_banks(S - 4 * C, S - 2 * C, 2)
                 open_banks(S - 2 * C, S, 1)
             weave_main(k)
-            if k > 0:
+            if 0 < k < 9:
                 quantise(k - 1)
             weave_side(k)
-            if k < last:
-                fetch_vector(k + 1)
+            fetch_vector(k + 1)
+        quantise(8)
+        quantise(9)
+        weave_main(last)
+        quantise(10)
         quantise(last)
         relu(2 * CHUNK, S - 2 * C)
         square(2 * CHUNK, 2 * CHUNK + HALF)
@@ -288,7 +295,7 @@ def tile_moe_pre_lin_relu2_kernel(
         nc.vector.tensor_scalar(y_sb[:, S - C : S], banks[E - 1], bias_sb[:, E - 1 : E], 0.0, ADD, MAX)
         square_vector(S - C, S)
 
-        picked = stage.tile([P, PACK, CHUNK], F32, name="main")
+        picked = stage.tile([P, PACK, T], F32, name="room", bufs=FETCH_BUFS)
         first, second, pair, total = (picked[:, r, :] for r in range(PACK))
 
         def results(r, c0, c1):

@@ -29,17 +29,17 @@ ACT = mybir.ActivationFunctionType
 
 CHUNK = 1024
 HALF = CHUNK // 2
-SHARE = 544
+SHARE = 560
 PICK = 352
 STEPS = (
-    (0, 0, CHUNK, 512, 768),
+    (0, 0, CHUNK, 512, 848),
     (1, 0, CHUNK, 480, SHARE),
     (0, CHUNK, CHUNK, PICK, SHARE),
     (1, CHUNK, CHUNK, PICK, SHARE),
     (2, CHUNK, CHUNK, PICK, SHARE),
     (2, 0, CHUNK, PICK, SHARE),
-    (0, 2 * CHUNK, CHUNK, PICK, 576),
-    (1, 2 * CHUNK, CHUNK, 288, 288),
+    (0, 2 * CHUNK, CHUNK, PICK, 656),
+    (1, 2 * CHUNK, CHUNK, 320, 320),
     (2, 2 * CHUNK, 512, 160, 160),
     (2, 2 * CHUNK + 512, 256, 0, 0),
     (2, 2 * CHUNK + 768, 128, 0, 0),
@@ -47,7 +47,8 @@ STEPS = (
 )
 FETCH_BUFS = 3
 SIDE_BUFS = 2
-EARLY = (272, 720)
+FIRST = 384
+EARLY = (192, 720)
 SPREADS = {1: 2, 2: 3, 4: 1, 5: 4, 6: 5}
 FINISH = {6: CHUNK, 10: 0}
 ALONE = 192
@@ -120,8 +121,10 @@ def tile_moe_pre_lin_relu2_kernel(
         nc.sync.dma_start(out=gate_rows[:], in_=gate.rearrange("k (g j) -> (k g) j", j=P)[0:P, :])
         for t in range(1, PACK):
             load_x(0, t)
-        load_gate(*EARLY)
+        ahead = ((FIRST, HALF), (HALF, EARLY[1]), (EARLY[0], FIRST))
         for t in range(PACK):
+            if t < len(ahead):
+                load_gate(*ahead[t])
             load_x(1, t)
         load_gate(0, EARLY[0])
         gate_late = stage.tile([P, CHUNK - EARLY[1]], F32, name="side")
@@ -199,7 +202,9 @@ def tile_moe_pre_lin_relu2_kernel(
             main[k] = rooms[-1][:, PACK * at : PACK * (at + n - g)].rearrange("p (t c) -> p t c", t=PACK)
             m0 = s0 + (g if k % 2 else 0)
             for t in range(PACK):
-                nc.scalar.activation(main[k][:, t, :], window(a, t, m0, m0 + n - g), ACT.Copy)
+                cuts = ((FIRST, n - g), (0, FIRST)) if (k, t) == (0, PACK - 1) else ((0, n - g),)
+                for c0, c1 in cuts:
+                    nc.scalar.activation(main[k][:, t, c0:c1], window(a, t, m0 + c0, m0 + c1), ACT.Copy)
 
         def fetch_vector(k):
             a, s0, n, g, p = STEPS[k]
@@ -229,7 +234,7 @@ def tile_moe_pre_lin_relu2_kernel(
             by_scalar, by_vector = ((g, p), (0, g)) if k % 2 else ((n - p, n - g), (n - g, n))
             runs = [by_scalar, by_vector]
             if k == 0:
-                runs = [(EARLY[0], g0), (g0, EARLY[1]), (n - p, EARLY[0]), (EARLY[1], n)]
+                runs = [(FIRST, g0), (g0, EARLY[1]), (EARLY[0], FIRST), (n - p, EARLY[0]), (EARLY[1], n)]
             for c0, c1 in runs:
                 if c0 < c1:
                     planes = side[k][:, :, c0 - g0 : c1 - g0] if g0 <= c0 < g0 + g else main[k][:, :, c0 - m0 : c1 - m0]

@@ -29,7 +29,7 @@ ACT = mybir.ActivationFunctionType
 
 CHUNK = 1024
 HALF = CHUNK // 2
-SHARE = 560
+SHARE = 552
 PICK = 352
 STEPS = (
     (0, 0, CHUNK, 512, 848),
@@ -37,8 +37,8 @@ STEPS = (
     (0, CHUNK, CHUNK, PICK, SHARE),
     (1, CHUNK, CHUNK, PICK, SHARE),
     (2, CHUNK, CHUNK, PICK, SHARE),
-    (2, 0, CHUNK, PICK, SHARE),
-    (0, 2 * CHUNK, CHUNK, PICK, 656),
+    (2, 0, CHUNK, PICK, 512),
+    (0, 2 * CHUNK, CHUNK, PICK, 632),
     (1, 2 * CHUNK, CHUNK, 320, 320),
     (2, 2 * CHUNK, 512, 160, 160),
     (2, 2 * CHUNK + 512, 256, 0, 0),
@@ -87,7 +87,6 @@ def tile_moe_pre_lin_relu2_kernel(
         x_sb = [[keep.tile([P, T + PAD], F32, name=f"x_sb{a}_{t}") for t in range(PACK)] for a in range(PASSES)]
         woven_sb = keep.tile([P, WOVEN, PACK], BF16, name="woven_sb", align_bytes=64)
         w_sb = keep.tile([P, E * PASSES, 2 * N], U8, name="w_sb", align_bytes=64)
-        ws_sb = keep.tile([P, E * PASSES, N], U8, name="ws_sb", align_bytes=64)
         codes = [keep.tile([P, S], U32, name=f"codes{a}", align_bytes=64) for a in range(PASSES)]
         scales = [keep.tile([P, S], U8, name=f"scales{a}", align_bytes=64) for a in range(PASSES)]
         y_sb = keep.tile([P, S], F32, name="y_sb")
@@ -104,17 +103,17 @@ def tile_moe_pre_lin_relu2_kernel(
         nc.vector.memset(warm[:, 0:1], 0.0)
         nc.scalar.activation(warm[:, 1:2], warm[:, 0:1], ACT.Copy)
 
-        ones = keep.tile([P, P], F32, name="ones", align_bytes=64)
-        column = keep.tile([P, P], F32, name="column", align_bytes=64)
-        across = keep.tile([P, P], F32, name="across", align_bytes=64)
-        nc.vector.memset(ones[:], 1.0)
+        counting = keep.tile([P, 3 * P], F32, name="reused", align_bytes=64)
+        ones, column, across = (counting[:, i * P : (i + 1) * P] for i in range(3))
+        nc.vector.memset(ones, 1.0)
         nc.vector.memset(identity[:], 0.0)
-        nc.vector.tensor_tensor_scan(column[:], ones[:], ones[:], 0.0, MULT, ADD)
-        nc.vector.transpose(across[:], column[:])
+        nc.vector.tensor_tensor_scan(column, ones, ones, 0.0, MULT, ADD)
+        nc.vector.transpose(across, column)
         for q in range(0, P, 32):
             nc.vector.tensor_tensor(identity[q : q + 32, q : q + 32], across[q : q + 32, q : q + 32], column[q : q + 32, q : q + 32], mybir.AluOpType.is_equal)
 
-        nc.vector.memset(ws_sb[:].rearrange("p g n -> p (g n)").bitcast(I32), 0)
+        ws_sb = keep.tile([P, E * PASSES, N], U8, name="reused", align_bytes=64)
+        nc.gpsimd.memset(ws_sb[:].rearrange("p g n -> p (g n)").bitcast(I32), 0)
 
         nc.sync.dma_start(offs_sb[:], offs)
         load_x(0, 0)

@@ -29,43 +29,25 @@ ACT = mybir.ActivationFunctionType
 
 CHUNK = 1024
 HALF = CHUNK // 2
-SHARE = 552
-PICK = 352
-STEPS = (
-    (0, 0, CHUNK, 512, 848),
-    (1, 0, CHUNK, 480, SHARE),
-    (0, CHUNK, CHUNK, PICK, SHARE),
-    (1, CHUNK, CHUNK, PICK, SHARE),
-    (2, CHUNK, CHUNK, PICK, SHARE),
-    (2, 0, CHUNK, PICK, 512),
-    (0, 2 * CHUNK, CHUNK, PICK, 632),
-    (1, 2 * CHUNK, CHUNK, 320, 320),
-    (2, 2 * CHUNK, 512, 160, 160),
-    (2, 2 * CHUNK + 512, 256, 0, 0),
-    (2, 2 * CHUNK + 768, 128, 0, 0),
-    (2, 2 * CHUNK + 896, 128, 0, 0),
-)
-FETCH_BUFS = 3
-SIDE_BUFS = 2
-FIRST = 384
-EARLY = (192, 720)
-SPREADS = {1: 2, 2: 3, 4: 1, 5: 4, 6: 5}
-FINISH = {6: CHUNK, 10: 0}
+STEPS = ((0, 0), (0, 1), (0, 2), (1, 0), (1, 1), (2, 0), (2, 1), (1, 2))
+SHARE = 528
+EXTRA = 128
+EXTRA_HEAD = 960
+CUTS = ((0, HALF), (HALF, HALF + C), (HALF + C, CHUNK))
+OVER8 = 64
+FIN0 = 6
+TAIL_C = 512
+TAIL_A = 1024
+TAIL_B = 0
+ENDS = ((2 * CHUNK, HALF, TAIL_A), (2 * CHUNK + HALF, 3 * C, TAIL_B), (S - C, C, TAIL_C))
+SHARE8 = 264
+LEAD = 64
+FIRST_OWN = 0
+SHARE6 = 520
+SHARE7 = 336
+LAST_SHARE = 208
 ALONE = 192
 MID, END = 608, 896
-
-
-def woven_starts():
-    starts = [0]
-    for k in range(1, len(STEPS)):
-        n, p = STEPS[k][2], STEPS[k][4]
-        end = starts[-1] + STEPS[k - 1][2]
-        starts.append(end - p if k % 2 or not p else starts[-1] - (n - p))
-    return starts
-
-
-STARTS = woven_starts()
-WOVEN = max(at + step[2] for at, step in zip(STARTS, STEPS))
 
 
 def tile_moe_pre_lin_relu2_kernel(
@@ -74,36 +56,39 @@ def tile_moe_pre_lin_relu2_kernel(
     nc = tc.nc
     with ExitStack() as ctx:
         keep = ctx.enter_context(tc.tile_pool(name="keep", bufs=1))
-        stage = ctx.enter_context(tc.tile_pool(name="stage", bufs=SIDE_BUFS))
+        stage = ctx.enter_context(tc.tile_pool(name="stage", bufs=1))
         psum = ctx.enter_context(tc.psum_pool(name="psum", bufs=1))
 
         offs_sb = keep.tile([P, S // LANE], U16, name="offs_sb")
         pos_sb = [keep.tile([P, T // LANE], U16, name=f"pos_sb{r}") for r in range(3)]
-        gate_sb = keep.tile([P, S], F32, name="gate_sb")
-        gate_rows = keep.tile([P, P], F32, name="gate_rows")
+        gate_sb = [keep.tile([P, CHUNK], F32, name=f"gate_sb{c}") for c in range(S // CHUNK)]
         gate_cols = keep.tile([P, S // P], F32, name="gate_cols")
         identity = keep.tile([P, P], F32, name="identity")
         bias_sb = keep.tile([P, E], F32, name="bias_sb")
         x_sb = [[keep.tile([P, T + PAD], F32, name=f"x_sb{a}_{t}") for t in range(PACK)] for a in range(PASSES)]
-        woven_sb = keep.tile([P, WOVEN, PACK], BF16, name="woven_sb", align_bytes=64)
+        woven_sb = keep.tile([P, CHUNK, PACK], BF16, name="woven_sb", align_bytes=64)
         w_sb = keep.tile([P, E * PASSES, 2 * N], U8, name="w_sb", align_bytes=64)
+        ws_sb = keep.tile([P, E * PASSES, N], U8, name="ws_sb", align_bytes=64)
         codes = [keep.tile([P, S], U32, name=f"codes{a}", align_bytes=64) for a in range(PASSES)]
         scales = [keep.tile([P, S], U8, name=f"scales{a}", align_bytes=64) for a in range(PASSES)]
         y_sb = keep.tile([P, S], F32, name="y_sb")
+
+        def room(k, shape):
+            return stage.tile(shape, F32, name=f"room{k % 3}")
 
         x_rows = xT.rearrange("(a p t) c -> a t p c", p=P, t=PACK)
 
         def load_x(a, t):
             nc.sync.dma_start(out=x_sb[a][t][:, 0:T], in_=x_rows[a, t])
 
-        def load_gate(s0, s1):
-            nc.sync.dma_start(out=gate_sb[:, s0:s1], in_=gate[0:P, s0:s1])
+        def load_gate(c, s0, s1):
+            nc.sync.dma_start(out=gate_sb[c][:, s0:s1], in_=gate[0:P, c * CHUNK + s0 : c * CHUNK + s1])
 
         warm = keep.tile([P, 2], F32, name="warm")
         nc.vector.memset(warm[:, 0:1], 0.0)
         nc.scalar.activation(warm[:, 1:2], warm[:, 0:1], ACT.Copy)
 
-        counting = keep.tile([P, 3 * P], F32, name="reused", align_bytes=64)
+        counting = keep.tile([P, 3 * P], F32, name="counting", align_bytes=64)
         ones, column, across = (counting[:, i * P : (i + 1) * P] for i in range(3))
         nc.vector.memset(ones, 1.0)
         nc.vector.memset(identity[:], 0.0)
@@ -112,25 +97,23 @@ def tile_moe_pre_lin_relu2_kernel(
         for q in range(0, P, 32):
             nc.vector.tensor_tensor(identity[q : q + 32, q : q + 32], across[q : q + 32, q : q + 32], column[q : q + 32, q : q + 32], mybir.AluOpType.is_equal)
 
-        ws_sb = keep.tile([P, E * PASSES, N], U8, name="reused", align_bytes=64)
-        nc.gpsimd.memset(ws_sb[:].rearrange("p g n -> p (g n)").bitcast(I32), 0)
+        nc.vector.memset(ws_sb[:].rearrange("p g n -> p (g n)").bitcast(I32), 0)
 
         nc.sync.dma_start(offs_sb[:], offs)
-        load_x(0, 0)
-        nc.sync.dma_start(out=gate_rows[:], in_=gate.rearrange("k (g j) -> (k g) j", j=P)[0:P, :])
-        for t in range(1, PACK):
-            load_x(0, t)
-        ahead = ((FIRST, HALF), (HALF, EARLY[1]), (EARLY[0], FIRST))
         for t in range(PACK):
-            if t < len(ahead):
-                load_gate(*ahead[t])
+            load_x(0, t)
+        gate_rows = room(1, [P, P])
+        nc.sync.dma_start(out=gate_rows[:], in_=gate.rearrange("k (g j) -> (k g) j", j=P)[0:P, :])
+        gate_lead = room(2, [P, LEAD])
+        nc.sync.dma_start(out=gate_lead[:], in_=gate[0:P, 0:LEAD])
+        load_gate(0, LEAD, CHUNK - FIRST_OWN)
+        for t in range(PACK):
             load_x(1, t)
-        load_gate(0, EARLY[0])
-        gate_late = stage.tile([P, CHUNK - EARLY[1]], F32, name="side")
-        nc.sync.dma_start(out=gate_late[:], in_=gate[0:P, EARLY[1] : CHUNK])
+        load_gate(1, 0, SHARE)
         for t in range(PACK):
             load_x(2, t)
-        load_gate(CHUNK, 2 * CHUNK)
+        load_gate(2, 0, HALF + LAST_SHARE)
+        load_gate(0, 0, LEAD)
         nc.sync.dma_start(out=bias_sb[:], in_=b)
         ws_rows = w_scales.rearrange("e a (g r) n -> r g (e a) n", r=4)
         w_rows = w_words.rearrange("e a p m -> p (e a) m")
@@ -139,13 +122,18 @@ def tile_moe_pre_lin_relu2_kernel(
             for r in range(4):
                 nc.sync.dma_start(out=ws_sb[r:P:32, groups, :].bitcast(I32), in_=ws_rows[r, :, groups].bitcast(I32))
             nc.sync.dma_start(out=w_sb[:, groups, :].bitcast(I32), in_=w_rows[:, groups, :].bitcast(I32))
-        load_gate(2 * CHUNK, 2 * CHUNK + STEPS[7][4])
-        load_gate(2 * CHUNK + HALF - STEPS[8][4], S)
         for r, pos in enumerate((pos1, pos2, pos3)):
             nc.sync.dma_start(pos_sb[r][:], pos)
 
         def window(a, t, s0, s1):
             return x_sb[a][t][:].indirect(offs_sb[:, s0 // LANE : s1 // LANE])
+
+        def gather(engine, planes, a, s0, t, c0, c1):
+            if c0 < c1:
+                if engine == "scalar":
+                    nc.scalar.activation(planes[:, t, c0:c1], window(a, t, s0 + c0, s0 + c1), ACT.Copy)
+                else:
+                    nc.vector.tensor_copy(planes[:, t, c0:c1], window(a, t, s0 + c0, s0 + c1))
 
         def scale_weave(engine, woven, planes, gates):
             w = planes.shape[2]
@@ -156,13 +144,14 @@ def tile_moe_pre_lin_relu2_kernel(
                 MULT,
             )
 
-        turned = psum.tile([P, HALF], F32, name="gates", bufs=2)
+        turned = psum.tile([P, HALF], F32, name="gates0")
         nc.tensor.transpose(turned[:, 0:P], gate_rows[:], identity[:])
+        nc.vector.tensor_copy(gate_cols[:], turned[:, 0 : S // P])
         gate_ps = {}
 
-        def spread_gate(h, groups=HALF // P):
-            gate_ps[h] = psum.tile([P, HALF], F32, name="gates", bufs=2)
-            for j in range(groups):
+        def spread_gate(h, bank):
+            gate_ps[h] = psum.tile([P, HALF], F32, name=bank)
+            for j in range(HALF // P):
                 g = h * (HALF // P) + j
                 nc.tensor.transpose(
                     gate_ps[h][:, j * P : (j + 1) * P], gate_cols[:, g : g + 1].to_broadcast([P, P]), identity[:]
@@ -171,135 +160,159 @@ def tile_moe_pre_lin_relu2_kernel(
         banks = {}
         opens, closes = set(), set()
 
-        def open_banks(s0, s1, share):
-            for e0 in range(s0 // C, s1 // C, share):
-                bank = psum.tile([N, HALF], F32, name="bank", bufs=BANKS - 2)
-                for e in range(e0, min(e0 + share, s1 // C)):
-                    banks[e] = bank[:, (e - e0) * C : (e - e0 + 1) * C]
-                opens.add(e0)
-                closes.add(min(e0 + share, s1 // C) - 1)
+        def open_bank(e0, e1, at):
+            bank = psum.tile([N, HALF], F32, name=at)
+            for e in range(e0, e1):
+                banks[e] = bank[:, (e - e0) * C : (e - e0 + 1) * C]
+            opens.add(e0)
+            closes.add(e1 - 1)
 
-        def multiply(a, e, c0):
-            g = e * PASSES + a
-            nc.tensor.matmul_mx(
-                out=banks[e],
-                lhsT=w_sb[:, g, :].bitcast(FP4X4),
-                lhsT_scale=ws_sb[:, g, :],
-                rhs=codes[a][:, c0 : c0 + C].bitcast(FP8X4),
-                rhs_scale=scales[a][:, c0 : c0 + C],
-                start=(a == 0 and e in opens),
-                stop=(a == PASSES - 1 and e in closes),
-            )
-
-        main, side, rooms = {}, {}, []
-
-        def fetch(k):
-            a, s0, n, g, p = STEPS[k]
-            if s0 % CHUNK == 0:
-                rooms.append(stage.tile([P, PACK * CHUNK], F32, name="room", bufs=FETCH_BUFS))
-            at = max(0, s0 % CHUNK - STEPS[8][3])
-            main[k] = rooms[-1][:, PACK * at : PACK * (at + n - g)].rearrange("p (t c) -> p t c", t=PACK)
-            m0 = s0 + (g if k % 2 else 0)
-            for t in range(PACK):
-                cuts = ((FIRST, n - g), (0, FIRST)) if (k, t) == (0, PACK - 1) else ((0, n - g),)
-                for c0, c1 in cuts:
-                    nc.scalar.activation(main[k][:, t, c0:c1], window(a, t, m0 + c0, m0 + c1), ACT.Copy)
-
-        def fetch_vector(k):
-            a, s0, n, g, p = STEPS[k]
-            if k == 0:
-                side[k] = stage.tile([P, PACK, HALF], F32, name="room", bufs=FETCH_BUFS)
-            elif g:
-                side[k] = stage.tile([P, PACK, HALF], F32, name="side")
-            g0 = s0 + (0 if k % 2 else n - g)
-            for t in range(PACK if g else 0):
-                nc.vector.tensor_copy(side[k][:, t, 0:g], window(a, t, g0, g0 + g))
-
-        def weave_main(k):
-            a, s0, n, g, p = STEPS[k]
-            woven = woven_sb[:, STARTS[k] : STARTS[k] + n, :]
-            m0 = g if k % 2 else 0
-            c0, c1 = (p, n) if k % 2 else (0, n - p)
-            for b0, b1 in ((c0, min(c1, HALF)), (max(c0, HALF), c1)):
-                if b0 < b1:
-                    h, at = divmod(s0 + b0, HALF)
-                    gates = gate_ps[h][:, at : at + b1 - b0]
-                    scale_weave(nc.vector, woven[:, b0:b1, :], main[k][:, :, b0 - m0 : b1 - m0], gates)
-
-        def weave_side(k):
-            a, s0, n, g, p = STEPS[k]
-            woven = woven_sb[:, STARTS[k] : STARTS[k] + n, :]
-            g0, m0 = (0, g) if k % 2 else (n - g, 0)
-            by_scalar, by_vector = ((g, p), (0, g)) if k % 2 else ((n - p, n - g), (n - g, n))
-            runs = [by_scalar, by_vector]
-            if k == 0:
-                runs = [(FIRST, g0), (g0, EARLY[1]), (EARLY[0], FIRST), (n - p, EARLY[0]), (EARLY[1], n)]
-            for c0, c1 in runs:
-                if c0 < c1:
-                    planes = side[k][:, :, c0 - g0 : c1 - g0] if g0 <= c0 < g0 + g else main[k][:, :, c0 - m0 : c1 - m0]
-                    gates = gate_late[:, 0 : c1 - c0] if (k, c0) == (0, EARLY[1]) else gate_sb[:, s0 + c0 : s0 + c1]
-                    scale_weave(nc.gpsimd, woven[:, c0:c1, :], planes, gates)
-
-        def quantise(k):
-            a, s0, n, g, p = STEPS[k]
+        def quantise(a, s0, at, n):
             nc.vector.quantize_mx(
                 out=codes[a][:, s0 : s0 + n].bitcast(FP8X4),
                 scales=scales[a][:, s0 : s0 + n],
-                in_=woven_sb[:, STARTS[k] : STARTS[k] + n, :].rearrange("p c t -> p (c t)"),
+                in_=woven_sb[:, at : at + n, :].rearrange("p c t -> p (c t)"),
             )
-            for e in range(s0 // C, (s0 + n) // C):
-                multiply(a, e, e * C)
 
-        def relu(s0, s1):
-            for e in range(s0 // C, s1 // C):
+        def multiply(a, e0, e1):
+            for e in range(e0, e1):
+                g = e * PASSES + a
+                nc.tensor.matmul_mx(
+                    out=banks[e],
+                    lhsT=w_sb[:, g, :].bitcast(FP4X4),
+                    lhsT_scale=ws_sb[:, g, :],
+                    rhs=codes[a][:, e * C : (e + 1) * C].bitcast(FP8X4),
+                    rhs_scale=scales[a][:, e * C : (e + 1) * C],
+                    start=(a == 0 and e in opens),
+                    stop=(a == PASSES - 1 and e in closes),
+                )
+
+        rooms = {}
+
+        def fetch(k, extra):
+            a, c = STEPS[k]
+            rooms[k] = room(k, [P, PACK, CHUNK])
+            gather("vector", rooms[k], a, c * CHUNK, 0, 0, CHUNK)
+            gather("vector", rooms[k], a, c * CHUNK, 1, 0, extra)
+            gather("scalar", rooms[k], a, c * CHUNK, 1, extra, CHUNK)
+            for t in (2, 3):
+                gather("scalar", rooms[k], a, c * CHUNK, t, 0, CHUNK)
+
+        def fetch_end(k, s0, n, mine):
+            rooms[k] = room(k, [P, PACK, n])
+            for t in range(PACK):
+                cut = min(max(mine - t * n, 0), n)
+                gather("vector", rooms[k], 2, s0, t, 0, cut)
+                gather("scalar", rooms[k], 2, s0, t, cut, n)
+
+        def weave_vector(planes, s0, at, n):
+            h, c0 = divmod(s0, HALF)
+            scale_weave(nc.vector, woven_sb[:, at : at + n, :], planes, gate_ps[h][:, c0 : c0 + n])
+
+        def share(k):
+            return CHUNK - FIRST_OWN if k == 0 else SHARE if k < 6 else SHARE6 if k == 6 else SHARE7
+
+        def own(k):
+            a, c = STEPS[k]
+            for c0, c1 in ((share(k), HALF), (max(share(k), HALF), CHUNK)):
+                if c0 < c1:
+                    weave_vector(rooms[k][:, :, c0:c1], c * CHUNK + c0, c0, c1 - c0)
+
+        def shared(k):
+            a, c = STEPS[k]
+            c0, c1 = 0 if k else LEAD, share(k)
+            scale_weave(nc.gpsimd, woven_sb[:, c0:c1, :], rooms[k][:, :, c0:c1], gate_sb[c][:, c0:c1])
+
+        def quantise_step(k):
+            a, c = STEPS[k]
+            for c0, c1 in CUTS:
+                quantise(a, c * CHUNK + c0, c0, c1 - c0)
+            if k != 2:
+                multiply(a, 8 * c, min(8 * c + 8, 20))
+
+        def relu(e0, e1):
+            for e in range(e0, e1):
                 nc.scalar.activation(y_sb[:, e * C : (e + 1) * C], banks[e], ACT.Relu, bias=bias_sb[:, e : e + 1])
 
-        def square(s0, s1):
-            for c0 in range(s0, s1, HALF):
-                nc.scalar.activation(y_sb[:, c0 : c0 + HALF], y_sb[:, c0 : c0 + HALF], ACT.Square)
+        def relu_vector(into, e):
+            nc.vector.tensor_scalar(into, banks[e], bias_sb[:, e : e + 1], 0.0, ADD, MAX)
 
-        last = len(STEPS) - 1
-        open_banks(CHUNK, 2 * CHUNK, 4)
-        open_banks(0, CHUNK, 4)
-        fetch(0)
-        fetch_vector(0)
-        nc.vector.tensor_copy(gate_cols[:], turned[:, 0 : S // P])
-        spread_gate(0, 2)
-        spread_gate(1)
-        for k in range(last):
-            fetch(k + 1)
-            if k in SPREADS:
-                spread_gate(SPREADS[k])
-            if k in FINISH:
-                relu(FINISH[k], FINISH[k] + CHUNK)
-                square(FINISH[k], FINISH[k] + CHUNK)
-            if k == 7:
-                open_banks(2 * CHUNK, S - 4 * C, 4)
-                open_banks(S - 4 * C, S - 2 * C, 2)
-                open_banks(S - 2 * C, S, 1)
-            weave_main(k)
-            if 0 < k < 9:
-                quantise(k - 1)
-            weave_side(k)
-            fetch_vector(k + 1)
-        quantise(8)
-        quantise(9)
-        weave_main(last)
-        quantise(10)
-        quantise(last)
-        relu(2 * CHUNK, S - 2 * C)
-        square(2 * CHUNK, 2 * CHUNK + HALF)
-        relu(S - 2 * C, S - C)
-        nc.scalar.activation(y_sb[:, S - 2 * C : S - C], y_sb[:, S - 2 * C : S - C], ACT.Square)
+        def square(s0, s1):
+            nc.scalar.activation(y_sb[:, s0:s1], y_sb[:, s0:s1], ACT.Square)
 
         def square_vector(s0, s1):
             nc.vector.tensor_tensor(y_sb[:, s0:s1], y_sb[:, s0:s1], y_sb[:, s0:s1], MULT)
 
-        square_vector(S - 4 * C, S - 2 * C)
-        nc.vector.tensor_scalar(y_sb[:, S - C : S], banks[E - 1], bias_sb[:, E - 1 : E], 0.0, ADD, MAX)
+        def finish(c):
+            relu(8 * c, 8 * c + 8)
+            for h in range(2):
+                square(c * CHUNK + h * HALF, c * CHUNK + (h + 1) * HALF)
+
+        for at in range(5):
+            open_bank(4 * at, 4 * at + 4, f"bank{at}")
+
+        rooms[0] = room(0, [P, PACK, CHUNK])
+        for t in range(PACK):
+            if t == PACK - 1:
+                gather("scalar", rooms[0], 0, 0, t, 0, LEAD)
+                gather("scalar", rooms[0], 0, 0, t, LEAD, HALF)
+            else:
+                gather("scalar", rooms[0], 0, 0, t, 0, HALF)
+            gather("vector", rooms[0], 0, 0, t, HALF, CHUNK)
+        scale_weave(nc.gpsimd, woven_sb[:, 0:LEAD, :], rooms[0][:, :, 0:LEAD], gate_lead[:])
+        for c in (1, 0, 2):
+            spread_gate(2 * c + 1, f"gates{c}")
+        fetch(1, EXTRA_HEAD)
+        last = len(STEPS) - 1
+        s8 = 2 * CHUNK
+        for k in range(len(STEPS)):
+            shared(k)
+            if k + 2 <= last:
+                fetch(k + 2, EXTRA_HEAD if k == 0 else EXTRA)
+            else:
+                fetch_end(k + 2, *ENDS[k + 1 - last])
+            own(k)
+            quantise_step(k)
+            if k == 2:
+                multiply(0, 16, 20)
+            if k == 5:
+                spread_gate(4, "gates0")
+            if k == 6:
+                open_bank(20, 22, "gates1")
+                multiply(0, 20, 22)
+        multiply(1, 20, 22)
+        lower, upper = rooms[last + 1], rooms[last + 2]
+        at = HALF + C - HALF // 2 - OVER8
+        scale_weave(nc.gpsimd, woven_sb[:, at : at + SHARE8, :], lower[:, :, 0:SHARE8], gate_sb[2][:, 0:SHARE8])
+        fetch_end(last + 3, *ENDS[2])
+        weave_vector(lower[:, :, SHARE8:HALF], s8 + SHARE8, at + SHARE8, HALF - SHARE8)
+        for e0 in (16, 18):
+            quantise(2, e0 * C, at + (e0 - 16) * C, 2 * C)
+        multiply(2, 16, 20)
+        finish(0)
+        open_bank(22, 23, "bank0")
+        open_bank(23, 24, "bank1")
+        for a in range(2):
+            multiply(a, 22, 24)
+        finish(1)
+        at = at + HALF // 2 - LAST_SHARE
+        scale_weave(nc.gpsimd, woven_sb[:, at : at + LAST_SHARE, :], upper[:, :, 0:LAST_SHARE], gate_sb[2][:, HALF : HALF + LAST_SHARE])
+        weave_vector(upper[:, :, LAST_SHARE : 3 * C], s8 + HALF + LAST_SHARE, at + LAST_SHARE, 3 * C - LAST_SHARE)
+        weave_vector(rooms[last + 3][:], S - C, at + 3 * C, C)
+        for e in range(16, 20):
+            relu_vector(y_sb[:, e * C : (e + 1) * C], e)
+        square(s8, s8 + HALF)
+        for e0, e1 in ((20, 22), (22, 23), (23, 24)):
+            quantise(2, e0 * C, at + (e0 - 20) * C, (e1 - e0) * C)
+            multiply(2, e0, e1)
+        for e in (20, 21, 23):
+            relu_vector(y_sb[:, e * C : (e + 1) * C], e)
+        relu(22, 23)
+        square(22 * C, 23 * C)
+        square_vector(20 * C, 22 * C)
         square_vector(S - C, S)
 
-        picked = stage.tile([P, PACK, T], F32, name="room", bufs=FETCH_BUFS)
+        picked = room(last + 1, [P, PACK, T])
         first, second, pair, total = (picked[:, r, :] for r in range(PACK))
 
         def results(r, c0, c1):

@@ -28,6 +28,7 @@ MAX = mybir.AluOpType.max
 ACT = mybir.ActivationFunctionType
 
 CHUNK = 1024
+GROUP = CHUNK // C * PASSES
 HALF = CHUNK // 2
 STEPS = ((0, 0), (0, 1), (0, 2), (1, 0), (1, 1), (2, 0), (2, 1), (1, 2))
 SHARE = 528
@@ -67,7 +68,7 @@ def tile_moe_pre_lin_relu2_kernel(
         bias_sb = keep.tile([P, E], F32, name="bias_sb")
         x_sb = [[keep.tile([P, T + PAD], F32, name=f"x_sb{a}_{t}") for t in range(PACK)] for a in range(PASSES)]
         woven_sb = keep.tile([P, CHUNK, PACK], BF16, name="woven_sb", align_bytes=64)
-        w_sb = keep.tile([P, E * PASSES, 2 * N], U8, name="w_sb", align_bytes=64)
+        w_sb = [keep.tile([P, GROUP, 2 * N], U8, name=f"w_sb{c}", align_bytes=64) for c in range(S // CHUNK)]
         ws_sb = keep.tile([P, E * PASSES, N], U8, name="ws_sb", align_bytes=64)
         codes = [keep.tile([P, S], U32, name=f"codes{a}", align_bytes=64) for a in range(PASSES)]
         scales = [keep.tile([P, S], U8, name=f"scales{a}", align_bytes=64) for a in range(PASSES)]
@@ -88,6 +89,8 @@ def tile_moe_pre_lin_relu2_kernel(
         nc.vector.memset(warm[:, 0:1], 0.0)
         nc.scalar.activation(warm[:, 1:2], warm[:, 0:1], ACT.Copy)
 
+        nc.gpsimd.memset(ws_sb[:].rearrange("p g n -> p (g n)").bitcast(I32), 0)
+
         counting = keep.tile([P, 3 * P], F32, name="counting", align_bytes=64)
         ones, column, across = (counting[:, i * P : (i + 1) * P] for i in range(3))
         nc.vector.memset(ones, 1.0)
@@ -97,7 +100,6 @@ def tile_moe_pre_lin_relu2_kernel(
         for q in range(0, P, 32):
             nc.vector.tensor_tensor(identity[q : q + 32, q : q + 32], across[q : q + 32, q : q + 32], column[q : q + 32, q : q + 32], mybir.AluOpType.is_equal)
 
-        nc.vector.memset(ws_sb[:].rearrange("p g n -> p (g n)").bitcast(I32), 0)
 
         nc.sync.dma_start(offs_sb[:], offs)
         for t in range(PACK):
@@ -109,19 +111,19 @@ def tile_moe_pre_lin_relu2_kernel(
         load_gate(0, LEAD, CHUNK - FIRST_OWN)
         for t in range(PACK):
             load_x(1, t)
+        ws_rows = w_scales.rearrange("e a (q r) n -> q r (e a) n", r=4)
+        w_rows = w_words.rearrange("e a p m -> p (e a) m")
+
         load_gate(1, 0, SHARE)
         for t in range(PACK):
             load_x(2, t)
         load_gate(2, 0, HALF + LAST_SHARE)
+        for q in range(4):
+            nc.sync.dma_start(out=ws_sb[32 * q : 32 * q + 4].bitcast(I32), in_=ws_rows[q].bitcast(I32))
+        for c in range(S // CHUNK):
+            nc.sync.dma_start(out=w_sb[c][:].bitcast(I32), in_=w_rows[:, c * GROUP : (c + 1) * GROUP, :].bitcast(I32))
         load_gate(0, 0, LEAD)
         nc.sync.dma_start(out=bias_sb[:], in_=b)
-        ws_rows = w_scales.rearrange("e a (g r) n -> r g (e a) n", r=4)
-        w_rows = w_words.rearrange("e a p m -> p (e a) m")
-        for g0 in range(0, E * PASSES, BANKS * PASSES):
-            groups = slice(g0, g0 + BANKS * PASSES)
-            for r in range(4):
-                nc.sync.dma_start(out=ws_sb[r:P:32, groups, :].bitcast(I32), in_=ws_rows[r, :, groups].bitcast(I32))
-            nc.sync.dma_start(out=w_sb[:, groups, :].bitcast(I32), in_=w_rows[:, groups, :].bitcast(I32))
         for r, pos in enumerate((pos1, pos2, pos3)):
             nc.sync.dma_start(pos_sb[r][:], pos)
 
@@ -176,11 +178,11 @@ def tile_moe_pre_lin_relu2_kernel(
 
         def multiply(a, e0, e1):
             for e in range(e0, e1):
-                g = e * PASSES + a
+                c, g = divmod(e * PASSES + a, GROUP)
                 nc.tensor.matmul_mx(
                     out=banks[e],
-                    lhsT=w_sb[:, g, :].bitcast(FP4X4),
-                    lhsT_scale=ws_sb[:, g, :],
+                    lhsT=w_sb[c][:, g, :].bitcast(FP4X4),
+                    lhsT_scale=ws_sb[:, e * PASSES + a, :],
                     rhs=codes[a][:, e * C : (e + 1) * C].bitcast(FP8X4),
                     rhs_scale=scales[a][:, e * C : (e + 1) * C],
                     start=(a == 0 and e in opens),
@@ -243,11 +245,6 @@ def tile_moe_pre_lin_relu2_kernel(
         def square_vector(s0, s1):
             nc.vector.tensor_tensor(y_sb[:, s0:s1], y_sb[:, s0:s1], y_sb[:, s0:s1], MULT)
 
-        def finish(c):
-            relu(8 * c, 8 * c + 8)
-            for h in range(2):
-                square(c * CHUNK + h * HALF, c * CHUNK + (h + 1) * HALF)
-
         for at in range(5):
             open_bank(4 * at, 4 * at + 4, f"bank{at}")
 
@@ -289,18 +286,23 @@ def tile_moe_pre_lin_relu2_kernel(
         for e0 in (16, 18):
             quantise(2, e0 * C, at + (e0 - 16) * C, 2 * C)
         multiply(2, 16, 20)
-        finish(0)
+        for e0 in (0, 8, 12):
+            relu(e0, e0 + 4)
+        for e0 in (0, 8, 12):
+            square(e0 * C, e0 * C + HALF)
         open_bank(22, 23, "bank0")
-        open_bank(23, 24, "bank1")
+        open_bank(23, 24, "bank2")
         for a in range(2):
             multiply(a, 22, 24)
-        finish(1)
         at = at + HALF // 2 - LAST_SHARE
         scale_weave(nc.gpsimd, woven_sb[:, at : at + LAST_SHARE, :], upper[:, :, 0:LAST_SHARE], gate_sb[2][:, HALF : HALF + LAST_SHARE])
+        late = room(last + 1, [P, HALF])
+        for e in range(4, 8):
+            relu_vector(late[:, (e - 4) * C : (e - 3) * C], e)
         weave_vector(upper[:, :, LAST_SHARE : 3 * C], s8 + HALF + LAST_SHARE, at + LAST_SHARE, 3 * C - LAST_SHARE)
         weave_vector(rooms[last + 3][:], S - C, at + 3 * C, C)
-        for e in range(16, 20):
-            relu_vector(y_sb[:, e * C : (e + 1) * C], e)
+        nc.scalar.activation(y_sb[:, HALF:CHUNK], late[:], ACT.Square)
+        relu(16, 20)
         square(s8, s8 + HALF)
         for e0, e1 in ((20, 22), (22, 23), (23, 24)):
             quantise(2, e0 * C, at + (e0 - 20) * C, (e1 - e0) * C)

@@ -118,12 +118,12 @@ def tile_moe_pre_lin_relu2_kernel(
         for t in range(PACK):
             load_x(2, t)
         load_gate(2, 0, HALF + LAST_SHARE)
+        load_gate(0, 0, LEAD)
+        nc.sync.dma_start(out=bias_sb[:], in_=b)
         for q in range(4):
             nc.sync.dma_start(out=ws_sb[32 * q : 32 * q + 4].bitcast(I32), in_=ws_rows[q].bitcast(I32))
         for c in range(S // CHUNK):
             nc.sync.dma_start(out=w_sb[c][:].bitcast(I32), in_=w_rows[:, c * GROUP : (c + 1) * GROUP, :].bitcast(I32))
-        load_gate(0, 0, LEAD)
-        nc.sync.dma_start(out=bias_sb[:], in_=b)
         for r, pos in enumerate((pos1, pos2, pos3)):
             nc.sync.dma_start(pos_sb[r][:], pos)
 

@@ -46,7 +46,7 @@ LEAD = 64
 FIRST_OWN = 0
 SHARE6 = 520
 SHARE7 = 336
-LAST_SHARE = 208
+LAST_SHARE = 160
 ALONE = 192
 MID, END = 608, 896
 
@@ -89,8 +89,6 @@ def tile_moe_pre_lin_relu2_kernel(
         nc.vector.memset(warm[:, 0:1], 0.0)
         nc.scalar.activation(warm[:, 1:2], warm[:, 0:1], ACT.Copy)
 
-        nc.gpsimd.memset(ws_sb[:].rearrange("p g n -> p (g n)").bitcast(I32), 0)
-
         counting = keep.tile([P, 3 * P], F32, name="counting", align_bytes=64)
         ones, column, across = (counting[:, i * P : (i + 1) * P] for i in range(3))
         nc.vector.memset(ones, 1.0)
@@ -100,6 +98,8 @@ def tile_moe_pre_lin_relu2_kernel(
         for q in range(0, P, 32):
             nc.vector.tensor_tensor(identity[q : q + 32, q : q + 32], across[q : q + 32, q : q + 32], column[q : q + 32, q : q + 32], mybir.AluOpType.is_equal)
 
+
+        nc.vector.memset(ws_sb[:].rearrange("p g n -> p (g n)").bitcast(I32), 0)
 
         nc.sync.dma_start(offs_sb[:], offs)
         for t in range(PACK):
@@ -195,10 +195,13 @@ def tile_moe_pre_lin_relu2_kernel(
             a, c = STEPS[k]
             rooms[k] = room(k, [P, PACK, CHUNK])
             gather("vector", rooms[k], a, c * CHUNK, 0, 0, CHUNK)
-            gather("vector", rooms[k], a, c * CHUNK, 1, 0, extra)
             gather("scalar", rooms[k], a, c * CHUNK, 1, extra, CHUNK)
             for t in (2, 3):
                 gather("scalar", rooms[k], a, c * CHUNK, t, 0, CHUNK)
+
+        def fetch_extra(k, extra):
+            a, c = STEPS[k]
+            gather("vector", rooms[k], a, c * CHUNK, 1, 0, extra)
 
         def fetch_end(k, s0, n, mine):
             rooms[k] = room(k, [P, PACK, n])
@@ -245,7 +248,7 @@ def tile_moe_pre_lin_relu2_kernel(
         def square_vector(s0, s1):
             nc.vector.tensor_tensor(y_sb[:, s0:s1], y_sb[:, s0:s1], y_sb[:, s0:s1], MULT)
 
-        for at in range(5):
+        for at in range(4):
             open_bank(4 * at, 4 * at + 4, f"bank{at}")
 
         rooms[0] = room(0, [P, PACK, CHUNK])
@@ -257,9 +260,11 @@ def tile_moe_pre_lin_relu2_kernel(
                 gather("scalar", rooms[0], 0, 0, t, 0, HALF)
             gather("vector", rooms[0], 0, 0, t, HALF, CHUNK)
         scale_weave(nc.gpsimd, woven_sb[:, 0:LEAD, :], rooms[0][:, :, 0:LEAD], gate_lead[:])
-        for c in (1, 0, 2):
+        for c in (1, 2, 0):
             spread_gate(2 * c + 1, f"gates{c}")
+        spread_gate(4, "gates3")
         fetch(1, EXTRA_HEAD)
+        fetch_extra(1, EXTRA_HEAD)
         last = len(STEPS) - 1
         s8 = 2 * CHUNK
         for k in range(len(STEPS)):
@@ -269,11 +274,12 @@ def tile_moe_pre_lin_relu2_kernel(
             else:
                 fetch_end(k + 2, *ENDS[k + 1 - last])
             own(k)
+            if k + 2 <= last:
+                fetch_extra(k + 2, EXTRA_HEAD if k == 0 else EXTRA)
             quantise_step(k)
-            if k == 2:
-                multiply(0, 16, 20)
             if k == 5:
-                spread_gate(4, "gates0")
+                open_bank(16, 20, "gates0")
+                multiply(0, 16, 20)
             if k == 6:
                 open_bank(20, 22, "gates1")
                 multiply(0, 20, 22)
@@ -298,15 +304,15 @@ def tile_moe_pre_lin_relu2_kernel(
         scale_weave(nc.gpsimd, woven_sb[:, at : at + LAST_SHARE, :], upper[:, :, 0:LAST_SHARE], gate_sb[2][:, HALF : HALF + LAST_SHARE])
         late = room(last + 1, [P, HALF])
         for e in range(4, 8):
-            relu_vector(late[:, (e - 4) * C : (e - 3) * C], e)
+            nc.scalar.activation(late[:, (e - 4) * C : (e - 3) * C], banks[e], ACT.Relu, bias=bias_sb[:, e : e + 1])
         weave_vector(upper[:, :, LAST_SHARE : 3 * C], s8 + HALF + LAST_SHARE, at + LAST_SHARE, 3 * C - LAST_SHARE)
         weave_vector(rooms[last + 3][:], S - C, at + 3 * C, C)
-        nc.scalar.activation(y_sb[:, HALF:CHUNK], late[:], ACT.Square)
         relu(16, 20)
         square(s8, s8 + HALF)
         for e0, e1 in ((20, 22), (22, 23), (23, 24)):
             quantise(2, e0 * C, at + (e0 - 20) * C, (e1 - e0) * C)
             multiply(2, e0, e1)
+        nc.vector.tensor_tensor(y_sb[:, HALF:CHUNK], late[:], late[:], MULT)
         for e in (20, 21, 23):
             relu_vector(y_sb[:, e * C : (e + 1) * C], e)
         relu(22, 23)

@@ -32,10 +32,9 @@ GROUP = CHUNK // C * PASSES
 HALF = CHUNK // 2
 STEPS = ((0, 0), (0, 1), (0, 2), (1, 0), (1, 1), (2, 0), (2, 1), (1, 2))
 SHARE = 528
-EXTRA = 128
-EXTRA_HEAD = 960
-CUTS = ((0, HALF), (HALF, HALF + C), (HALF + C, CHUNK))
-OVER8 = 64
+EXTRA = 96
+EXTRA_HEAD = 896
+CUTS = ((0, HALF), (HALF, CHUNK))
 FIN0 = 6
 TAIL_C = 512
 TAIL_A = 1024
@@ -49,6 +48,14 @@ SHARE7 = 336
 LAST_SHARE = 160
 ALONE = 192
 MID, END = 608, 896
+
+
+def share(k):
+    return CHUNK - FIRST_OWN if k == 0 else SHARE if k < 6 else SHARE6 if k == 6 else SHARE7
+
+
+def place(k):
+    return sum(max(share(j) - HALF, 0) for j in range(k + 1, len(STEPS)))
 
 
 def tile_moe_pre_lin_relu2_kernel(
@@ -67,7 +74,7 @@ def tile_moe_pre_lin_relu2_kernel(
         identity = keep.tile([P, P], F32, name="identity")
         bias_sb = keep.tile([P, E], F32, name="bias_sb")
         x_sb = [[keep.tile([P, T + PAD], F32, name=f"x_sb{a}_{t}") for t in range(PACK)] for a in range(PASSES)]
-        woven_sb = keep.tile([P, CHUNK, PACK], BF16, name="woven_sb", align_bytes=64)
+        woven_sb = keep.tile([P, CHUNK + place(0), PACK], BF16, name="woven_sb", align_bytes=64)
         w_sb = [keep.tile([P, GROUP, 2 * N], U8, name=f"w_sb{c}", align_bytes=64) for c in range(S // CHUNK)]
         ws_sb = keep.tile([P, E * PASSES, N], U8, name="ws_sb", align_bytes=64)
         codes = [keep.tile([P, S], U32, name=f"codes{a}", align_bytes=64) for a in range(PASSES)]
@@ -214,24 +221,21 @@ def tile_moe_pre_lin_relu2_kernel(
             h, c0 = divmod(s0, HALF)
             scale_weave(nc.vector, woven_sb[:, at : at + n, :], planes, gate_ps[h][:, c0 : c0 + n])
 
-        def share(k):
-            return CHUNK - FIRST_OWN if k == 0 else SHARE if k < 6 else SHARE6 if k == 6 else SHARE7
-
         def own(k):
             a, c = STEPS[k]
             for c0, c1 in ((share(k), HALF), (max(share(k), HALF), CHUNK)):
                 if c0 < c1:
-                    weave_vector(rooms[k][:, :, c0:c1], c * CHUNK + c0, c0, c1 - c0)
+                    weave_vector(rooms[k][:, :, c0:c1], c * CHUNK + c0, place(k) + c0, c1 - c0)
 
         def shared(k):
             a, c = STEPS[k]
             c0, c1 = 0 if k else LEAD, share(k)
-            scale_weave(nc.gpsimd, woven_sb[:, c0:c1, :], rooms[k][:, :, c0:c1], gate_sb[c][:, c0:c1])
+            scale_weave(nc.gpsimd, woven_sb[:, place(k) + c0 : place(k) + c1, :], rooms[k][:, :, c0:c1], gate_sb[c][:, c0:c1])
 
         def quantise_step(k):
             a, c = STEPS[k]
             for c0, c1 in CUTS:
-                quantise(a, c * CHUNK + c0, c0, c1 - c0)
+                quantise(a, c * CHUNK + c0, place(k) + c0, c1 - c0)
             if k != 2:
                 multiply(a, 8 * c, min(8 * c + 8, 20))
 
@@ -259,7 +263,7 @@ def tile_moe_pre_lin_relu2_kernel(
             else:
                 gather("scalar", rooms[0], 0, 0, t, 0, HALF)
             gather("vector", rooms[0], 0, 0, t, HALF, CHUNK)
-        scale_weave(nc.gpsimd, woven_sb[:, 0:LEAD, :], rooms[0][:, :, 0:LEAD], gate_lead[:])
+        scale_weave(nc.gpsimd, woven_sb[:, place(0) : place(0) + LEAD, :], rooms[0][:, :, 0:LEAD], gate_lead[:])
         for c in (1, 2, 0):
             spread_gate(2 * c + 1, f"gates{c}")
         spread_gate(4, "gates3")
@@ -285,7 +289,7 @@ def tile_moe_pre_lin_relu2_kernel(
                 multiply(0, 20, 22)
         multiply(1, 20, 22)
         lower, upper = rooms[last + 1], rooms[last + 2]
-        at = HALF + C - HALF // 2 - OVER8
+        at = HALF - SHARE8
         scale_weave(nc.gpsimd, woven_sb[:, at : at + SHARE8, :], lower[:, :, 0:SHARE8], gate_sb[2][:, 0:SHARE8])
         fetch_end(last + 3, *ENDS[2])
         weave_vector(lower[:, :, SHARE8:HALF], s8 + SHARE8, at + SHARE8, HALF - SHARE8)

@@ -31,7 +31,7 @@ CHUNK = 1024
 GROUP = CHUNK // C * PASSES
 HALF = CHUNK // 2
 STEPS = ((0, 0), (0, 1), (0, 2), (1, 0), (1, 1), (2, 0), (2, 1), (1, 2))
-SHARE = 528
+SHARE = 520
 EXTRA = 96
 EXTRA_HEAD = 896
 CUTS = ((0, HALF), (HALF, CHUNK))
@@ -44,7 +44,7 @@ SHARE8 = 264
 LEAD = 64
 FIRST_OWN = 0
 SHARE6 = 520
-SHARE7 = 336
+SHARE7 = 320
 LAST_SHARE = 160
 ALONE = 192
 MID, END = 608, 896
@@ -296,33 +296,29 @@ def tile_moe_pre_lin_relu2_kernel(
         for e0 in (16, 18):
             quantise(2, e0 * C, at + (e0 - 16) * C, 2 * C)
         multiply(2, 16, 20)
-        for e0 in (0, 8, 12):
-            relu(e0, e0 + 4)
-        for e0 in (0, 8, 12):
-            square(e0 * C, e0 * C + HALF)
+        relu(0, 16)
+        for e0, e1 in ((0, 3), (3, 7), (7, 11), (11, 15)):
+            square(e0 * C, e1 * C)
         open_bank(22, 23, "bank0")
-        open_bank(23, 24, "bank2")
+        open_bank(23, 24, "bank1")
         for a in range(2):
             multiply(a, 22, 24)
         at = at + HALF // 2 - LAST_SHARE
         scale_weave(nc.gpsimd, woven_sb[:, at : at + LAST_SHARE, :], upper[:, :, 0:LAST_SHARE], gate_sb[2][:, HALF : HALF + LAST_SHARE])
-        late = room(last + 1, [P, HALF])
-        for e in range(4, 8):
-            nc.scalar.activation(late[:, (e - 4) * C : (e - 3) * C], banks[e], ACT.Relu, bias=bias_sb[:, e : e + 1])
         weave_vector(upper[:, :, LAST_SHARE : 3 * C], s8 + HALF + LAST_SHARE, at + LAST_SHARE, 3 * C - LAST_SHARE)
         weave_vector(rooms[last + 3][:], S - C, at + 3 * C, C)
         relu(16, 20)
-        square(s8, s8 + HALF)
+        square(15 * C, 19 * C)
         for e0, e1 in ((20, 22), (22, 23), (23, 24)):
             quantise(2, e0 * C, at + (e0 - 20) * C, (e1 - e0) * C)
             multiply(2, e0, e1)
-        nc.vector.tensor_tensor(y_sb[:, HALF:CHUNK], late[:], late[:], MULT)
-        for e in (20, 21, 23):
+        relu(20, 22)
+        square(19 * C, 21 * C)
+        square(21 * C, 22 * C)
+        for e in (22, 23):
             relu_vector(y_sb[:, e * C : (e + 1) * C], e)
-        relu(22, 23)
-        square(22 * C, 23 * C)
-        square_vector(20 * C, 22 * C)
-        square_vector(S - C, S)
+        for e in (22, 23):
+            square_vector(e * C, (e + 1) * C)
 
         picked = room(last + 1, [P, PACK, T])
         first, second, pair, total = (picked[:, r, :] for r in range(PACK))

@@ -31,19 +31,19 @@ CHUNK = 1024
 GROUP = CHUNK // C * PASSES
 HALF = CHUNK // 2
 STEPS = ((0, 0), (0, 1), (0, 2), (1, 0), (1, 1), (2, 0), (2, 1), (1, 2))
-SHARE = 520
+SHARE = 536
 EXTRA = 96
-EXTRA_HEAD = 896
+EXTRA_HEAD = 864
 CUTS = ((0, HALF), (HALF, CHUNK))
 FIN0 = 6
 TAIL_C = 512
 TAIL_A = 1024
 TAIL_B = 0
 ENDS = ((2 * CHUNK, HALF, TAIL_A), (2 * CHUNK + HALF, 3 * C, TAIL_B), (S - C, C, TAIL_C))
-SHARE8 = 264
-LEAD = 64
+SHARE8 = 272
+LEAD = 128
 FIRST_OWN = 0
-SHARE6 = 520
+SHARE6 = 536
 SHARE7 = 320
 LAST_SHARE = 160
 ALONE = 192
@@ -230,7 +230,8 @@ def tile_moe_pre_lin_relu2_kernel(
         def shared(k):
             a, c = STEPS[k]
             c0, c1 = 0 if k else LEAD, share(k)
-            scale_weave(nc.gpsimd, woven_sb[:, place(k) + c0 : place(k) + c1, :], rooms[k][:, :, c0:c1], gate_sb[c][:, c0:c1])
+            for b0, b1 in ((c0, HALF), (HALF, c1)) if 0 < k < 7 else ((c0, c1),):
+                scale_weave(nc.gpsimd, woven_sb[:, place(k) + b0 : place(k) + b1, :], rooms[k][:, :, b0:b1], gate_sb[c][:, b0:b1])
 
         def quantise_step(k):
             a, c = STEPS[k]
@@ -290,14 +291,15 @@ def tile_moe_pre_lin_relu2_kernel(
         multiply(1, 20, 22)
         lower, upper = rooms[last + 1], rooms[last + 2]
         at = HALF - SHARE8
-        scale_weave(nc.gpsimd, woven_sb[:, at : at + SHARE8, :], lower[:, :, 0:SHARE8], gate_sb[2][:, 0:SHARE8])
+        for b0, b1 in ((0, HALF // 2), (HALF // 2, SHARE8)):
+            scale_weave(nc.gpsimd, woven_sb[:, at + b0 : at + b1, :], lower[:, :, b0:b1], gate_sb[2][:, b0:b1])
         fetch_end(last + 3, *ENDS[2])
         weave_vector(lower[:, :, SHARE8:HALF], s8 + SHARE8, at + SHARE8, HALF - SHARE8)
         for e0 in (16, 18):
             quantise(2, e0 * C, at + (e0 - 16) * C, 2 * C)
         multiply(2, 16, 20)
-        relu(0, 16)
-        for e0, e1 in ((0, 3), (3, 7), (7, 11), (11, 15)):
+        relu(0, 12)
+        for e0, e1 in ((0, 3), (3, 7), (7, 11)):
             square(e0 * C, e1 * C)
         open_bank(22, 23, "bank0")
         open_bank(23, 24, "bank1")
@@ -307,11 +309,16 @@ def tile_moe_pre_lin_relu2_kernel(
         scale_weave(nc.gpsimd, woven_sb[:, at : at + LAST_SHARE, :], upper[:, :, 0:LAST_SHARE], gate_sb[2][:, HALF : HALF + LAST_SHARE])
         weave_vector(upper[:, :, LAST_SHARE : 3 * C], s8 + HALF + LAST_SHARE, at + LAST_SHARE, 3 * C - LAST_SHARE)
         weave_vector(rooms[last + 3][:], S - C, at + 3 * C, C)
+        late = room(last + 1, [P, HALF])
+        for e in range(12, 16):
+            nc.scalar.activation(late[:, (e - 12) * C : (e - 11) * C], banks[e], ACT.Relu, bias=bias_sb[:, e : e + 1])
+        square(11 * C, 12 * C)
         relu(16, 20)
-        square(15 * C, 19 * C)
+        square(16 * C, 19 * C)
         for e0, e1 in ((20, 22), (22, 23), (23, 24)):
             quantise(2, e0 * C, at + (e0 - 20) * C, (e1 - e0) * C)
             multiply(2, e0, e1)
+        nc.vector.tensor_tensor(y_sb[:, 12 * C : 16 * C], late[:], late[:], MULT)
         relu(20, 22)
         square(19 * C, 21 * C)
         square(21 * C, 22 * C)

@@ -31,7 +31,7 @@ CHUNK = 1024
 GROUP = CHUNK // C * PASSES
 HALF = CHUNK // 2
 STEPS = ((0, 0), (0, 1), (0, 2), (1, 0), (1, 1), (2, 0), (2, 1), (1, 2))
-SHARE = 536
+SHARE = 528
 EXTRA = 96
 EXTRA_HEAD = 864
 CUTS = ((0, HALF), (HALF, CHUNK))
@@ -40,10 +40,10 @@ TAIL_C = 512
 TAIL_A = 1024
 TAIL_B = 0
 ENDS = ((2 * CHUNK, HALF, TAIL_A), (2 * CHUNK + HALF, 3 * C, TAIL_B), (S - C, C, TAIL_C))
-SHARE8 = 272
-LEAD = 128
+SHARE8 = 264
+LEAD = 96
 FIRST_OWN = 0
-SHARE6 = 536
+SHARE6 = 520
 SHARE7 = 320
 LAST_SHARE = 160
 ALONE = 192

@@ -9,7 +9,6 @@ PACK = 4
 PASSES = K // (P * PACK)
 LANE = 16
 PAD = 16
-BANKS = 8
 
 FLOPS = 2 * K * N * S
 BYTES = 4 * K * T + E * K * N // 2 + E * K * N // 32 + 4 * N * E + 4 * S + 2 * P * (S + 3 * T) // LANE + 4 * N * T
@@ -28,30 +27,28 @@ MAX = mybir.AluOpType.max
 ACT = mybir.ActivationFunctionType
 
 CHUNK = 1024
-GROUP = CHUNK // C * PASSES
+CHUNKS = S // CHUNK
 HALF = CHUNK // 2
+QUARTER = HALF // 2
+PER_CHUNK = CHUNK // C
+PER_BANK = HALF // C
+GROUP = PER_CHUNK * PASSES
 STEPS = ((0, 0), (0, 1), (0, 2), (1, 0), (1, 1), (2, 0), (2, 1), (1, 2))
+LAST = len(STEPS) - 1
 SHARE = 528
+SHARE_LAST = 320
+OVER = 8
+SHARE_LOWER = QUARTER + OVER
+SHARE_UPPER = 160
+LEAD = C
 EXTRA = 96
 EXTRA_HEAD = 864
-CUTS = ((0, HALF), (HALF, CHUNK))
-FIN0 = 6
-TAIL_C = 512
-TAIL_A = 1024
-TAIL_B = 0
-ENDS = ((2 * CHUNK, HALF, TAIL_A), (2 * CHUNK + HALF, 3 * C, TAIL_B), (S - C, C, TAIL_C))
-SHARE8 = 264
-LEAD = 96
-FIRST_OWN = 0
-SHARE6 = 520
-SHARE7 = 320
-LAST_SHARE = 160
 ALONE = 192
 MID, END = 608, 896
 
 
 def share(k):
-    return CHUNK - FIRST_OWN if k == 0 else SHARE if k < 6 else SHARE6 if k == 6 else SHARE7
+    return CHUNK if k == 0 else SHARE_LAST if k == LAST else SHARE
 
 
 def place(k):
@@ -69,13 +66,13 @@ def tile_moe_pre_lin_relu2_kernel(
 
         offs_sb = keep.tile([P, S // LANE], U16, name="offs_sb")
         pos_sb = [keep.tile([P, T // LANE], U16, name=f"pos_sb{r}") for r in range(3)]
-        gate_sb = [keep.tile([P, CHUNK], F32, name=f"gate_sb{c}") for c in range(S // CHUNK)]
+        gate_sb = [keep.tile([P, CHUNK], F32, name=f"gate_sb{c}") for c in range(CHUNKS)]
         gate_cols = keep.tile([P, S // P], F32, name="gate_cols")
         identity = keep.tile([P, P], F32, name="identity")
         bias_sb = keep.tile([P, E], F32, name="bias_sb")
         x_sb = [[keep.tile([P, T + PAD], F32, name=f"x_sb{a}_{t}") for t in range(PACK)] for a in range(PASSES)]
         woven_sb = keep.tile([P, CHUNK + place(0), PACK], BF16, name="woven_sb", align_bytes=64)
-        w_sb = [keep.tile([P, GROUP, 2 * N], U8, name=f"w_sb{c}", align_bytes=64) for c in range(S // CHUNK)]
+        w_sb = [keep.tile([P, GROUP, 2 * N], U8, name=f"w_sb{c}", align_bytes=64) for c in range(CHUNKS)]
         ws_sb = keep.tile([P, E * PASSES, N], U8, name="ws_sb", align_bytes=64)
         codes = [keep.tile([P, S], U32, name=f"codes{a}", align_bytes=64) for a in range(PASSES)]
         scales = [keep.tile([P, S], U8, name=f"scales{a}", align_bytes=64) for a in range(PASSES)]
@@ -83,14 +80,6 @@ def tile_moe_pre_lin_relu2_kernel(
 
         def room(k, shape):
             return stage.tile(shape, F32, name=f"room{k % 3}")
-
-        x_rows = xT.rearrange("(a p t) c -> a t p c", p=P, t=PACK)
-
-        def load_x(a, t):
-            nc.sync.dma_start(out=x_sb[a][t][:, 0:T], in_=x_rows[a, t])
-
-        def load_gate(c, s0, s1):
-            nc.sync.dma_start(out=gate_sb[c][:, s0:s1], in_=gate[0:P, c * CHUNK + s0 : c * CHUNK + s1])
 
         warm = keep.tile([P, 2], F32, name="warm")
         nc.vector.memset(warm[:, 0:1], 0.0)
@@ -103,33 +92,40 @@ def tile_moe_pre_lin_relu2_kernel(
         nc.vector.tensor_tensor_scan(column, ones, ones, 0.0, MULT, ADD)
         nc.vector.transpose(across, column)
         for q in range(0, P, 32):
-            nc.vector.tensor_tensor(identity[q : q + 32, q : q + 32], across[q : q + 32, q : q + 32], column[q : q + 32, q : q + 32], mybir.AluOpType.is_equal)
-
+            block = slice(q, q + 32)
+            nc.vector.tensor_tensor(
+                identity[block, block], across[block, block], column[block, block], mybir.AluOpType.is_equal
+            )
 
         nc.vector.memset(ws_sb[:].rearrange("p g n -> p (g n)").bitcast(I32), 0)
 
+        x_rows = xT.rearrange("(a p t) c -> a t p c", p=P, t=PACK)
+
+        def load_pass(a):
+            for t in range(PACK):
+                nc.sync.dma_start(out=x_sb[a][t][:, 0:T], in_=x_rows[a, t])
+
+        def load_gate(c, s0, s1):
+            nc.sync.dma_start(out=gate_sb[c][:, s0:s1], in_=gate[0:P, c * CHUNK + s0 : c * CHUNK + s1])
+
         nc.sync.dma_start(offs_sb[:], offs)
-        for t in range(PACK):
-            load_x(0, t)
+        load_pass(0)
         gate_rows = room(1, [P, P])
         nc.sync.dma_start(out=gate_rows[:], in_=gate.rearrange("k (g j) -> (k g) j", j=P)[0:P, :])
         gate_lead = room(2, [P, LEAD])
         nc.sync.dma_start(out=gate_lead[:], in_=gate[0:P, 0:LEAD])
-        load_gate(0, LEAD, CHUNK - FIRST_OWN)
-        for t in range(PACK):
-            load_x(1, t)
-        ws_rows = w_scales.rearrange("e a (q r) n -> q r (e a) n", r=4)
-        w_rows = w_words.rearrange("e a p m -> p (e a) m")
-
+        load_gate(0, LEAD, CHUNK)
+        load_pass(1)
         load_gate(1, 0, SHARE)
-        for t in range(PACK):
-            load_x(2, t)
-        load_gate(2, 0, HALF + LAST_SHARE)
+        load_pass(2)
+        load_gate(2, 0, HALF + SHARE_UPPER)
         load_gate(0, 0, LEAD)
         nc.sync.dma_start(out=bias_sb[:], in_=b)
+        ws_rows = w_scales.rearrange("e a (q r) n -> q r (e a) n", r=4)
         for q in range(4):
             nc.sync.dma_start(out=ws_sb[32 * q : 32 * q + 4].bitcast(I32), in_=ws_rows[q].bitcast(I32))
-        for c in range(S // CHUNK):
+        w_rows = w_words.rearrange("e a p m -> p (e a) m")
+        for c in range(CHUNKS):
             nc.sync.dma_start(out=w_sb[c][:].bitcast(I32), in_=w_rows[:, c * GROUP : (c + 1) * GROUP, :].bitcast(I32))
         for r, pos in enumerate((pos1, pos2, pos3)):
             nc.sync.dma_start(pos_sb[r][:], pos)
@@ -137,25 +133,21 @@ def tile_moe_pre_lin_relu2_kernel(
         def window(a, t, s0, s1):
             return x_sb[a][t][:].indirect(offs_sb[:, s0 // LANE : s1 // LANE])
 
-        def gather(engine, planes, a, s0, t, c0, c1):
-            if c0 < c1:
-                if engine == "scalar":
-                    nc.scalar.activation(planes[:, t, c0:c1], window(a, t, s0 + c0, s0 + c1), ACT.Copy)
-                else:
-                    nc.vector.tensor_copy(planes[:, t, c0:c1], window(a, t, s0 + c0, s0 + c1))
+        def gather_scalar(planes, a, s0, t, c0, c1):
+            nc.scalar.activation(planes[:, t, c0:c1], window(a, t, s0 + c0, s0 + c1), ACT.Copy)
 
-        def scale_weave(engine, woven, planes, gates):
-            w = planes.shape[2]
+        def gather_vector(planes, a, s0, t, c0, c1):
+            nc.vector.tensor_copy(planes[:, t, c0:c1], window(a, t, s0 + c0, s0 + c1))
+
+        def scale_weave(engine, at, planes, gates):
+            n = planes.shape[2]
             engine.tensor_tensor(
-                woven.rearrange("p (c i) t -> p c t i", i=4),
+                woven_sb[:, at : at + n, :].rearrange("p (c i) t -> p c t i", i=4),
                 planes.rearrange("p t (c i) -> p c t i", i=4),
-                gates.rearrange("p (c o i) -> p c o i", o=1, i=4).to_broadcast([P, w // 4, PACK, 4]),
+                gates.rearrange("p (c o i) -> p c o i", o=1, i=4).to_broadcast([P, n // 4, PACK, 4]),
                 MULT,
             )
 
-        turned = psum.tile([P, HALF], F32, name="gates0")
-        nc.tensor.transpose(turned[:, 0:P], gate_rows[:], identity[:])
-        nc.vector.tensor_copy(gate_cols[:], turned[:, 0 : S // P])
         gate_ps = {}
 
         def spread_gate(h, bank):
@@ -166,13 +158,21 @@ def tile_moe_pre_lin_relu2_kernel(
                     gate_ps[h][:, j * P : (j + 1) * P], gate_cols[:, g : g + 1].to_broadcast([P, P]), identity[:]
                 )
 
-        banks = {}
+        def weave_vector(at, planes, s0):
+            h, c0 = divmod(s0, HALF)
+            scale_weave(nc.vector, at, planes, gate_ps[h][:, c0 : c0 + planes.shape[2]])
+
+        def weave_gpsimd(at, planes, gates, cuts):
+            for c0, c1 in cuts:
+                scale_weave(nc.gpsimd, at + c0, planes[:, :, c0:c1], gates[:, c0:c1])
+
+        sums = {}
         opens, closes = set(), set()
 
-        def open_bank(e0, e1, at):
-            bank = psum.tile([N, HALF], F32, name=at)
+        def open_bank(e0, e1, bank):
+            tile = psum.tile([N, HALF], F32, name=bank)
             for e in range(e0, e1):
-                banks[e] = bank[:, (e - e0) * C : (e - e0 + 1) * C]
+                sums[e] = tile[:, (e - e0) * C : (e - e0 + 1) * C]
             opens.add(e0)
             closes.add(e1 - 1)
 
@@ -187,7 +187,7 @@ def tile_moe_pre_lin_relu2_kernel(
             for e in range(e0, e1):
                 c, g = divmod(e * PASSES + a, GROUP)
                 nc.tensor.matmul_mx(
-                    out=banks[e],
+                    out=sums[e],
                     lhsT=w_sb[c][:, g, :].bitcast(FP4X4),
                     lhsT_scale=ws_sb[:, e * PASSES + a, :],
                     rhs=codes[a][:, e * C : (e + 1) * C].bitcast(FP8X4),
@@ -196,138 +196,137 @@ def tile_moe_pre_lin_relu2_kernel(
                     stop=(a == PASSES - 1 and e in closes),
                 )
 
+        def relu_scalar(into, e):
+            nc.scalar.activation(into, sums[e], ACT.Relu, bias=bias_sb[:, e : e + 1])
+
+        def y_of(e0, e1):
+            return y_sb[:, e0 * C : e1 * C]
+
+        def square_scalar(e0, e1):
+            nc.scalar.activation(y_of(e0, e1), y_of(e0, e1), ACT.Square)
+
         rooms = {}
 
         def fetch(k, extra):
             a, c = STEPS[k]
             rooms[k] = room(k, [P, PACK, CHUNK])
-            gather("vector", rooms[k], a, c * CHUNK, 0, 0, CHUNK)
-            gather("scalar", rooms[k], a, c * CHUNK, 1, extra, CHUNK)
+            gather_vector(rooms[k], a, c * CHUNK, 0, 0, CHUNK)
+            gather_scalar(rooms[k], a, c * CHUNK, 1, extra, CHUNK)
             for t in (2, 3):
-                gather("scalar", rooms[k], a, c * CHUNK, t, 0, CHUNK)
+                gather_scalar(rooms[k], a, c * CHUNK, t, 0, CHUNK)
 
         def fetch_extra(k, extra):
             a, c = STEPS[k]
-            gather("vector", rooms[k], a, c * CHUNK, 1, 0, extra)
+            gather_vector(rooms[k], a, c * CHUNK, 1, 0, extra)
 
-        def fetch_end(k, s0, n, mine):
-            rooms[k] = room(k, [P, PACK, n])
-            for t in range(PACK):
-                cut = min(max(mine - t * n, 0), n)
-                gather("vector", rooms[k], 2, s0, t, 0, cut)
-                gather("scalar", rooms[k], 2, s0, t, cut, n)
-
-        def weave_vector(planes, s0, at, n):
-            h, c0 = divmod(s0, HALF)
-            scale_weave(nc.vector, woven_sb[:, at : at + n, :], planes, gate_ps[h][:, c0 : c0 + n])
-
-        def own(k):
-            a, c = STEPS[k]
-            for c0, c1 in ((share(k), HALF), (max(share(k), HALF), CHUNK)):
-                if c0 < c1:
-                    weave_vector(rooms[k][:, :, c0:c1], c * CHUNK + c0, place(k) + c0, c1 - c0)
-
-        def shared(k):
-            a, c = STEPS[k]
-            c0, c1 = 0 if k else LEAD, share(k)
-            for b0, b1 in ((c0, HALF), (HALF, c1)) if 0 < k < 7 else ((c0, c1),):
-                scale_weave(nc.gpsimd, woven_sb[:, place(k) + b0 : place(k) + b1, :], rooms[k][:, :, b0:b1], gate_sb[c][:, b0:b1])
-
-        def quantise_step(k):
-            a, c = STEPS[k]
-            for c0, c1 in CUTS:
-                quantise(a, c * CHUNK + c0, place(k) + c0, c1 - c0)
-            if k != 2:
-                multiply(a, 8 * c, min(8 * c + 8, 20))
-
-        def relu(e0, e1):
-            for e in range(e0, e1):
-                nc.scalar.activation(y_sb[:, e * C : (e + 1) * C], banks[e], ACT.Relu, bias=bias_sb[:, e : e + 1])
-
-        def relu_vector(into, e):
-            nc.vector.tensor_scalar(into, banks[e], bias_sb[:, e : e + 1], 0.0, ADD, MAX)
-
-        def square(s0, s1):
-            nc.scalar.activation(y_sb[:, s0:s1], y_sb[:, s0:s1], ACT.Square)
-
-        def square_vector(s0, s1):
-            nc.vector.tensor_tensor(y_sb[:, s0:s1], y_sb[:, s0:s1], y_sb[:, s0:s1], MULT)
-
-        for at in range(4):
-            open_bank(4 * at, 4 * at + 4, f"bank{at}")
+        lower0 = 2 * PER_CHUNK
+        upper0 = lower0 + PER_BANK
+        final = E - 1
+        for i in range(lower0 // PER_BANK):
+            open_bank(i * PER_BANK, (i + 1) * PER_BANK, f"bank{i}")
 
         rooms[0] = room(0, [P, PACK, CHUNK])
         for t in range(PACK):
-            if t == PACK - 1:
-                gather("scalar", rooms[0], 0, 0, t, 0, LEAD)
-                gather("scalar", rooms[0], 0, 0, t, LEAD, HALF)
-            else:
-                gather("scalar", rooms[0], 0, 0, t, 0, HALF)
-            gather("vector", rooms[0], 0, 0, t, HALF, CHUNK)
-        scale_weave(nc.gpsimd, woven_sb[:, place(0) : place(0) + LEAD, :], rooms[0][:, :, 0:LEAD], gate_lead[:])
+            for c0, c1 in ((0, LEAD), (LEAD, HALF)) if t == PACK - 1 else ((0, HALF),):
+                gather_scalar(rooms[0], 0, 0, t, c0, c1)
+            gather_vector(rooms[0], 0, 0, t, HALF, CHUNK)
+
+        turned = psum.tile([P, HALF], F32, name="gates0")
+        nc.tensor.transpose(turned[:, 0:P], gate_rows[:], identity[:])
+        for h0, h1 in ((1, 2), (3, 6)):
+            used = slice(h0 * HALF // P, h1 * HALF // P)
+            nc.vector.tensor_copy(gate_cols[:, used], turned[:, used])
+        scale_weave(nc.gpsimd, place(0), rooms[0][:, :, 0:LEAD], gate_lead[:])
         for c in (1, 2, 0):
             spread_gate(2 * c + 1, f"gates{c}")
         spread_gate(4, "gates3")
+
         fetch(1, EXTRA_HEAD)
         fetch_extra(1, EXTRA_HEAD)
-        last = len(STEPS) - 1
-        s8 = 2 * CHUNK
-        for k in range(len(STEPS)):
-            shared(k)
-            if k + 2 <= last:
-                fetch(k + 2, EXTRA_HEAD if k == 0 else EXTRA)
+        for k, (a, c) in enumerate(STEPS):
+            if k == 0:
+                cuts = ((LEAD, CHUNK),)
+            elif k == LAST:
+                cuts = ((0, SHARE_LAST),)
             else:
-                fetch_end(k + 2, *ENDS[k + 1 - last])
-            own(k)
-            if k + 2 <= last:
-                fetch_extra(k + 2, EXTRA_HEAD if k == 0 else EXTRA)
-            quantise_step(k)
-            if k == 5:
-                open_bank(16, 20, "gates0")
-                multiply(0, 16, 20)
-            if k == 6:
-                open_bank(20, 22, "gates1")
-                multiply(0, 20, 22)
-        multiply(1, 20, 22)
-        lower, upper = rooms[last + 1], rooms[last + 2]
-        at = HALF - SHARE8
-        for b0, b1 in ((0, HALF // 2), (HALF // 2, SHARE8)):
-            scale_weave(nc.gpsimd, woven_sb[:, at + b0 : at + b1, :], lower[:, :, b0:b1], gate_sb[2][:, b0:b1])
-        fetch_end(last + 3, *ENDS[2])
-        weave_vector(lower[:, :, SHARE8:HALF], s8 + SHARE8, at + SHARE8, HALF - SHARE8)
-        for e0 in (16, 18):
-            quantise(2, e0 * C, at + (e0 - 16) * C, 2 * C)
-        multiply(2, 16, 20)
-        relu(0, 12)
-        for e0, e1 in ((0, 3), (3, 7), (7, 11)):
-            square(e0 * C, e1 * C)
-        open_bank(22, 23, "bank0")
-        open_bank(23, 24, "bank1")
-        for a in range(2):
-            multiply(a, 22, 24)
-        at = at + HALF // 2 - LAST_SHARE
-        scale_weave(nc.gpsimd, woven_sb[:, at : at + LAST_SHARE, :], upper[:, :, 0:LAST_SHARE], gate_sb[2][:, HALF : HALF + LAST_SHARE])
-        weave_vector(upper[:, :, LAST_SHARE : 3 * C], s8 + HALF + LAST_SHARE, at + LAST_SHARE, 3 * C - LAST_SHARE)
-        weave_vector(rooms[last + 3][:], S - C, at + 3 * C, C)
-        late = room(last + 1, [P, HALF])
-        for e in range(12, 16):
-            nc.scalar.activation(late[:, (e - 12) * C : (e - 11) * C], banks[e], ACT.Relu, bias=bias_sb[:, e : e + 1])
-        square(11 * C, 12 * C)
-        relu(16, 20)
-        square(16 * C, 19 * C)
-        for e0, e1 in ((20, 22), (22, 23), (23, 24)):
-            quantise(2, e0 * C, at + (e0 - 20) * C, (e1 - e0) * C)
-            multiply(2, e0, e1)
-        nc.vector.tensor_tensor(y_sb[:, 12 * C : 16 * C], late[:], late[:], MULT)
-        relu(20, 22)
-        square(19 * C, 21 * C)
-        square(21 * C, 22 * C)
-        for e in (22, 23):
-            relu_vector(y_sb[:, e * C : (e + 1) * C], e)
-        for e in (22, 23):
-            square_vector(e * C, (e + 1) * C)
+                cuts = ((0, HALF), (HALF, SHARE))
+            weave_gpsimd(place(k), rooms[k], gate_sb[c], cuts)
+            extra = EXTRA_HEAD if k == 0 else EXTRA
+            if k + 2 <= LAST:
+                fetch(k + 2, extra)
+            elif k + 1 == LAST:
+                lower = room(k + 2, [P, PACK, HALF])
+                for t in (0, 1):
+                    gather_vector(lower, 2, lower0 * C, t, 0, HALF)
+                gather_vector(lower, 2, lower0 * C, 2, 0, EXTRA)
+                gather_scalar(lower, 2, lower0 * C, 2, EXTRA, HALF)
+                gather_scalar(lower, 2, lower0 * C, 3, 0, HALF)
+            else:
+                upper = room(k + 2, [P, PACK, (final - upper0) * C])
+                for t in range(PACK):
+                    gather_scalar(upper, 2, upper0 * C, t, 0, (final - upper0) * C)
+            if k == LAST:
+                weave_vector(SHARE_LAST, rooms[k][:, :, SHARE_LAST:HALF], c * CHUNK + SHARE_LAST)
+            if k:
+                c0 = max(share(k), HALF)
+                weave_vector(place(k) + c0, rooms[k][:, :, c0:CHUNK], c * CHUNK + c0)
+            if k + 2 <= LAST:
+                fetch_extra(k + 2, extra)
+            for c0 in (0, HALF):
+                quantise(a, c * CHUNK + c0, place(k) + c0, HALF)
+            if c < 2:
+                multiply(a, c * PER_CHUNK, (c + 1) * PER_CHUNK)
+                if a == PASSES - 1:
+                    e0, e1 = (upper0, upper0 + 2) if c else (lower0, upper0)
+                    open_bank(e0, e1, f"gates{c}")
+                    multiply(0, e0, e1)
+        multiply(1, lower0, upper0 + 2)
 
-        picked = room(last + 1, [P, PACK, T])
+        at = HALF - SHARE_LOWER
+        weave_gpsimd(at, lower, gate_sb[2], ((0, QUARTER), (QUARTER, SHARE_LOWER)))
+        third = room(LAST, [P, PACK, C])
+        for t in range(PACK):
+            gather_vector(third, 2, final * C, t, 0, C)
+        weave_vector(at + SHARE_LOWER, lower[:, :, SHARE_LOWER:HALF], lower0 * C + SHARE_LOWER)
+        for c0 in (0, QUARTER):
+            quantise(2, lower0 * C + c0, at + c0, QUARTER)
+        multiply(2, lower0, upper0)
+
+        late0 = lower0 - PER_BANK
+        for e in range(late0):
+            relu_scalar(y_of(e, e + 1), e)
+        for e1 in range(PER_BANK - 1, late0, PER_BANK):
+            square_scalar(max(e1 - PER_BANK, 0), e1)
+        open_bank(final - 1, final, "bank0")
+        open_bank(final, E, "bank1")
+        for a in range(PASSES - 1):
+            multiply(a, final - 1, E)
+
+        at = at + QUARTER - SHARE_UPPER
+        weave_gpsimd(at, upper, gate_sb[2][:, HALF:CHUNK], ((0, SHARE_UPPER),))
+        weave_vector(at + SHARE_UPPER, upper[:, :, SHARE_UPPER : (final - upper0) * C], upper0 * C + SHARE_UPPER)
+        weave_vector(at + (final - upper0) * C, third[:], final * C)
+        late = room(LAST + 1, [P, HALF])
+        for e in range(late0, lower0):
+            relu_scalar(late[:, (e - late0) * C : (e - late0 + 1) * C], e)
+        square_scalar(late0 - 1, late0)
+        for e in range(lower0, upper0):
+            relu_scalar(y_of(e, e + 1), e)
+        square_scalar(lower0, upper0 - 1)
+        for e0, e1 in ((upper0, final - 1), (final - 1, final), (final, E)):
+            quantise(2, e0 * C, at + (e0 - upper0) * C, (e1 - e0) * C)
+            multiply(2, e0, e1)
+        nc.vector.tensor_tensor(y_of(late0, lower0), late[:], late[:], MULT)
+        for e in range(upper0, final - 1):
+            relu_scalar(y_of(e, e + 1), e)
+        square_scalar(upper0 - 1, upper0 + 1)
+        square_scalar(upper0 + 1, final - 1)
+        for e in (final - 1, final):
+            nc.vector.tensor_scalar(y_of(e, e + 1), sums[e], bias_sb[:, e : e + 1], 0.0, ADD, MAX)
+        for e in (final - 1, final):
+            nc.vector.tensor_tensor(y_of(e, e + 1), y_of(e, e + 1), y_of(e, e + 1), MULT)
+
+        picked = room(LAST + 1, [P, PACK, T])
         first, second, pair, total = (picked[:, r, :] for r in range(PACK))
 
         def results(r, c0, c1):

@@ -35,14 +35,14 @@ PER_BANK = HALF // C
 GROUP = PER_CHUNK * PASSES
 STEPS = ((0, 0), (0, 1), (0, 2), (1, 0), (1, 1), (2, 0), (2, 1), (1, 2))
 LAST = len(STEPS) - 1
-SHARE = 528
+SHARE = 536
 SHARE_LAST = 320
 OVER = 8
 SHARE_LOWER = QUARTER + OVER
 SHARE_UPPER = 160
-LEAD = C
-EXTRA = 96
-EXTRA_HEAD = 864
+LEAD = 384
+EXTRA = 160
+EXTRA_HEAD = 704
 ALONE = 192
 MID, END = 608, 896
 
@@ -109,11 +109,13 @@ def tile_moe_pre_lin_relu2_kernel(
             nc.sync.dma_start(out=gate_sb[c][:, s0:s1], in_=gate[0:P, c * CHUNK + s0 : c * CHUNK + s1])
 
         nc.sync.dma_start(offs_sb[:], offs)
-        load_pass(0)
+        gate_lead = room(2, [P, LEAD])
+        for t in range(PACK):
+            if t == 2:
+                nc.sync.dma_start(out=gate_lead[:], in_=gate[0:P, 0:LEAD])
+            nc.sync.dma_start(out=x_sb[0][t][:, 0:T], in_=x_rows[0, t])
         gate_rows = room(1, [P, P])
         nc.sync.dma_start(out=gate_rows[:], in_=gate.rearrange("k (g j) -> (k g) j", j=P)[0:P, :])
-        gate_lead = room(2, [P, LEAD])
-        nc.sync.dma_start(out=gate_lead[:], in_=gate[0:P, 0:LEAD])
         load_gate(0, LEAD, CHUNK)
         load_pass(1)
         load_gate(1, 0, SHARE)
@@ -139,12 +141,12 @@ def tile_moe_pre_lin_relu2_kernel(
         def gather_vector(planes, a, s0, t, c0, c1):
             nc.vector.tensor_copy(planes[:, t, c0:c1], window(a, t, s0 + c0, s0 + c1))
 
-        def scale_weave(engine, at, planes, gates):
-            n = planes.shape[2]
+        def scale_weave(engine, at, planes, gates, t0=0):
+            depth, n = planes.shape[1:]
             engine.tensor_tensor(
-                woven_sb[:, at : at + n, :].rearrange("p (c i) t -> p c t i", i=4),
+                woven_sb[:, at : at + n, t0 : t0 + depth].rearrange("p (c i) t -> p c t i", i=4),
                 planes.rearrange("p t (c i) -> p c t i", i=4),
-                gates.rearrange("p (c o i) -> p c o i", o=1, i=4).to_broadcast([P, n // 4, PACK, 4]),
+                gates.rearrange("p (c o i) -> p c o i", o=1, i=4).to_broadcast([P, n // 4, depth, 4]),
                 MULT,
             )
 
@@ -227,8 +229,7 @@ def tile_moe_pre_lin_relu2_kernel(
 
         rooms[0] = room(0, [P, PACK, CHUNK])
         for t in range(PACK):
-            for c0, c1 in ((0, LEAD), (LEAD, HALF)) if t == PACK - 1 else ((0, HALF),):
-                gather_scalar(rooms[0], 0, 0, t, c0, c1)
+            gather_scalar(rooms[0], 0, 0, t, 0, HALF)
             gather_vector(rooms[0], 0, 0, t, HALF, CHUNK)
 
         turned = psum.tile([P, HALF], F32, name="gates0")
@@ -236,7 +237,8 @@ def tile_moe_pre_lin_relu2_kernel(
         for h0, h1 in ((1, 2), (3, 6)):
             used = slice(h0 * HALF // P, h1 * HALF // P)
             nc.vector.tensor_copy(gate_cols[:, used], turned[:, used])
-        scale_weave(nc.gpsimd, place(0), rooms[0][:, :, 0:LEAD], gate_lead[:])
+        for t in (0, 2):
+            scale_weave(nc.gpsimd, place(0), rooms[0][:, t : t + 2, 0:LEAD], gate_lead[:], t)
         for c in (1, 2, 0):
             spread_gate(2 * c + 1, f"gates{c}")
         spread_gate(4, "gates3")

from contextlib import ExitStack

import concourse.mybir as mybir

K, T, E, C, N = 1536, 1024, 24, 128, 128
S = E * C
P = 128
PACK = 4
PASSES = K // (P * PACK)
LANE = 16
PAD = 16

FLOPS = 2 * K * N * S
BYTES = 4 * K * T + E * K * N // 2 + E * K * N // 32 + 4 * N * E + 4 * S + 2 * P * (S + 3 * T) // LANE + 4 * N * T

F32 = mybir.dt.float32
BF16 = mybir.dt.bfloat16
I32 = mybir.dt.int32
U32 = mybir.dt.uint32
U16 = mybir.dt.uint16
U8 = mybir.dt.uint8
FP8X4 = mybir.dt.float8_e4m3fn_x4
FP4X4 = mybir.dt.float4_e2m1fn_x4
MULT = mybir.AluOpType.mult
ADD = mybir.AluOpType.add
MAX = mybir.AluOpType.max
ACT = mybir.ActivationFunctionType

CHUNK = 1024
CHUNKS = S // CHUNK
HALF = CHUNK // 2
QUARTER = HALF // 2
PER_CHUNK = CHUNK // C
PER_BANK = HALF // C
GROUP = PER_CHUNK * PASSES
STEPS = ((0, 0), (0, 1), (0, 2), (1, 0), (1, 1), (2, 0), (2, 1), (1, 2))
LAST = len(STEPS) - 1
SHARE = 536
SHARE_LAST = 320
OVER = 8
SHARE_LOWER = QUARTER + OVER
SHARE_UPPER = 160
LEAD = 384
EXTRA = 160
EXTRA_HEAD = 704
ALONE = 192
MID, END = 608, 896


def share(k):
    return CHUNK if k == 0 else SHARE_LAST if k == LAST else SHARE


def place(k):
    return sum(max(share(j) - HALF, 0) for j in range(k + 1, len(STEPS)))


def tile_moe_pre_lin_relu2_kernel(
    tc, xT, w_words, w_scales, b, gate, offs, pos1, pos2, pos3, out
):
    nc = tc.nc
    with ExitStack() as ctx:
        keep = ctx.enter_context(tc.tile_pool(name="keep", bufs=1))
        stage = ctx.enter_context(tc.tile_pool(name="stage", bufs=1))
        psum = ctx.enter_context(tc.psum_pool(name="psum", bufs=1))

        offs_sb = keep.tile([P, S // LANE], U16, name="offs_sb")
        pos_sb = [keep.tile([P, T // LANE], U16, name=f"pos_sb{r}") for r in range(3)]
        gate_sb = [keep.tile([P, CHUNK], F32, name=f"gate_sb{c}") for c in range(CHUNKS)]
        gate_cols = keep.tile([P, S // P], F32, name="gate_cols")
        identity = keep.tile([P, P], F32, name="identity")
        bias_sb = keep.tile([P, E], F32, name="bias_sb")
        x_sb = [[keep.tile([P, T + PAD], F32, name=f"x_sb{a}_{t}") for t in range(PACK)] for a in range(PASSES)]
        woven_sb = keep.tile([P, CHUNK + place(0), PACK], BF16, name="woven_sb", align_bytes=64)
        w_sb = [keep.tile([P, GROUP, 2 * N], U8, name=f"w_sb{c}", align_bytes=64) for c in range(CHUNKS)]
        ws_sb = keep.tile([P, E * PASSES, N], U8, name="ws_sb", align_bytes=64)
        codes = [keep.tile([P, S], U32, name=f"codes{a}", align_bytes=64) for a in range(PASSES)]
        scales = [keep.tile([P, S], U8, name=f"scales{a}", align_bytes=64) for a in range(PASSES)]
        y_sb = keep.tile([P, S], F32, name="y_sb")

        def room(k, shape):
            return stage.tile(shape, F32, name=f"room{k % 3}")

        warm = keep.tile([P, 2], F32, name="warm")
        nc.vector.memset(warm[:, 0:1], 0.0)
        nc.scalar.activation(warm[:, 1:2], warm[:, 0:1], ACT.Copy)

        counting = keep.tile([P, 3 * P], F32, name="counting", align_bytes=64)
        ones, column, across = (counting[:, i * P : (i + 1) * P] for i in range(3))
        nc.vector.memset(ones, 1.0)
        nc.vector.memset(identity[:], 0.0)
        nc.vector.tensor_tensor_scan(column, ones, ones, 0.0, MULT, ADD)
        nc.vector.transpose(across, column)
        for q in range(0, P, 32):
            block = slice(q, q + 32)
            nc.vector.tensor_tensor(
                identity[block, block], across[block, block], column[block, block], mybir.AluOpType.is_equal
            )

        nc.vector.memset(ws_sb[:].rearrange("p g n -> p (g n)").bitcast(I32), 0)

        x_rows = xT.rearrange("(a p t) c -> a t p c", p=P, t=PACK)

        def load_pass(a):
            for t in range(PACK):
                nc.sync.dma_start(out=x_sb[a][t][:, 0:T], in_=x_rows[a, t])

        def load_gate(c, s0, s1):
            nc.sync.dma_start(out=gate_sb[c][:, s0:s1], in_=gate[0:P, c * CHUNK + s0 : c * CHUNK + s1])

        nc.sync.dma_start(offs_sb[:], offs)
        gate_lead = room(2, [P, LEAD])
        for t in range(PACK):
            if t == 2:
                nc.sync.dma_start(out=gate_lead[:], in_=gate[0:P, 0:LEAD])
            nc.sync.dma_start(out=x_sb[0][t][:, 0:T], in_=x_rows[0, t])
        gate_rows = room(1, [P, P])
        nc.sync.dma_start(out=gate_rows[:], in_=gate.rearrange("k (g j) -> (k g) j", j=P)[0:P, :])
        load_gate(0, LEAD, CHUNK)
        load_pass(1)
        load_gate(1, 0, SHARE)
        load_pass(2)
        load_gate(2, 0, HALF + SHARE_UPPER)
        load_gate(0, 0, LEAD)
        nc.sync.dma_start(out=bias_sb[:], in_=b)
        ws_rows = w_scales.rearrange("e a (q r) n -> q r (e a) n", r=4)
        for q in range(4):
            nc.sync.dma_start(out=ws_sb[32 * q : 32 * q + 4].bitcast(I32), in_=ws_rows[q].bitcast(I32))
        w_rows = w_words.rearrange("e a p m -> p (e a) m")
        for c in range(CHUNKS):
            nc.sync.dma_start(out=w_sb[c][:].bitcast(I32), in_=w_rows[:, c * GROUP : (c + 1) * GROUP, :].bitcast(I32))
        for r, pos in enumerate((pos1, pos2, pos3)):
            nc.sync.dma_start(pos_sb[r][:], pos)

        def window(a, t, s0, s1):
            return x_sb[a][t][:].indirect(offs_sb[:, s0 // LANE : s1 // LANE])

        def gather_scalar(planes, a, s0, t, c0, c1):
            nc.scalar.activation(planes[:, t, c0:c1], window(a, t, s0 + c0, s0 + c1), ACT.Copy)

        def gather_vector(planes, a, s0, t, c0, c1):
            nc.vector.tensor_copy(planes[:, t, c0:c1], window(a, t, s0 + c0, s0 + c1))

        def scale_weave(engine, at, planes, gates, t0=0):
            depth, n = planes.shape[1:]
            engine.tensor_tensor(
                woven_sb[:, at : at + n, t0 : t0 + depth].rearrange("p (c i) t -> p c t i", i=4),
                planes.rearrange("p t (c i) -> p c t i", i=4),
                gates.rearrange("p (c o i) -> p c o i", o=1, i=4).to_broadcast([P, n // 4, depth, 4]),
                MULT,
            )

        gate_ps = {}

        def spread_gate(h, bank):
            gate_ps[h] = psum.tile([P, HALF], F32, name=bank)
            for j in range(HALF // P):
                g = h * (HALF // P) + j
                nc.tensor.transpose(
                    gate_ps[h][:, j * P : (j + 1) * P], gate_cols[:, g : g + 1].to_broadcast([P, P]), identity[:]
                )

        def weave_vector(at, planes, s0):
            h, c0 = divmod(s0, HALF)
            scale_weave(nc.vector, at, planes, gate_ps[h][:, c0 : c0 + planes.shape[2]])

        def weave_gpsimd(at, planes, gates, cuts):
            for c0, c1 in cuts:
                scale_weave(nc.gpsimd, at + c0, planes[:, :, c0:c1], gates[:, c0:c1])

        sums = {}
        opens, closes = set(), set()

        def open_bank(e0, e1, bank):
            tile = psum.tile([N, HALF], F32, name=bank)
            for e in range(e0, e1):
                sums[e] = tile[:, (e - e0) * C : (e - e0 + 1) * C]
            opens.add(e0)
            closes.add(e1 - 1)

        def quantise(a, s0, at, n):
            nc.vector.quantize_mx(
                out=codes[a][:, s0 : s0 + n].bitcast(FP8X4),
                scales=scales[a][:, s0 : s0 + n],
                in_=woven_sb[:, at : at + n, :].rearrange("p c t -> p (c t)"),
            )

        def multiply(a, e0, e1):
            for e in range(e0, e1):
                c, g = divmod(e * PASSES + a, GROUP)
                nc.tensor.matmul_mx(
                    out=sums[e],
                    lhsT=w_sb[c][:, g, :].bitcast(FP4X4),
                    lhsT_scale=ws_sb[:, e * PASSES + a, :],
                    rhs=codes[a][:, e * C : (e + 1) * C].bitcast(FP8X4),
                    rhs_scale=scales[a][:, e * C : (e + 1) * C],
                    start=(a == 0 and e in opens),
                    stop=(a == PASSES - 1 and e in closes),
                )

        def relu_scalar(into, e):
            nc.scalar.activation(into, sums[e], ACT.Relu, bias=bias_sb[:, e : e + 1])

        def y_of(e0, e1):
            return y_sb[:, e0 * C : e1 * C]

        def square_scalar(e0, e1):
            nc.scalar.activation(y_of(e0, e1), y_of(e0, e1), ACT.Square)

        rooms = {}

        def fetch(k, extra):
            a, c = STEPS[k]
            rooms[k] = room(k, [P, PACK, CHUNK])
            gather_vector(rooms[k], a, c * CHUNK, 0, 0, CHUNK)
            gather_scalar(rooms[k], a, c * CHUNK, 1, extra, CHUNK)
            for t in (2, 3):
                gather_scalar(rooms[k], a, c * CHUNK, t, 0, CHUNK)

        def fetch_extra(k, extra):
            a, c = STEPS[k]
            gather_vector(rooms[k], a, c * CHUNK, 1, 0, extra)

        lower0 = 2 * PER_CHUNK
        upper0 = lower0 + PER_BANK
        final = E - 1
        for i in range(lower0 // PER_BANK):
            open_bank(i * PER_BANK, (i + 1) * PER_BANK, f"bank{i}")

        rooms[0] = room(0, [P, PACK, CHUNK])
        for t in range(PACK):
            gather_scalar(rooms[0], 0, 0, t, 0, HALF)
            gather_vector(rooms[0], 0, 0, t, HALF, CHUNK)

        turned = psum.tile([P, HALF], F32, name="gates0")
        nc.tensor.transpose(turned[:, 0:P], gate_rows[:], identity[:])
        for h0, h1 in ((1, 2), (3, 6)):
            used = slice(h0 * HALF // P, h1 * HALF // P)
            nc.vector.tensor_copy(gate_cols[:, used], turned[:, used])
        for t in (0, 2):
            scale_weave(nc.gpsimd, place(0), rooms[0][:, t : t + 2, 0:LEAD], gate_lead[:], t)
        for c in (1, 2, 0):
            spread_gate(2 * c + 1, f"gates{c}")
        spread_gate(4, "gates3")

        fetch(1, EXTRA_HEAD)
        fetch_extra(1, EXTRA_HEAD)
        for k, (a, c) in enumerate(STEPS):
            if k == 0:
                cuts = ((LEAD, CHUNK),)
            elif k == LAST:
                cuts = ((0, SHARE_LAST),)
            else:
                cuts = ((0, HALF), (HALF, SHARE))
            weave_gpsimd(place(k), rooms[k], gate_sb[c], cuts)
            extra = EXTRA_HEAD if k == 0 else EXTRA
            if k + 2 <= LAST:
                fetch(k + 2, extra)
            elif k + 1 == LAST:
                lower = room(k + 2, [P, PACK, HALF])
                for t in (0, 1):
                    gather_vector(lower, 2, lower0 * C, t, 0, HALF)
                gather_vector(lower, 2, lower0 * C, 2, 0, EXTRA)
                gather_scalar(lower, 2, lower0 * C, 2, EXTRA, HALF)
                gather_scalar(lower, 2, lower0 * C, 3, 0, HALF)
            else:
                upper = room(k + 2, [P, PACK, (final - upper0) * C])
                for t in range(PACK):
                    gather_scalar(upper, 2, upper0 * C, t, 0, (final - upper0) * C)
            if k == LAST:
                weave_vector(SHARE_LAST, rooms[k][:, :, SHARE_LAST:HALF], c * CHUNK + SHARE_LAST)
            if k:
                c0 = max(share(k), HALF)
                weave_vector(place(k) + c0, rooms[k][:, :, c0:CHUNK], c * CHUNK + c0)
            if k + 2 <= LAST:
                fetch_extra(k + 2, extra)
            for c0 in (0, HALF):
                quantise(a, c * CHUNK + c0, place(k) + c0, HALF)
            if c < 2:
                multiply(a, c * PER_CHUNK, (c + 1) * PER_CHUNK)
                if a == PASSES - 1:
                    e0, e1 = (upper0, upper0 + 2) if c else (lower0, upper0)
                    open_bank(e0, e1, f"gates{c}")
                    multiply(0, e0, e1)
        multiply(1, lower0, upper0 + 2)

        at = HALF - SHARE_LOWER
        weave_gpsimd(at, lower, gate_sb[2], ((0, QUARTER), (QUARTER, SHARE_LOWER)))
        third = room(LAST, [P, PACK, C])
        for t in range(PACK):
            gather_vector(third, 2, final * C, t, 0, C)
        weave_vector(at + SHARE_LOWER, lower[:, :, SHARE_LOWER:HALF], lower0 * C + SHARE_LOWER)
        for c0 in (0, QUARTER):
            quantise(2, lower0 * C + c0, at + c0, QUARTER)
        multiply(2, lower0, upper0)

        late0 = lower0 - PER_BANK
        for e in range(late0):
            relu_scalar(y_of(e, e + 1), e)
        for e1 in range(PER_BANK - 1, late0, PER_BANK):
            square_scalar(max(e1 - PER_BANK, 0), e1)
        open_bank(final - 1, final, "bank0")
        open_bank(final, E, "bank1")
        for a in range(PASSES - 1):
            multiply(a, final - 1, E)

        at = at + QUARTER - SHARE_UPPER
        weave_gpsimd(at, upper, gate_sb[2][:, HALF:CHUNK], ((0, SHARE_UPPER),))
        weave_vector(at + SHARE_UPPER, upper[:, :, SHARE_UPPER : (final - upper0) * C], upper0 * C + SHARE_UPPER)
        weave_vector(at + (final - upper0) * C, third[:], final * C)
        late = room(LAST + 1, [P, HALF])
        for e in range(late0, lower0):
            relu_scalar(late[:, (e - late0) * C : (e - late0 + 1) * C], e)
        square_scalar(late0 - 1, late0)
        for e in range(lower0, upper0):
            relu_scalar(y_of(e, e + 1), e)
        square_scalar(lower0, upper0 - 1)
        for e0, e1 in ((upper0, final - 1), (final - 1, final), (final, E)):
            quantise(2, e0 * C, at + (e0 - upper0) * C, (e1 - e0) * C)
            multiply(2, e0, e1)
        nc.vector.tensor_tensor(y_of(late0, lower0), late[:], late[:], MULT)
        for e in range(upper0, final - 1):
            relu_scalar(y_of(e, e + 1), e)
        square_scalar(upper0 - 1, upper0 + 1)
        square_scalar(upper0 + 1, final - 1)
        for e in (final - 1, final):
            nc.vector.tensor_scalar(y_of(e, e + 1), sums[e], bias_sb[:, e : e + 1], 0.0, ADD, MAX)
        for e in (final - 1, final):
            nc.vector.tensor_tensor(y_of(e, e + 1), y_of(e, e + 1), y_of(e, e + 1), MULT)

        picked = room(LAST + 1, [P, PACK, T])
        first, second, pair, total = (picked[:, r, :] for r in range(PACK))

        def results(r, c0, c1):
            return y_sb[:].indirect(pos_sb[r][:, c0 // LANE : c1 // LANE])

        def pick(into, r, c0, c1):
            nc.scalar.activation(into[:, c0:c1], results(r, c0, c1), ACT.Copy)

        def pick_add(into, r, other, c0, c1):
            nc.vector.tensor_tensor(into[:, c0:c1], results(r, c0, c1), other[:, c0:c1], ADD)

        def add_store(c0, c1, stored):
            nc.vector.tensor_tensor(total[:, c0:c1], pair[:, c0:c1], second[:, c0:c1], ADD)
            nc.sync.dma_start(out=out[:, stored:c1], in_=total[:, stored:c1])

        pick(first, 0, ALONE, MID)
        pick(second, 1, ALONE, MID)
        pick(first, 0, MID, T)
        pick(second, 1, MID, END)
        pick(second, 1, END, T)
        nc.vector.tensor_copy(first[:, 0:ALONE], results(0, 0, ALONE))
        pick_add(pair, 1, first, 0, ALONE)
        pick_add(pair, 2, first, ALONE, MID)
        pick_add(total, 2, pair, 0, ALONE)
        add_store(ALONE, MID, 0)
        pick_add(pair, 2, first, MID, END)
        pick_add(pair, 2, first, END, T)
        add_store(MID, END, MID)
        add_store(END, T, END)
